import numpy as np, ml_dtypes
CORES = [25,29,65,69,153,157,193,197]
N = 8
BF = ml_dtypes.bfloat16
def gentries(a):
    return np.ascontiguousarray(a.reshape(8, 16, -1).transpose(0, 2, 1)).reshape(8, -1)
def gtable(e):
    e = np.asarray(e); return np.ascontiguousarray(e.reshape(8, -1, 16).transpose(0, 2, 1)).reshape(128, -1).astype(np.int32)
V, W, SH, CH, RO = 256, 4096, 2, 3, 3
def parts(rng):
    s = rng.integers(0, 256, (N, 8, 16, W), dtype=np.uint8); x = rng.integers(0, 256, (N, 8, 16, V), dtype=np.uint8)
    r = rng.integers(0, 256, (N, 8, 16, V)); r = np.where(rng.random((N, 8, 1, V)) < 0.5, r, 64 + (r >> 1))
    nx = rng.integers(0, V, (N, 8, V)); sr = rng.integers(0, V, (N, 8, V)); ft = rng.integers(17000, 27000, (N, 8, V))
    return s, r, x, nx, sr, ft
def pack(s, r, x, nx, sr, ft):
    return {"prof": s.reshape(N, 128, W).astype(np.float32).astype(BF), "resid": np.ascontiguousarray(r.reshape(N, 128, V)).astype(np.int32), "obs": x.reshape(N, 128, V).astype(np.float32).astype(BF),
            "nx0": np.stack([gtable(a) for a in nx]), "src0": np.stack([gtable(a) for a in sr]), "fit0": np.ascontiguousarray(ft.reshape(N, 8, V)).astype(np.int32)}
def setup_inputs(rng):
    return pack(*parts(rng))
def setup_inputs_spread(rng):
    s = np.minimum(np.exp2(8 * rng.random((N, 8, 1, W))) * rng.random((N, 8, 16, W), dtype=np.float32), 255).astype(np.uint8)
    x = np.minimum(np.exp2(8 * rng.random((N, 8, 1, V))) * rng.random((N, 8, 16, V)), 255).astype(np.uint8)
    r = np.minimum(np.exp2(8 * rng.random((1, 8, 16, 1))) * rng.random((N, 8, 16, V)), 255).astype(np.int64)
    nx = np.minimum((V * rng.random((N, 8, V)) ** 3).astype(np.int64), V - 1); sr = V - 1 - np.minimum((V * rng.random((N, 8, V)) ** 3).astype(np.int64), V - 1)
    ft = np.minimum(np.exp2(16 * rng.random((N, 8, V)) ** 0.5), 65535).astype(np.int64)
    return pack(s, r, x, nx, sr, ft)
def setup_inputs_ends(rng):
    s, r, x, nx, sr, ft = parts(rng)
    s = 255 * rng.integers(0, 2, (N, 8, 16, W), dtype=np.uint8); x = 255 * rng.integers(0, 2, (N, 8, 16, V), dtype=np.uint8)
    cnt = np.clip(np.array([8, 16, 8, 0, 8, 16, 8, 8])[None, :, None] + rng.integers(-1, 2, (N, 8, V)), 0, 16)
    r = np.where(np.argsort(rng.random((N, 8, 16, V)), axis=2) < cnt[:, :, None, :], 255, 0)
    alt = 255 * (np.arange(16) & 1); r[:, 7, :, 0] = alt; r[:, 7, :, V - 1] = 255 - alt; r[N - 1, 7, 15, V - 1] = 255
    for q in range(N):
        for g in range(8):
            if (N - 1 - q + 7 - g) % 2 == 0:
                bit = rng.permutation(np.array([0, 1] + [int(b) for b in rng.integers(0, 2, 14)])).astype(np.uint8); row = (255 * bit)[:, None]
                s[q, g] = row; kind = rng.integers(0, 4, V); kind[0] = 0; kind[V - 1] = 0
                x[q, g] = np.where(kind[None, :] < 2, 255 - row, np.where(kind[None, :] == 2, row, x[q, g]))
    ft = np.where(rng.random((N, 8, V)) < 0.7, 65535, 0); ft[:, :, 0] = 65535; ft[:, :, V - 1] = 65535
    nx = np.where(rng.random((N, 8, V)) < 0.8, (V - 1) * rng.integers(0, 2, (N, 8, V)), nx); sr = np.where(rng.random((N, 8, V)) < 0.8, (V - 1) * rng.integers(0, 2, (N, 8, V)), sr)
    nx[:, :, V - 1] = V - 1; sr[:, :, V - 1] = 0
    return pack(s, r, x, nx, sr, ft)
def setup_inputs_corners(rng):
    s, r, x, nx, sr, ft = parts(rng); own = np.arange(V)
    for q in range(N):
        r[q, 0:2] = rng.integers(0, 8, (2, 16, V)) if q % 2 == 0 else rng.integers(248, 256, (2, 16, V))
    v = rng.integers(0, 2, (N, 2, 8, V)); e = 128 + np.concatenate([v, -v], axis=2)
    e = np.take_along_axis(e, np.argsort(rng.random(e.shape), axis=2), 2)
    d = np.where((own & 1) == 1, rng.choice(np.array([-129, -128, -127, -1, 0, 1, 126, 127, 128]), (N, 2, V)), 0)
    e[:, :, 0] += d >> 1; e[:, :, 15] += d - (d >> 1); r[:, 2:4] = e
    nx[:, 2:4] = 2 * rng.integers(0, V // 2, (N, 2, V)); sr[:, 2:4] = 2 * rng.integers(0, V // 2, (N, 2, V))
    top = rng.random((N, 1, V)) < 0.5; low = np.zeros((N, 16, V), np.int64)
    np.put_along_axis(low, rng.integers(0, 16, (N, 1, V)), rng.choice(np.array([0, 0, 1, 2, 100, 254, 255]), (N, 1, V)), 1)
    r[:, 4] = np.where(top, 255 - low, low)
    for q in range(N):
        for g in range(8):
            m = (q + g) % 6
            if g not in (2, 3):
                if m == 0: nx[q, g] = own; sr[q, g] = own
                if m == 1: nx[q, g] = 0; sr[q, g] = V - 1
                if m == 2: nx[q, g] = V - 1; sr[q, g] = 0
                if m == 3: nx[q, g] = own; sr[q, g] = (own + 1) % V
                if m == 4: nx[q, g] = np.stack([0 * own, 0 * own + V - 1, own])[rng.integers(0, 3, V), own]
            m = (2 * q + g) % 5
            if m == 0: ft[q, g] = 0
            if m == 1: ft[q, g] = 65535
            if m == 2: ft[q, g] = rng.choice(np.array([0, 1, 7, 8, 20000, 65279, 65280, 65281, 65535]), V)
    return pack(s, r, x, nx, sr, ft)
def setup_inputs_near(rng):
    s, r, x, nx, sr, ft = parts(rng); own = np.arange(V)
    mid = 112 + (r[:, 5:7] & 15); s = s & 3; x = x & 3; r[:, ::2] = r[:, ::2] & 3; r[:, 5:7] = mid
    sr = np.where(rng.random((N, 8, V)) < 0.25, own, sr); ft = rng.integers(285, 336, (N, 8, V))
    ft[:, 5:7] = np.where(rng.random((N, 2, V)) < 0.5, 65535, ft[:, 5:7])
    return pack(s, r, x, nx, sr, ft)
def setup_inputs_rounds(rng):
    s, r, x, nx, sr, ft = parts(rng); m = V - N; e = np.arange(m); st = (3 * e) // m
    for g in range(8):
        if g in (3, 7):
            s[:, g] = s[:, g] & 3; x[:, g] = x[:, g] & 3; r[:, g] = 112 + (r[:, g] & 7); ft[:, g] = 65535
            continue
        o = rng.permutation(V); tg = o[:N]
        for q in range(N):
            row = 255 * rng.integers(0, 2, (16, 1)); kind = rng.integers(0, 3, (1, V))
            d = np.where(kind == 0, 255, np.where(kind == 1, 255 - rng.integers(0, 101, (16, V)), rng.integers(0, 128, (16, V))))
            s[q, g] = row.astype(np.uint8); x[q, g] = np.where(row == 0, d, 255 - d).astype(np.uint8)
            mid = 112 + (r[q, g] & 7); mid[:, tg[np.arange(N) != q]] = rng.integers(0, 8, (16, N - 1)) + 248 * rng.integers(0, 2, (1, N - 1)); r[q, g] = mid
            sl = rng.permutation(o[N:]); nx[q, g, tg] = tg; sr[q, g, tg] = tg; nx[q, g, sl] = tg[(q + 1 + st) % N]
            w = 1 + (q + 3 * g) % 7; c = 8 * int(rng.integers(1, 4)) + w
            later = e % (w + 1) if (q + g) % 2 == 0 else e % 10
            off = np.where(st == 0, np.where(e < c, 1 + e % 9, -(e % 9)), np.where(st == 1, later, e % 10))
            ft[q, g] = 0; ft[q, g, sl] = np.maximum(16 * np.add.reduce(d, axis=0)[sl] + off, 0)
    return pack(s, r, x, nx, sr, ft)
def check_inputs(d):
    bad = []
    for k, lo, hi in (("prof", 0, 255), ("resid", 0, 255), ("obs", 0, 255), ("nx0", 0, V - 1), ("src0", 0, V - 1), ("fit0", 0, 65535)):
        v = np.asarray(d[k]).astype(np.float64)
        if not (np.min(v) >= lo and np.max(v) <= hi): bad.append("range of " + k)
        elif np.any(v != np.floor(v)): bad.append("whole numbers of " + k)
    return bad
def reference(prof, resid, obs, nx0, src0, fit0):
    sp = np.ascontiguousarray(prof.astype(np.float32).astype(np.int16).reshape(N, 8, 16, W).transpose(0, 1, 3, 2)).reshape(N, 8 * W, 16)
    ob = np.ascontiguousarray(obs.astype(np.float32).astype(np.int16).reshape(N, 8, 16, V).transpose(0, 1, 3, 2))
    r = resid.astype(np.int64).reshape(N, 8, 16, V); ft = fit0.astype(np.int64)
    nx = np.stack([gentries(a) for a in nx0]).astype(np.int64); sr = np.stack([gentries(a) for a in src0]).astype(np.int64)
    acc = np.zeros((N, 8), np.int64); odd = 2 * np.arange(V) + 1; first = (np.arange(8) * W)[:, None, None]; site = np.arange(16)[None, :, None]; none = 2 ** 20
    def cost(a, p):
        col = ((odd * (p + 4096)) >> SH) & (W - 1)
        return np.add.reduce(np.abs(np.take(sp[a], first + col, axis=0) - ob[a][:, None]), axis=-1, dtype=np.int64)
    for t in range(RO):
        tot = np.add.reduce(r, axis=2); r2, nx2, sr2, ft2, took = [], [], [], [], []
        for a in range(N):
            q = (a + 1 + t % (N - 1)) % N; n = nx[a]
            best = np.full((8, V), none, np.int64); bn = np.zeros((8, V), np.int64); bl = r[a]
            for z in range(CH):
                if z > 0: n = np.take_along_axis(sr[q], n, 1)
                l = np.take_along_axis(r[q], n[:, None, :], 2)
                dl = (tot[a] - np.take_along_axis(tot[q], n, 1))[:, None, :]
                p = np.add.accumulate(l, axis=1); g = cost(a, p); h = cost(a, p + dl)
                sc = np.add.accumulate(g, axis=1) - g + np.add.accumulate(h[:, ::-1], axis=1)[:, ::-1]
                sc = np.where((l + dl >= 0) & (l + dl <= 255), sc, none)
                j = np.argmin(sc, axis=1); m = np.min(sc, axis=1); better = m < best
                bl = np.where(better[:, None, :], l + np.where(site == j[:, None, :], dl, 0), bl)
                bn = np.where(better, n, bn); best = np.where(better, m, best)
            ok = best < ft[a] - (acc[a] & 7)[:, None]
            r2.append(np.where(ok[:, None, :], bl, r[a])); ft2.append(np.where(ok, best, ft[a])); sr2.append(np.where(ok, bn, sr[a]))
            nx2.append(np.where(ok, (13 * bn + best) & (V - 1), n)); took.append(np.add.reduce(ok.astype(np.int64), axis=1))
        r, nx, sr, ft = np.stack(r2), np.stack(nx2), np.stack(sr2), np.stack(ft2); acc = acc + np.stack(took)
    return {"yr": r.reshape(N, 128, V).astype(np.float32), "yf": ft.astype(np.float32), "yn": nx.astype(np.float32)}

@@ -1,0 +1,635 @@
+import numpy as np
+from concourse.bass import DstId, RemoteDMATransfer
+from concourse.mybir import dt, AluOpType, AxisListType, ActivationFunctionType
+
+AL = AluOpType
+AF = ActivationFunctionType
+NR = 3
+V = 256
+DS, DE = 16, 128
+NA, ND = DS + V - DE, DE - DS
+ABLK = [(DE + (V - DE) * i // 4, DE + (V - DE) * (i + 1) // 4) for i in range(4)]
+ALATE = (0, DS)
+DBLK = [(32, 64), (64, 96), (96, DE)]
+DLATE = (DS, 32)
+CHUNKS = [[("A", DE, DE + 16)], [("A", DE + 16, DE + 80)], [("A", DE + 80, V)],
+          [("D", 32, 64), ("D", 64, 96)], [("D", 96, DE)], [("A", 0, DS), ("D", DS, 32)]]
+ORDER = ["A0", "D0", "A1", "D1", "A2", "D2", "A3"]
+KEYBANK = [(0, 32, "psKB"), (32, DE, "psKC"), (DE, V, "psKA")]
+PAY = 272
+CUT = 1024
+BIG = 33554432.0
+MAGIC = 1.5 * 2.0 ** 31
+
+
+def sb(cols, kind="bfloat16"):
+    return ("sbuf", [128, cols], kind)
+
+
+SCRATCH = {
+    "S": sb(4096), "obs_s": sb(256), "nobs": sb(256, "float32"), "Xe": sb(ND * 48),
+    "rawR": sb(256, "int32"), "raws": sb(16, "int32"), "rawn": sb(16, "int32"),
+    "fitb": sb(256, "int32"), "fitf": sb(256, "float32"), "fitt": sb(256, "float32"),
+    "W0": sb(1040), "W1": sb(1040), "W2": sb(1040), "land0": sb(PAY), "land1": sb(PAY), "land2": sb(PAY),
+    "LQ1": sb(256), "LQ2": sb(256), "srcU": sb(16, "uint16"), "n0U": sb(16, "uint16"), "offB": sb(32, "uint16"),
+    "B1": sb(256), "X": sb(256), "X2": sb(256), "nX": sb(512), "T12": sb(512),
+    "off": sb(1536, "uint16"), "odd": sb(1536, "float32"),
+    "v1a": sb(384, "int32"), "v1b": sb(384, "int32"), "v2a": sb(384, "int32"), "v2b": sb(384, "int32"),
+    "pen": sb(768), "A": sb(NA * 96), "dd": sb(ND * 96), "rr": sb(ND * 96),
+    "z1": sb(768, "float32"), "tr": sb(256, "float32"), "s2": sb(256, "int32"),
+    "sc": sb(16, "int32"), "z16": sb(16, "int32"), "st": sb(16, "int32"), "SWa": sb(32),
+    "acc0": sb(32), "acc1": sb(32), "IND": sb(48), "PQ": sb(48), "TP": sb(48),
+    "nL": sb(16), "nLn": sb(16), "srcA": sb(16), "srcB": sb(16),
+    "F": sb(16, "float32"), "thr": sb(16, "float32"), "Ai": sb(16, "int32"), "A7": sb(16, "int32"),
+    "b1": sb(16, "float32"), "bn": sb(16, "float32"), "h1": sb(16, "float32"), "h2": sb(16, "int32"), "h3": sb(16, "int32"),
+    "d3": sb(16, "float32"), "d4": sb(16, "float32"), "d5": sb(16, "float32"), "d6": sb(16, "float32"),
+    "Rb": sb(256), "OH": sb(256), "md": sb(256), "Rf": sb(256, "float32"), "B2": sb(256, "float32"), "oT": sb(256, "float32"),
+    "ones": sb(128), "I": sb(128), "BLK": sb(128), "TRI": sb(128), "TMO": sb(128), "IMO": sb(128), "NBLK": sb(128), "BIGI": sb(128),
+    "BLK32": sb(128), "B48": ("sbuf", [128, 8, 48], "bfloat16"), "WT": ("sbuf", [128, 248, 16], "bfloat16"), "E": sb(512), "E16": sb(512),
+    "c4096": sb(64), "cm127": sb(160), "pi": sb(1, "int32"), "pj": sb(1, "int32"), "jcol": sb(1, "float32"),
+    "kct": sb(120, "float32"), "KC": sb(120), "ilt": sb(16, "float32"), "ilist": sb(16), "zit": sb(16, "float32"), "ZI": sb(16),
+    "RS3": sb(420, "float32"), "RS16": sb(256, "float32"),
+    "psP0": ("psum", [128, 512], "float32"), "psP1": ("psum", [128, 512], "float32"), "psQ": ("psum", [128, 512], "float32"),
+    "psKA": ("psum", [128, 512], "float32"), "psKB": ("psum", [128, 512], "float32"), "psKC": ("psum", [128, 512], "float32"),
+    "psS": ("psum", [128, 512], "float32"), "psD": ("psum", [128, 512], "float32"),
+}
+SEMAPHORES = (["qv", "qa", "qp", "qg", "go", "ldf"] + ["ld%d" % i for i in range(6)] + ["st%d" % i for i in range(4)]
+              + ["%s%s%d" % (n, p, t) for n in ("arr", "hop", "loc", "hl") for t in range(NR) for p in "EL"])
+
+
+def route(q, t, cores, topo):
+    n = len(cores)
+    src, dst = cores[q], cores[(q - 1 - (t % (n - 1))) % n]
+    if topo.may_write(src, dst):
+        return dst, None
+    for c in topo.cores_of(src):
+        if c not in cores and topo.die(c) == topo.die(src) and topo.may_write(c, dst):
+            return dst, c
+    return dst, None
+
+
+def pick(src, dst, topo):
+    e = topo.engines(src, dst)[:8]
+    return sum(1 << i for i in e), len(e)
+
+
+def pieces(t):
+    return [("L", 0, 16), ("E", 16, PAY)] if t == 0 else [("E", 0, PAY)]
+
+
+def relay_program(g, core, T, topo):
+    held = []
+    for t in range(NR):
+        for q in range(len(T.cores)):
+            dst, via = route(q, t, T.cores, topo)
+            if via != core:
+                continue
+            _, n1 = pick(T.cores[q], core, topo)
+            m, n2 = pick(core, dst, topo)
+            rid, pid = topo.addr(dst, core)
+            for p, a, b in pieces(t):
+                land = T["land%d" % t][:, a:b]
+                g.wait_ge(T.sem["hop%s%d" % (p, t)], n1)
+                g.remote_dma(out_ap=land, in_ap=land, remote_sem=T.sem["arr%s%d" % (p, t)], local_sem=T.sem["hl%s%d" % (p, t)],
+                             pid=pid, routing_id=rid, dma_engine_mask=m)
+                held.append(("hl%s%d" % (p, t), n2))
+    for s, n in held:
+        g.wait_ge(T.sem[s], n)
+
+
+def rank_program(g, core, T, topo):
+    rank = T.rank_of(core)
+    if rank is None:
+        relay_program(g, core, T, topo)
+        return
+    ENG = {"v": g.vector, "a": g.scalar, "p": g.tensor, "g": g, "s": g.sync}
+    total, known, hist, rec, bank = {}, {k: {} for k in ENG}, {}, {}, {}
+    nload = [0]
+
+    def need(want, tok):
+        s, c = tok
+        if want.get(s, 0) < c:
+            want[s] = c
+
+    def learn(q, s, c):
+        k = known[q]
+        for a, b in hist.get((s, c), {}).items():
+            if k.get(a, 0) < b:
+                k[a] = b
+        if k.get(s, 0) < c:
+            k[s] = c
+
+    def wait(q, want):
+        for s, c in sorted(want.items(), key=lambda x: x[0]):
+            if known[q].get(s, 0) < c:
+                ENG[q].wait_ge(T.sem[s], c)
+                learn(q, s, c)
+
+    def step(v):
+        return v[4] if len(v) > 4 else 1
+
+    def clash(r, v):
+        s = step(v)
+        return r[1] < v[3] and v[2] < r[2] and not (s > 1 and s == r[5] and (r[1] - v[2]) % s)
+
+    def covers(v, r):
+        s = step(v)
+        return v[2] <= r[1] and r[2] <= v[3] and (s == 1 or (s == r[5] and (r[1] - v[2]) % s == 0))
+
+    def op(q, fn, reads, writes, sem=None, inc=1, then=True):
+        own = sem is None
+        s = "q" + q if own else sem
+        tag = q if own else "x" + sem
+        want = {}
+        for v in reads + writes:
+            if v[1][:2] == "ps":
+                for a, tok in bank.get(v[1], {}).items():
+                    if a != tag:
+                        need(want, tok)
+        for v in reads:
+            for r in rec.get(v[1], []):
+                if r[0] == "w" and clash(r, v):
+                    need(want, r[4])
+        for v in writes:
+            for r in rec.get(v[1], []):
+                if (r[3] != tag or r[0] == "w") and clash(r, v):
+                    need(want, r[4])
+        wait(q, want)
+        ins = fn(ENG[q])
+        total[s] = total.get(s, 0) + inc
+        tok = (s, total[s])
+        if then:
+            ins.then_inc(T.sem[s], inc)
+        hist[tok] = dict(known[q])
+        for v in reads:
+            if v[1][:2] == "ps":
+                bank.setdefault(v[1], {})[tag] = tok
+                continue
+            L = [r for r in rec.get(v[1], []) if not (r[0] == "r" and r[3] == tag and covers(v, r))]
+            L.append(("r", v[2], v[3], tag, tok, step(v)))
+            rec[v[1]] = L
+        for v in writes:
+            if v[1][:2] == "ps":
+                bank.setdefault(v[1], {})[tag] = tok
+                continue
+            L = [r for r in rec.get(v[1], []) if not covers(v, r)]
+            L.append(("w", v[2], v[3], tag, tok, step(v)))
+            rec[v[1]] = L
+        return tok
+
+    def arrived(name, lo, hi, sem, n):
+        total[sem] = total.get(sem, 0) + n
+        rec.setdefault(name, []).append(("w", lo, hi, "x" + sem, (sem, total[sem]), 1))
+
+    def B(name, lo=0, hi=None, step=1):
+        t = T[name]
+        hi = t.shape[1] if hi is None else hi
+        return (t[:, lo:hi] if step == 1 else t[:, lo:hi:step], name, lo, hi, step)
+
+    def ind(win, of):
+        return win[0].indirect(of[0])
+
+    def tt(out, a, b, o):
+        return op("v", lambda e: e.tensor_tensor(out[0], a[0], b[0], o), [a, b], [out])
+
+    def ts(out, a, s1, s2, o0, o1=None, col=None):
+        x = col[0] if col else s1
+        if o1 is None:
+            return op("v", lambda e: e.tensor_scalar(out[0], a[0], x, None, o0), [a] + ([col] if col else []), [out])
+        return op("v", lambda e: e.tensor_scalar(out[0], a[0], x, s2, o0, o1), [a] + ([col] if col else []), [out])
+
+    def vcopy(out, a):
+        return op("v", lambda e: e.tensor_copy(out[0], a[0]), [a], [out])
+
+    def acopy(out, a):
+        return op("a", lambda e: e.activation(out[0], a[0], AF.Copy), [a], [out])
+
+    def vgather(out, win, of):
+        return op("v", lambda e: e.tensor_copy(out[0], ind(win, of)), [win, of], [out])
+
+    def agather(out, win, of):
+        return op("a", lambda e: e.activation(out[0], ind(win, of), AF.Copy), [win, of], [out])
+
+    def vtrans(out, a):
+        return op("v", lambda e: e.transpose(out[0], a[0]), [a], [out])
+
+    def memset(out, c):
+        return op("v", lambda e: e.memset(out[0], c), [], [out])
+
+    def scan(out, d0, d1):
+        return op("v", lambda e: e.tensor_tensor_scan(out[0], d0[0], d1[0], 0.0, AL.add, AL.min), [d0, d1], [out])
+
+    def mm(out, l, r, start, stop):
+        return op("p", lambda e: e.matmul(out[0], l[0], r[0], start, stop), [l, r], [out])
+
+    def load(q, out, src):
+        k = nload[0]
+        nload[0] += 1
+        return op(q, lambda e: e.dma_start(out[0], src), [], [out], sem="ld%d" % k, inc=16)
+
+    def store(q, out, src, sem):
+        return op(q, lambda e: e.dma_start(out, src[0]), [src], [], sem=sem, inc=16)
+
+    def iota(out, pattern, base, cm, f=True):
+        if f:
+            return op("g", lambda e: e.iota(out[0], pattern, base, cm, allow_small_or_imprecise_dtypes=True), [], [out])
+        return op("g", lambda e: e.iota(out[0], pattern, base, cm), [], [out])
+
+    def sel(out, a, pattern, cmp, base, cm):
+        return op("g", lambda e: e.affine_select(out[0], a[0], pattern, cmp, 0.0, base, cm), [a], [out])
+
+    def apos(s):
+        return s if s < DS else s - ND
+
+    def weight(gh, k):
+        n = 15 * gh + k
+        return (T.WT[:, 8 * n:8 * n + 8, :], "WT", n, n + 1)
+
+    def put_weight(gh, k, q):
+        lo = 15 - k if gh == 0 else 31 - k
+        (vcopy if q == "v" else acopy)(weight(gh, k), (T.B48[:, :, lo:lo + 16], "B48", 0, 384))
+
+    def swap(field, col, extra=None, name="E", a=0, b=16):
+        fb, fo = field
+        for h in range(2):
+            o = B("psS", col + a + h, col + b, 2)
+            if extra is not None:
+                mm(o, B("I"), B(extra, a + h, b, 2), True, False)
+            for e in range(2):
+                k = 128 * (2 * e + h)
+                mm(o, B(name, k, k + 128), B(fb, fo + a + e, fo + b, 2), extra is None and e == 0, e == 1)
+
+    W = ["W0", "W1", "W2"]
+    load("s", B("rawR"), T.resid[:])
+    load("a", B("raws"), T.src0[:])
+    load("a", B("rawn"), T.nx0[:])
+    load("s", B("S", 0, CUT), T.prof[:, 0:CUT])
+    load("a", B("obs_s"), T.obs[:])
+    memset(B("ones"), 1.0)
+    memset(B("E"), 0.0)
+    memset(B("fitb"), 0)
+    op("v", lambda e: e.memset(T.B48[:, :, 0:16], 0.0), [], [("", "B48", 0, 384)])
+    op("v", lambda e: e.memset(T.B48[:, :, 16:32], 64.0), [], [("", "B48", 0, 384)])
+    op("v", lambda e: e.memset(T.B48[:, :, 32:48], 0.0), [], [("", "B48", 0, 384)])
+    op("a", lambda e: e.dma_start(T.fitb[0:128:16, :], T.fit0[:]), [], [B("fitb")], sem="ldf", inc=16)
+    iota(B("pi"), [[0, 1]], 0, 1, False)
+    sel(B("I"), B("ones"), [[-1, 128]], AL.is_equal, 0, 1)
+    iota(B("ilt"), [[16, 16]], 0, 0)
+    iota(B("zit"), [[1, 16]], 0, 0)
+    sel(B("BLK"), B("ones"), [[-16, 8], [0, 16]], AL.is_ge, 0, 1)
+    sel(B("BLK"), B("BLK"), [[16, 8], [0, 16]], AL.is_ge, 15, -1)
+    memset(B("RS3"), 0.0)
+    memset(B("RS3", 0, 420, 3), BIG)
+    vcopy(B("W0", 0, 16), B("raws"))
+    vcopy(B("W0", 16, PAY), B("rawR"))
+
+    def send(t, piece):
+        p, a, b = piece
+        dst, via = route(rank, t, T.cores, topo)
+        to = dst if via is None else via
+        m, n = pick(core, to, topo)
+        rid, pid = topo.addr(to, core)
+        rs, ls = T.sem["%s%s%d" % ("arr" if via is None else "hop", p, t)], "loc%s%d" % (p, t)
+        src = B(W[t], a, b)
+        op("g", lambda e: e.remote_dma(out_ap=T["land%d" % t][:, a:b], in_ap=src[0], remote_sem=rs, local_sem=T.sem[ls],
+                                       pid=pid, routing_id=rid, dma_engine_mask=m), [src], [], sem=ls, inc=n, then=False)
+
+    def expect(t):
+        for q in range(len(T.cores)):
+            dst, via = route(q, t, T.cores, topo)
+            if dst == core:
+                for p, a, b in pieces(t):
+                    arrived("land%d" % t, a, b, "arr%s%d" % (p, t), pick(T.cores[q] if via is None else via, core, topo)[1])
+
+    for piece in pieces(0):
+        send(0, piece)
+    g.sem_inc(T.sem["go"], 1)
+    total["go"] = 1
+    g.sync.wait_ge(T.sem["go"], 1)
+    load("s", B("S", CUT, 4096), T.prof[:, CUT:4096])
+    sel(B("TRI"), B("BLK"), [[1, 128]], AL.is_ge, 0, -1)
+    iota(B("kct"), [[0, 40], [16, 3]], 16, 0)
+    b48 = (T.B48[:], "B48", 0, 384)
+    sel(b48, b48, [[-16, 8], [0, 48]], AL.is_ge, 0, 1)
+    sel(b48, b48, [[16, 8], [0, 48]], AL.is_ge, 15, -1)
+    iota(B("odd", 6 * DE, 1536), [[2, V - DE], [0, 6]], 2 * DE + 1, 0)
+    iota(B("odd", 0, 6 * DS), [[2, DS], [0, 6]], 1, 0)
+    for s0, s1 in DBLK + [DLATE]:
+        iota(B("odd", 6 * s0, 6 * s1), [[0, 2], [2, s1 - s0], [0, 3]], 2 * s0 + 1, 0)
+    sel(B("BLK32"), B("ones"), [[-32, 4], [0, 32]], AL.is_ge, 0, 1)
+    sel(B("BLK32"), B("BLK32"), [[32, 4], [0, 32]], AL.is_ge, 31, -1)
+    for e in range(2):
+        for h in range(2):
+            for a in range(4):
+                k = 128 * (2 * e + h) + 32 * a
+                vcopy(B("E", k + 16 * e, k + 16 * e + 16), B("I", 32 * a + 16 * h, 32 * a + 16 * h + 16))
+    ts(B("E16"), B("E"), 16.0, None, AL.mult)
+    vcopy(B("nL"), B("rawn"))
+    swap(("nL", 0), 32)
+    swap(("W0", 0), 48)
+    vcopy(B("n0U"), B("rawn"))
+    vcopy(B("nLn"), B("psS", 32, 48))
+    vcopy(B("srcA"), B("psS", 48, 64))
+    ts(B("pj"), B("pi"), 15, None, AL.bitwise_and)
+    vcopy(B("jcol"), B("pj"))
+    ts(B("ilist"), B("ilt"), None, None, AL.add, col=B("jcol"))
+    ts(B("ZI"), B("zit"), None, None, AL.is_equal, col=B("jcol"))
+    memset(B("c4096"), 4096.0)
+    memset(B("cm127"), -127.5)
+    tt(B("TMO"), B("TRI"), B("BLK"), AL.subtract)
+    tt(B("IMO"), B("I"), B("BLK"), AL.subtract)
+    ts(B("NBLK"), B("BLK"), -1.0, None, AL.mult)
+    ts(B("BIGI"), B("I"), 4194304.0, None, AL.mult)
+    memset(B("B1"), 0.0)
+    memset(B("B2"), 0.0)
+    memset(B("RS16"), 0.0)
+    memset(B("RS16", 0, 256, 16), BIG)
+    ts(B("nobs"), B("obs_s"), -1.0, None, AL.mult)
+    for k in range(48):
+        (acopy if k % 2 else vcopy)(B("Xe", k, ND * 48, 48), B("obs_s", DS, DE))
+    for gh in range(2):
+        for k in range(15 + gh):
+            put_weight(gh, k, "a" if k % 2 else "v")
+    ts(B("KC"), B("kct"), None, None, AL.add, col=B("jcol"))
+    vcopy(B("fitf"), B("fitb"))
+    vtrans(B("fitt"), B("fitf"))
+    vcopy(B("F"), B("fitt", 0, 256, 16))
+    ts(B("thr"), B("F"), 64.0, None, AL.mult)
+
+    nown, sown = ["nLn", "nL"], ["srcA", "srcB"]
+    for t in range(NR):
+        w, land, last = W[t], "land%d" % t, t == NR - 1
+        wn = None if last else W[t + 1]
+        expect(t)
+
+        def ro(a, b):
+            return B(w, 16 + a, 16 + b)
+
+        def rc(z, a, b):
+            return B(w, 16 + 256 * (z + 1) + a, 16 + 256 * (z + 1) + b)
+
+        lists = B(land, 16, PAY)
+        f0 = 2 * (DE // 32)
+        f1 = f0 + 2 * ((DE + 15) // 32 - DE // 32 + 1)
+        rest = [(0, f0), (f1, 16)]
+
+        def nx(c0, c1):
+            return B("n0U", c0, c1)
+        vcopy(B("srcU"), B(land, 0, 16))
+        agather(B("LQ1", 0, 128), lists, B("srcU", 0, 8))
+        vgather(B("LQ1", 128, 256), lists, B("srcU", 8, 16))
+        vgather(rc(0, 16 * f0, 16 * f1), lists, nx(f0, f1))
+        agather(B("LQ2", 0, 128), B("LQ1"), B("srcU", 0, 8))
+        vgather(B("LQ2", 128, 256), B("LQ1"), B("srcU", 8, 16))
+        vgather(rc(1, 16 * f0, 16 * f1), B("LQ1"), nx(f0, f1))
+        vgather(rc(2, 16 * f0, 16 * f1), B("LQ2"), nx(f0, f1))
+        for c0, c1 in rest:
+            agather(rc(1, 16 * c0, 16 * c1), B("LQ1"), nx(c0, c1))
+            agather(rc(2, 16 * c0, 16 * c1), B("LQ2"), nx(c0, c1))
+        def prefix(ci):
+            ch = CHUNKS[ci]
+            c0 = ch[0][1]
+            P = "psP%d" % (ci % 2)
+            for kind, s0, s1 in ch:
+                n = s1 - s0
+                for z in range(3):
+                    b = 6 * (s0 - c0)
+                    if kind == "A":
+                        og, oh = B(P, b + 2 * z, b + 6 * n, 6), B(P, b + 2 * z + 1, b + 6 * n, 6)
+                    else:
+                        og, oh = B(P, b + z, b + 3 * n, 3), B(P, b + 3 * n + z, b + 6 * n, 3)
+                    mm(og, B("I"), B("c4096", 0, n), True, False)
+                    mm(og, B("TRI"), rc(z, s0, s1), False, True)
+                    mm(oh, B("I"), B("c4096", 0, n), True, False)
+                    mm(oh, B("BLK"), ro(s0, s1), False, False)
+                    mm(oh, B("TMO"), rc(z, s0, s1), False, True)
+
+        def times(ci):
+            c0, c1 = CHUNKS[ci][0][1], CHUNKS[ci][-1][2]
+            n = 6 * (c1 - c0)
+            tt(B("v1" + "ab"[ci % 2], 0, n), B("psP%d" % (ci % 2), 0, n), B("odd", 6 * c0, 6 * c1), AL.mult)
+
+        def floor(ci):
+            n = 6 * (CHUNKS[ci][-1][2] - CHUNKS[ci][0][1])
+            ts(B("v2" + "ab"[ci % 2], 0, n), B("v1" + "ab"[ci % 2], 0, n), 2, 4095, AL.arith_shift_right, AL.bitwise_and)
+
+        def place(ci):
+            c0, c1 = CHUNKS[ci][0][1], CHUNKS[ci][-1][2]
+            vcopy(B("off", 6 * c0, 6 * c1), B("v2" + "ab"[ci % 2], 0, 6 * (c1 - c0)))
+
+        def allowed(P, c0, c1):
+            for z in range(3):
+                o = B(P, z, 3 * (c1 - c0), 3)
+                mm(o, B("I"), B("cm127", 0, c1 - c0), True, False)
+                mm(o, B("BLK"), ro(c0, c1), False, False)
+                mm(o, B("IMO"), rc(z, c0, c1), False, True)
+            ts(B("pen", 3 * c0, 3 * c1), B(P, 0, 3 * (c1 - c0)), MAGIC, MAGIC, AL.add, AL.not_equal)
+
+        prefix(0)
+        a, b = rest[0]
+        vgather(rc(0, 16 * a, 16 * b), lists, nx(a, b))
+        times(0)
+        floor(0)
+        place(0)
+        a, b = rest[1]
+        vgather(rc(0, 16 * a, 16 * b), lists, nx(a, b))
+        for c in (1, 3):
+            prefix(c)
+            prefix(c + 1)
+            times(c)
+            times(c + 1)
+            floor(c)
+            floor(c + 1)
+            place(c)
+            place(c + 1)
+        prefix(5)
+        times(5)
+        allowed("psQ", DE, V)
+        floor(5)
+        allowed("psP0", 32, DE)
+        place(5)
+        allowed("psP1", 0, 32)
+        swap((land, 0), 32)
+        n0, srcl = B(nown[0]), B(sown[0])
+        tt(B("PQ", 0, 16), n0, srcl, AL.subtract)
+
+        def absd(s0, s1):
+            for s in range(s0, s1):
+                p = 96 * apos(s)
+                o, of, bi = B("A", p, p + 96), B("off", 6 * s, 6 * s + 6), B("nobs", s, s + 1)
+                op("a", lambda e: e.activation(o[0], ind(B("S"), of), AF.Abs, bias=bi[0]), [B("S"), of, bi], [o])
+
+        def gat(blk):
+            s0, s1 = blk
+            n, base = 48 * (s1 - s0), 96 * (s0 - DS)
+            for gh in range(2):
+                lo = base + gh * n
+                c = 6 * s0 + gh * 3 * (s1 - s0)
+                of, x, o = B("off", c, c + 3 * (s1 - s0)), B("Xe", 48 * (s0 - DS), 48 * (s1 - DS)), B("dd", lo, lo + n)
+                op("v", lambda e: e.tensor_tensor(o[0], ind(B("S"), of), x[0], AL.subtract), [B("S"), of, x], [o])
+            for gh in range(2):
+                lo = base + gh * n
+                ts(B("rr", lo, lo + n), B("dd", lo, lo + n), 0.0, -2.0, AL.min, AL.mult)
+
+        def sums(kind, blk):
+            s0, s1 = blk
+            kb = [x for x in KEYBANK if x[0] <= s0 and s1 <= x[1]][0]
+            o, n = B(kb[2], 3 * (s0 - kb[0]), 3 * (s1 - kb[0])), 3 * (s1 - s0)
+            mm(o, B("I"), B("KC", 0, n), True, False)
+            mm(o, B("BIGI"), B("pen", 3 * s0, 3 * s1), False, False)
+            todo = []
+            for gh in range(2):
+                for buf in ("A",) if kind == "A" else ("dd", "rr"):
+                    for k in range(15 + gh):
+                        if kind == "A":
+                            p = 96 * apos(s0)
+                            todo.append((weight(gh, k), B(buf, p + 16 * gh + k, p + 32 * n, 32)))
+                        else:
+                            lo = 96 * (s0 - DS) + gh * 16 * n
+                            todo.append((weight(gh, k), B(buf, lo + k, lo + 16 * n, 16)))
+            for i, (wt, r) in enumerate(todo):
+                mm(o, wt, r, False, i == len(todo) - 1)
+
+        def best1(lo, hi, ps):
+            scan(B("z1", 3 * lo, 3 * hi), B("RS3", 0, 3 * (hi - lo)), B(ps, 0, 3 * (hi - lo)))
+
+        def turn(lo, hi):
+            vtrans(B("tr", lo, hi), B("z1", 3 * lo + 2, 3 * hi, 3))
+
+        def best2(lo, hi):
+            scan(B("s2", lo, hi), B("RS16", 0, hi - lo), B("tr", lo, hi))
+
+        def accept(lo, hi):
+            a, b = lo // 16, hi // 16
+            bi, ac = B("s2", lo + 15, hi, 16), B("IND", a, b)
+            ts(B("st", a, b), bi, 15, None, AL.bitwise_and)
+            ts(B("z16", a, b), bi, 48, None, AL.bitwise_and)
+            tt(ac, bi, B("thr", a, b), AL.is_lt)
+            vcopy(B("SWa", 16 + a, 16 + b), B("st", a, b))
+            tt(B("SWa", a, b), B("z16", a, b), ac, AL.mult)
+            swap(("SWa", 16), 16, None, "E", a, b)
+            swap(("SWa", 0), 0, "ilist", "E16", a, b)
+
+        def offsets(lo, hi):
+            a, b = lo // 16, hi // 16
+            vcopy(B("offB", a, b), B("psS", a, b))
+            vcopy(B("offB", 16 + a, 16 + b), B("psS", 16 + a, 16 + b))
+
+        def readlist(lo, hi):
+            agather(B("Rb", lo, hi), B(w, 16, 1040), B("offB", lo // 16, hi // 16))
+
+        def newlist(lo, hi, ps):
+            mm(B(ps, 0, hi - lo), B("BLK"), ro(lo, hi), True, False)
+            mm(B(ps, 0, hi - lo), B("NBLK"), B("Rb", lo, hi), False, True)
+            mm(B(ps, 256, 256 + hi - lo), B("I"), B("Rb", lo, hi), True, True)
+
+        def site(lo, hi, ps):
+            tt(B("md", lo, hi), B(ps, 0, hi - lo), B("OH", lo, hi), AL.mult)
+
+        def putlist(lo, hi, ps):
+            out = B("Rf", lo, hi) if last else B(wn, 16 + lo, 16 + hi)
+            tt(out, B(ps, 256, 256 + hi - lo), B("md", lo, hi), AL.add)
+            if last:
+                store("s", T.yr[:, lo:hi], out, "st%d" % (3 if lo else 0))
+
+        for s0, s1 in ABLK + [ALATE]:
+            absd(s0, s1)
+        for blk in DBLK:
+            gat(blk)
+        for nm in ORDER:
+            sums(nm[0], (ABLK if nm[0] == "A" else DBLK)[int(nm[1])])
+        vcopy(B("B1", 0, 256, 16), B("psS", 32, 48))
+        vtrans(B("X"), B("B1"))
+        gat(DLATE)
+        sums("D", DLATE)
+        sums("A", ALATE)
+        best1(32, DE, "psKC")
+        best1(DE, V, "psKA")
+        turn(32, V)
+        best2(32, V)
+        accept(32, V)
+        agather(B("nX", 0, 256), B("X"), B("n0U"))
+        agather(B("X2"), B("X"), B("srcU"))
+        agather(B("nX", 256, 512), B("X2"), B("n0U"))
+        vtrans(B("T12", 0, 256), B("nX", 0, 256))
+        best1(0, 32, "psKB")
+        n1, n2 = B("T12", 0, 256, 16), B("T12", 256, 512, 16)
+        acc = B("IND", 0, 16)
+        tt(B("PQ", 16, 32), n1, n0, AL.subtract)
+        turn(0, 32)
+        offsets(32, V)
+        best2(0, 32)
+        readlist(32, V)
+        agather(B("OH", 32, V), B("ZI"), B("offB", 18, 32))
+        accept(0, 32)
+        newlist(32, V, "psD")
+        vtrans(B("T12", 256, 512), B("nX", 256, 512))
+        ts(B("IND", 16, 32), B("SWa", 0, 16), 32.0, None, AL.is_ge)
+        ts(B("IND", 32, 48), B("SWa", 0, 16), 48.0, None, AL.is_ge)
+        tt(B("PQ", 32, 48), n2, n1, AL.subtract)
+        offsets(0, 32)
+        readlist(0, 32)
+        agather(B("OH", 0, 32), B("ZI"), B("offB", 16, 18))
+        newlist(0, 32, "psP1")
+        tt(B("TP"), B("IND"), B("PQ"), AL.mult)
+        if last:
+            tt(B("b1"), B("TP", 0, 16), B("TP", 16, 32), AL.add)
+        site(32, V, "psD")
+        if not last:
+            for h in range(2):
+                o = B("psP0", h, 16, 2)
+                mm(o, B("I"), B(w, h, 16, 2), True, False)
+                for f in range(3):
+                    for e in range(2):
+                        k = 128 * (2 * e + h)
+                        mm(o, B("E", k, k + 128), B("TP", 16 * f + e, 16 * f + 16, 2), False, f == 2 and e == 1)
+        if not last:
+            site(0, 32, "psP1")
+            putlist(32, V, "psD")
+            vcopy(B(wn, 0, 16), B("psP0", 0, 16))
+            putlist(0, 32, "psP1")
+            send(t + 1, pieces(t + 1)[0])
+            tt(B("b1"), B("TP", 0, 16), B("TP", 16, 32), AL.add)
+        tt(B("bn"), B("TP", 32, 48), B("b1"), AL.add)
+        ts(B("sc"), B("s2", 15, 256, 16), 6, None, AL.logical_shift_right)
+        if last:
+            site(0, 32, "psP1")
+        tt(B(sown[1]), B("bn"), srcl, AL.add)
+        if last:
+            putlist(32, V, "psD")
+        tt(B("d5"), B("sc"), B("F"), AL.subtract)
+        ts(B("h1"), B(sown[1]), 13.0, None, AL.mult)
+        if last:
+            putlist(0, 32, "psP1")
+        tt(B("d6"), B("d5"), acc, AL.mult)
+        tt(B("h2"), B("h1"), B("sc"), AL.add)
+        ts(B("h3"), B("h2"), 255, None, AL.bitwise_and)
+        tt(B("d3"), B("h3"), n2, AL.subtract)
+        if not last:
+            tt(B("F"), B("d6"), B("F"), AL.add)
+            tt(B("d4"), B("d3"), acc, AL.mult)
+            tt(B(nown[1]), B("d4"), n2, AL.add)
+            swap((nown[1], 0), 48)
+            vcopy(B("acc%d" % t, 0, 16), acc)
+            vcopy(B("acc%d" % t, 16, 32), acc)
+            vcopy(B("n0U"), B("psS", 48, 64))
+            k = 0
+            for r in range(t + 1):
+                for s in range(8):
+                    mm(B("psS", 64, 80), B("BLK32"), B("acc%d" % r, 2 * s, 2 * s + 16), k == 0, k == 8 * (t + 1) - 1)
+                    k += 1
+            vcopy(B("Ai"), B("psS", 64, 80))
+            ts(B("A7"), B("Ai"), 7, None, AL.bitwise_and)
+            tt(B("thr"), B("F"), B("A7"), AL.subtract)
+            ts(B("thr"), B("thr"), 64.0, None, AL.mult)
+            nown, sown = nown[::-1], sown[::-1]
+        else:
+            tt(B("B2", 0, 256, 16), B("d6"), B("F"), AL.add)
+            tt(B("d4"), B("d3"), acc, AL.mult)
+            tt(B("B2", 1, 256, 16), B("d4"), n2, AL.add)
+            vtrans(B("oT"), B("B2"))
+            op("s", lambda e: e.dma_start(T.yf[:], T.oT[0:128:16, :]), [B("oT")], [], sem="st1", inc=16)
+            op("a", lambda e: e.dma_start(T.yn[:], T.oT[1:128:16, :]), [B("oT")], [], sem="st2", inc=16)
+    for s in sorted(total):
+        if known["g"].get(s, 0) < total[s]:
+            g.wait_ge(T.sem[s], total[s])

@@ -5,21 +5,27 @@ from concourse.mybir import dt, AluOpType, AxisListType, ActivationFunctionType
 AL = AluOpType
 AF = ActivationFunctionType
 NR = 3
-V = 256
-DS, DE = 16, 128
-NA, ND = DS + V - DE, DE - DS
-ABLK = [(DE + (V - DE) * i // 4, DE + (V - DE) * (i + 1) // 4) for i in range(4)]
-ALATE = (0, DS)
-DBLK = [(32, 64), (64, 96), (96, DE)]
-DLATE = (DS, 32)
-CHUNKS = [[("A", DE, DE + 16)], [("A", DE + 16, DE + 80)], [("A", DE + 80, V)],
-          [("D", 32, 64), ("D", 64, 96)], [("D", 96, DE)], [("A", 0, DS), ("D", DS, 32)]]
-ORDER = ["A0", "D0", "A1", "D1", "A2", "D2", "A3"]
-KEYBANK = [(0, 32, "psKB"), (32, DE, "psKC"), (DE, V, "psKA")]
-PAY = 272
+NT = 2 * NR
 CUT = 1024
-BIG = 33554432.0
 MAGIC = 1.5 * 2.0 ** 31
+CH = 2048
+
+
+def pieces(on_scalar, folded, cut=32):
+    out, s = [], 0
+    while s < 768:
+        e = min(s + (64 if s < on_scalar else cut), s // 128 * 128 + 128)
+        e = min([e] + [x for x in (on_scalar, folded) if x > s])
+        out.append(("a" if s < on_scalar else "v", s // 128, s % 128, s % 128 + e - s, s < folded))
+        s = e
+    return out
+
+
+SHARE = [(576, 320)] * (NT - 1) + [(576, 256)]
+NU = 12
+PLAN = {"cycle": 0.00087, "pe": 0.00044, "gather": 1.5, "wake": 0.17, "issue": 0.5, "first": 1.0, "load": 1.4, "rate": 150e3,
+        "fold": 2.1, "landed": 0.7, "message": 3.8, "passes": 400, "leash": 2.0, "move": 0.3, "lift": 1.0,
+        "turn": 13, "tail": 0.4, "from": 0.1, "to": 1.1, "soon": 0.15, "first_z": 2, "before": 9}
 
 
 def sb(cols, kind="bfloat16"):
@@ -27,34 +33,32 @@ def sb(cols, kind="bfloat16"):
 
 
 SCRATCH = {
-    "S": sb(4096), "obs_s": sb(256), "nobs": sb(256, "float32"), "Xe": sb(ND * 48),
-    "rawR": sb(256, "int32"), "raws": sb(16, "int32"), "rawn": sb(16, "int32"),
-    "fitb": sb(256, "int32"), "fitf": sb(256, "float32"), "fitt": sb(256, "float32"),
-    "W0": sb(1040), "W1": sb(1040), "W2": sb(1040), "land0": sb(PAY), "land1": sb(PAY), "land2": sb(PAY),
-    "LQ1": sb(256), "LQ2": sb(256), "srcU": sb(16, "uint16"), "n0U": sb(16, "uint16"), "offB": sb(32, "uint16"),
-    "B1": sb(256), "X": sb(256), "X2": sb(256), "nX": sb(512), "T12": sb(512),
-    "off": sb(1536, "uint16"), "odd": sb(1536, "float32"),
-    "v1a": sb(384, "int32"), "v1b": sb(384, "int32"), "v2a": sb(384, "int32"), "v2b": sb(384, "int32"),
-    "pen": sb(768), "A": sb(NA * 96), "dd": sb(ND * 96), "rr": sb(ND * 96),
-    "z1": sb(768, "float32"), "tr": sb(256, "float32"), "s2": sb(256, "int32"),
-    "sc": sb(16, "int32"), "z16": sb(16, "int32"), "st": sb(16, "int32"), "SWa": sb(32),
-    "acc0": sb(32), "acc1": sb(32), "IND": sb(48), "PQ": sb(48), "TP": sb(48),
-    "nL": sb(16), "nLn": sb(16), "srcA": sb(16), "srcB": sb(16),
-    "F": sb(16, "float32"), "thr": sb(16, "float32"), "Ai": sb(16, "int32"), "A7": sb(16, "int32"),
-    "b1": sb(16, "float32"), "bn": sb(16, "float32"), "h1": sb(16, "float32"), "h2": sb(16, "int32"), "h3": sb(16, "int32"),
-    "d3": sb(16, "float32"), "d4": sb(16, "float32"), "d5": sb(16, "float32"), "d6": sb(16, "float32"),
-    "Rb": sb(256), "OH": sb(256), "md": sb(256), "Rf": sb(256, "float32"), "B2": sb(256, "float32"), "oT": sb(256, "float32"),
-    "ones": sb(128), "I": sb(128), "BLK": sb(128), "TRI": sb(128), "TMO": sb(128), "IMO": sb(128), "NBLK": sb(128), "BIGI": sb(128),
-    "BLK32": sb(128), "B48": ("sbuf", [128, 8, 48], "bfloat16"), "WT": ("sbuf", [128, 248, 16], "bfloat16"), "E": sb(512), "E16": sb(512),
-    "c4096": sb(64), "cm127": sb(160), "pi": sb(1, "int32"), "pj": sb(1, "int32"), "jcol": sb(1, "float32"),
-    "kct": sb(120, "float32"), "KC": sb(120), "ilt": sb(16, "float32"), "ilist": sb(16), "zit": sb(16, "float32"), "ZI": sb(16),
-    "RS3": sb(420, "float32"), "RS16": sb(256, "float32"),
-    "psP0": ("psum", [128, 512], "float32"), "psP1": ("psum", [128, 512], "float32"), "psQ": ("psum", [128, 512], "float32"),
-    "psKA": ("psum", [128, 512], "float32"), "psKB": ("psum", [128, 512], "float32"), "psKC": ("psum", [128, 512], "float32"),
-    "psS": ("psum", [128, 512], "float32"), "psD": ("psum", [128, 512], "float32"),
+    "rawR": sb(256, "int32"), "raws": sb(16, "int32"), "rawn": sb(16, "int32"), "fitb": sb(256, "int32"), "fitf": sb(256, "float32"),
+    "M0": sb(272), "land": sb(272), "nl": sb(16), "Lx": sb(256), "LxN": sb(256), "LxS": sb(256),
+    "nXa": sb(128), "nXb": sb(128), "s1": sb(128), "v1": sb(768, "int32"), "v2": sb(768, "int32"), "q16": sb(256, "int32"), "q64": sb(128, "int32"),
+    "best": sb(8, "int32"), "bi": sb(16, "int32"), "sc": sb(8, "int32"), "Lz": sb(64), "Ln": sb(64), "offW": sb(8, "uint16"),
+    "Rb": sb(128), "mask": sb(128), "md": sb(128), "h2": sb(8, "int32"), "h3": sb(8, "int32"), "d3": sb(8, "float32"), "d4": sb(8, "float32"),
+    "Ai": sb(8, "int32"), "u": sb(8, "float32"), "Fn": sb(8, "float32"), "Tn": sb(8, "float32"),
+    "qi": sb(256, "int32"), "pi": sb(1, "int32"), "ci": sb(16, "int32"), "cf": sb(16, "float32"), "row": sb(640, "int32"),
+    "ones": sb(128), "seven": sb(128), "I": sb(128), "NI": sb(128), "I13": sb(128), "I32": sb(128, "float32"), "BLK": sb(128), "NBLK": sb(128),
+    "TRI": sb(128), "TMO": sb(128), "IMO": sb(128), "DUP": sb(384), "SWP": sb(128), "DUPB": sb(128), "MASKR": sb(256), "RSM": sb(128),
+    "W128": sb(128), "Wm64": sb(128), "BIGP": sb(128), "WX": sb(384), "cnt": sb(256), "KC": sb(384), "BB": sb(32), "EW": sb(240),
+    "mA8": sb(64), "mA1": sb(64), "idx": sb(32, "uint16"), "thrc": sb(32), "RX": sb(256), "site": sb(128), "SEL": sb(8), "ilist": sb(8),
+    "odd": sb(256, "float32"), "c4096": sb(256), "cm127": sb(128), "obsM": sb(768),
+    "psK0": ("psum", [128, 512], "float32"), "psK1": ("psum", [128, 512], "float32"), "psP0": ("psum", [128, 512], "float32"),
+    "psP1": ("psum", [128, 512], "float32"), "psQ": ("psum", [128, 512], "float32"), "psX": ("psum", [128, 512], "float32"),
+    "psD": ("psum", [128, 512], "float32"), "psE": ("psum", [128, 512], "float32"),
 }
-SEMAPHORES = (["qv", "qa", "qp", "qg", "go", "ldf"] + ["ld%d" % i for i in range(6)] + ["st%d" % i for i in range(4)]
-              + ["%s%s%d" % (n, p, t) for n in ("arr", "hop", "loc", "hl") for t in range(NR) for p in "EL"])
+for x in range(2):
+    SCRATCH.update({n + str(x): v for n, v in {
+        "S": sb(4096), "obs": sb(128), "Xe": sb(CH), "W": sb(NR * 512), "ld": sb(512), "Tb": sb(512), "nU": sb(24, "uint16"),
+        "off": sb(768, "uint16"), "pen": sb(384), "Sg": sb(6 * CH), "Mx": sb(6 * CH), "Fh": sb(6 * CH), "FLD": sb(128), "DT": sb(512), "T1s": sb(128),
+        "NX": sb(8), "SR": sb(8), "IND": sb(NR * 32), "A7": sb(8, "int32"), "Rf": sb(128, "float32"), "OF": sb(16, "float32"),
+        "oT": sb(128, "float32")}.items()})
+SEMAPHORES = (["qv", "qa", "qp", "qg", "go", "hb"] + ["ld%d" % i for i in range(15)] + ["st%d" % i for i in range(8)]
+              + ["%s%d%d" % (n, m, p) for n in ("arr", "hop", "loc") for m in range(NT - 1) for p in range(2)]
+              + ["%s%d%d" % (n, x, u) for n in ("fa", "fb") for x in range(2) for u in range(NU)])
+ORDER = {}
 
 
 def route(q, t, cores, topo):
@@ -68,43 +72,172 @@ def route(q, t, cores, topo):
     return dst, None
 
 
-def pick(src, dst, topo):
+def helper(c, cores, topo):
+    used = [route(q, t, cores, topo)[1] for q in range(len(cores)) for t in range(NR)]
+    return [x for x in topo.cores_of(c) if x not in cores and x not in used and topo.die(x) == topo.die(c)][0]
+
+
+def lane(c, hc, u, topo):
+    return topo.engines(c, hc)
+
+
+def pick(src, dst, topo, ranks=()):
     e = topo.engines(src, dst)[:8]
     return sum(1 << i for i in e), len(e)
 
 
-def pieces(t):
-    return [("L", 0, 16), ("E", 16, PAY)] if t == 0 else [("E", 0, PAY)]
+def message(m):
+    if m == 0:
+        return 0, "land", [(0, 272)]
+    t, x = (m + 1) // 2, (m + 1) % 2
+    return t, "ld%d" % x, [(256 * (t - 1), 256 * (t - 1) + 128), (256 * (t - 1) + 128, 256 * t)]
 
 
-def relay_program(g, core, T, topo):
-    held = []
-    for t in range(NR):
+def folds(n):
+    return [(c, a, b) for e, c, a, b, f in pieces(*SHARE[n]) if f]
+
+
+def held(n):
+    return ["Mx", "Sg", "Fh"][n // 2] + str(n % 2)
+
+
+def other_program(g, core, T, topo):
+    sent = 0
+    for c in T.cores:
+        if helper(c, T.cores, topo) == core:
+            rid, pid = topo.addr(c, core)
+            seen = {}
+            for n in range(NT):
+                for u, (ch, a, b) in enumerate(folds(n)):
+                    s = "%d%d" % (n % 2, u)
+                    seen[s] = seen.get(s, 0) + len(lane(c, core, u, topo))
+                    lo, hi = CH * ch + 16 * a, CH * ch + 16 * b
+                    g.wait_ge(T.sem["fa" + s], seen[s])
+                    g.remote_dma(out_ap=T["Mx%d" % (n % 2)][:, lo:hi], in_ap=T[held(n)][:, lo:hi], remote_sem=T.sem["fb" + s],
+                                 local_sem=T.sem["hb"], pid=pid, routing_id=rid, dma_engine_mask=topo.mask(core, c))
+                    sent += len(topo.engines(core, c))
+    for m in range(NT - 1):
+        t, land, parts = message(m)
         for q in range(len(T.cores)):
             dst, via = route(q, t, T.cores, topo)
             if via != core:
                 continue
-            _, n1 = pick(T.cores[q], core, topo)
-            m, n2 = pick(core, dst, topo)
+            mask, n2 = pick(core, dst, topo)
             rid, pid = topo.addr(dst, core)
-            for p, a, b in pieces(t):
-                land = T["land%d" % t][:, a:b]
-                g.wait_ge(T.sem["hop%s%d" % (p, t)], n1)
-                g.remote_dma(out_ap=land, in_ap=land, remote_sem=T.sem["arr%s%d" % (p, t)], local_sem=T.sem["hl%s%d" % (p, t)],
-                             pid=pid, routing_id=rid, dma_engine_mask=m)
-                held.append(("hl%s%d" % (p, t), n2))
-    for s, n in held:
-        g.wait_ge(T.sem[s], n)
+            for p, (a, b) in enumerate(parts):
+                g.wait_ge(T.sem["hop%d%d" % (m, p)], pick(T.cores[q], core, topo, T.cores if m else ())[1])
+                g.remote_dma(out_ap=T[land][:, a:b], in_ap=T[land][:, a:b], remote_sem=T.sem["arr%d%d" % (m, p)], local_sem=T.sem["hb"],
+                             pid=pid, routing_id=rid, dma_engine_mask=mask)
+                sent += n2
+    if sent:
+        g.wait_ge(T.sem["hb"], sent)
+
+
+def clash(r, v):
+    s = v[4]
+    return r[2] < v[3] and v[2] < r[3] and not (s > 1 and s == r[4] and (r[2] - v[2]) % s)
+
+
+def covers(v, r):
+    s = v[4]
+    return v[5] and v[2] <= r[2] and r[3] <= v[3] and (s == 1 or (s == r[4] and (r[2] - v[2]) % s == 0))
+
+
+def arrange(steps):
+    wake, n = PLAN["wake"], len(steps)
+    pred, rec, bank = [dict() for _ in steps], {}, {}
+
+    def edge(a, b, data):
+        sa = steps[a]
+        lat = sa["lat"] + wake if data or sa["q"] != steps[b]["q"] or sa["lat"] else 0.0
+        if a != b and pred[b].get(a, -1.0) < lat:
+            pred[b][a] = lat
+    for i, st in enumerate(steps):
+        for a in st["after"]:
+            pred[i][a] = -steps[a]["bytes"] / PLAN["rate"]
+        views = [("r", v) for v in st["reads"]] + [("w", v) for v in st["writes"] + st["ghost"]]
+        for b in {v[1] for k, v in views if v[1][:2] == "ps"}:
+            last, loose = bank.get(b, ([], []))
+            for a in last + ([] if st["loose"] else loose):
+                edge(a, i, steps[a]["q"] != "p" and b in [v[1] for v in steps[a]["writes"]])
+            bank[b] = (last, loose + [i]) if st["loose"] else ([i], [])
+        for k, v in views:
+            for k2, r, a in rec.get(v[1], []) if v[1][:2] != "ps" else []:
+                if (k == "w" or k2 == "w") and clash(r, v) and not (st["load"] and steps[a]["load"]):
+                    edge(a, i, True)
+        for k, v in views:
+            if v[1][:2] != "ps":
+                rec[v[1]] = [e for e in rec.get(v[1], []) if not (k == "w" and covers(v, e[1]))] + [(k, v, i)]
+    span = [st["cost"] + st["bytes"] / PLAN["rate"] * (1 / st["lane"] + st["back"]) + (PLAN["fold"] if st["back"] else 0) for st in steps]
+    ahead = [max(span[i] + st["lat"], (NT + PLAN["tail"] - st["due"]) * PLAN["turn"]) for i, st in enumerate(steps)]
+    for i in range(n - 1, -1, -1):
+        for a, lat in pred[i].items():
+            ahead[a] = max(ahead[a], (span[a] + lat if lat >= 0 else steps[a]["cost"]) + ahead[i])
+    succ = [dict() for _ in steps]
+    for i in range(n):
+        for a, lat in pred[i].items():
+            succ[a][i] = lat
+
+    def place(order, before, back):
+        start, end, busy = [0.0] * n, [0.0] * n, {}
+        for i in order:
+            st = steps[i]
+            parts = [(st["q"], st["cost"])] + ([(st["lane"], st["bytes"] / PLAN["rate"] / st["lane"])] if st["bytes"] else [])
+            if st["back"]:
+                parts += [(-i, PLAN["fold"]), ("helper", st["bytes"] / PLAN["rate"])]
+            t = max([end[a] + lat if lat >= 0 or back else start[a] + steps[a]["cost"] for a, lat in before[i].items()]
+                    + [st["lat"] if back else 0.0])
+            for j, (q, d) in enumerate(parts[::-1] if back else parts):
+                L, k = busy.setdefault(q, []), 0
+                lo, hi = 0, len(L)
+                while lo < hi:
+                    mid = (lo + hi) // 2
+                    lo, hi = (mid + 1, hi) if L[mid][1] <= t else (lo, mid)
+                for k in range(lo, len(L) + 1):
+                    if k == len(L) or t + d <= L[k][0]:
+                        break
+                    t = max(t, L[k][1])
+                L.insert(k, (t, t + d))
+                if j == 0:
+                    start[i] = t
+                t += d
+            end[i] = t
+        return start, end
+    best, rank, seed = None, list(ahead), 1
+    for _ in range(PLAN["passes"]):
+        start, end = place(sorted(range(n), key=lambda i: (-rank[i], i)), pred, False)
+        i = max(range(n), key=lambda i: end[i] + steps[i]["lat"])
+        length = end[i] + steps[i]["lat"]
+        if best is None or length < best[1]:
+            best = (sorted(range(n), key=lambda i: (start[i], i)), length, list(rank))
+        elif length > best[1] + PLAN["leash"]:
+            rank = list(best[2])
+        ends = {(steps[a]["q"], round(start[a] + steps[a]["cost"], 6)): a for a in range(n)}
+        while i is not None:
+            ready = [(end[a] + lat if lat >= 0 else start[a] + steps[a]["cost"], a) for a, lat in pred[i].items()]
+            t, a = max(ready + [(0.0, None)], key=lambda v: v[0])
+            if start[i] > t + 1e-6:
+                a = ends.get((steps[i]["q"], round(start[i], 6)), a)
+                seed = (seed * 1103515245 + 12345) % 2 ** 31
+                if seed >> 16 < PLAN["move"] * 2 ** 15:
+                    rank[i] += min(start[i] - t, PLAN["lift"])
+            i = a
+        for i in range(n - 1, -1, -1):
+            for a in pred[i]:
+                rank[a] = max(rank[a], rank[i] + 1e-4)
+    return best[:2]
 
 
 def rank_program(g, core, T, topo):
     rank = T.rank_of(core)
     if rank is None:
-        relay_program(g, core, T, topo)
+        other_program(g, core, T, topo)
         return
     ENG = {"v": g.vector, "a": g.scalar, "p": g.tensor, "g": g, "s": g.sync}
     total, known, hist, rec, bank = {}, {k: {} for k in ENG}, {}, {}, {}
-    nload = [0]
+    ndma = {"ld": 0, "st": 0}
+    steps, name, tile = [], [""], {}
+    cyc = PLAN["cycle"]
 
     def need(want, tok):
         s, c = tok
@@ -125,18 +258,7 @@ def rank_program(g, core, T, topo):
                 ENG[q].wait_ge(T.sem[s], c)
                 learn(q, s, c)
 
-    def step(v):
-        return v[4] if len(v) > 4 else 1
-
-    def clash(r, v):
-        s = step(v)
-        return r[1] < v[3] and v[2] < r[2] and not (s > 1 and s == r[5] and (r[1] - v[2]) % s)
-
-    def covers(v, r):
-        s = step(v)
-        return v[2] <= r[1] and r[2] <= v[3] and (s == 1 or (s == r[5] and (r[1] - v[2]) % s == 0))
-
-    def op(q, fn, reads, writes, sem=None, inc=1, then=True):
+    def issue(q, fn, reads, writes, sem, inc, then):
         own = sem is None
         s = "q" + q if own else sem
         tag = q if own else "x" + sem
@@ -146,14 +268,19 @@ def rank_program(g, core, T, topo):
                 for a, tok in bank.get(v[1], {}).items():
                     if a != tag:
                         need(want, tok)
+                if q == "p":
+                    shape = (reads[0][7], reads[0][6], v[6])
+                    if tile.get(v[1], shape) != shape and "p" in bank[v[1]]:
+                        need(want, bank[v[1]]["p"])
+                    tile[v[1]] = shape
         for v in reads:
-            for r in rec.get(v[1], []):
-                if r[0] == "w" and clash(r, v):
-                    need(want, r[4])
+            for k, r, tg, tok in rec.get(v[1], []):
+                if k == "w" and clash(r, v):
+                    need(want, tok)
         for v in writes:
-            for r in rec.get(v[1], []):
-                if (r[3] != tag or r[0] == "w") and clash(r, v):
-                    need(want, r[4])
+            for k, r, tg, tok in rec.get(v[1], []):
+                if clash(r, v) and not (tg[:3] == "xld" and tag[:3] == "xld"):
+                    need(want, tok)
         wait(q, want)
         ins = fn(ENG[q])
         total[s] = total.get(s, 0) + inc
@@ -161,475 +288,480 @@ def rank_program(g, core, T, topo):
         if then:
             ins.then_inc(T.sem[s], inc)
         hist[tok] = dict(known[q])
-        for v in reads:
-            if v[1][:2] == "ps":
-                bank.setdefault(v[1], {})[tag] = tok
-                continue
-            L = [r for r in rec.get(v[1], []) if not (r[0] == "r" and r[3] == tag and covers(v, r))]
-            L.append(("r", v[2], v[3], tag, tok, step(v)))
-            rec[v[1]] = L
-        for v in writes:
-            if v[1][:2] == "ps":
-                bank.setdefault(v[1], {})[tag] = tok
-                continue
-            L = [r for r in rec.get(v[1], []) if not covers(v, r)]
-            L.append(("w", v[2], v[3], tag, tok, step(v)))
-            rec[v[1]] = L
-        return tok
+        for kind, views in (("r", reads), ("w", writes)):
+            for v in views:
+                if v[1][:2] == "ps":
+                    bank.setdefault(v[1], {})[tag] = tok
+                    if q == "p":
+                        continue
+                L = [e for e in rec.get(v[1], []) if not ((kind == "w" or (e[0] == "r" and e[2] == tag)) and covers(v, e[1]))]
+                rec[v[1]] = L + [(kind, v, tag, tok)]
 
-    def arrived(name, lo, hi, sem, n):
-        total[sem] = total.get(sem, 0) + n
-        rec.setdefault(name, []).append(("w", lo, hi, "x" + sem, (sem, total[sem]), 1))
+    def op(q, fn, reads, writes, cost, sem=None, inc=1, then=True, join=False, **more):
+        call = (q, fn, reads, writes, sem, inc, then)
+        if join:
+            st = steps[-1]
+            st["calls"].append(call)
+            st["reads"], st["writes"], st["cost"] = st["reads"] + reads, st["writes"] + writes, st["cost"] + cost
+        else:
+            steps.append(dict({"q": q, "calls": [call], "reads": reads, "writes": writes, "cost": cost, "lat": 0.0, "bytes": 0, "after": [],
+                               "ghost": [], "loose": False, "load": False, "back": False, "due": 99, "lane": 1, "name": name[0]}, **more))
+        return len(steps) - 1
 
-    def B(name, lo=0, hi=None, step=1):
+    def B(name, lo=0, hi=None, step=1, p=None):
         t = T[name]
         hi = t.shape[1] if hi is None else hi
-        return (t[:, lo:hi] if step == 1 else t[:, lo:hi:step], name, lo, hi, step)
+        a, b = p or (0, 128)
+        return (t[a:b, lo:hi] if step == 1 else t[a:b, lo:hi:step], name, lo, hi, step, p is None, b - a, a)
 
     def ind(win, of):
         return win[0].indirect(of[0])
 
+    def cols(v):
+        return (v[3] - v[2] + v[4] - 1) // v[4]
+
+    def stream(out, *ins):
+        narrow = all(SCRATCH[v[1]][0] == "sbuf" and SCRATCH[v[1]][2] in ("bfloat16", "uint16") for v in (out,) + ins)
+        return max(64, cols(out) * (0.5 if narrow else 1)) * cyc
+
+    def picked(out):
+        return (65 + cols(out) * PLAN["gather"]) * cyc
+
     def tt(out, a, b, o):
-        return op("v", lambda e: e.tensor_tensor(out[0], a[0], b[0], o), [a, b], [out])
+        c = max(64, cols(out) * (1 if "ps" in (a[1][:2], b[1][:2]) else 2)) * cyc
+        return op("v", lambda e: e.tensor_tensor(out[0], a[0], b[0], o), [a, b], [out], c)
 
-    def ts(out, a, s1, s2, o0, o1=None, col=None):
-        x = col[0] if col else s1
+    def gtt(out, win, of, b, o):
+        return op("v", lambda e: e.tensor_tensor(out[0], ind(win, of), b[0], o), [win, of, b], [out], picked(out))
+
+    def ts(out, a, s1, s2, o0, o1=None):
+        col = [s for s in (s1, s2) if isinstance(s, tuple)]
+        x, y = [s[0] if isinstance(s, tuple) else s for s in (s1, s2)]
         if o1 is None:
-            return op("v", lambda e: e.tensor_scalar(out[0], a[0], x, None, o0), [a] + ([col] if col else []), [out])
-        return op("v", lambda e: e.tensor_scalar(out[0], a[0], x, s2, o0, o1), [a] + ([col] if col else []), [out])
+            return op("v", lambda e: e.tensor_scalar(out[0], a[0], x, None, o0), [a] + col, [out], stream(out, a))
+        return op("v", lambda e: e.tensor_scalar(out[0], a[0], x, y, o0, o1), [a] + col, [out], stream(out, a))
 
-    def vcopy(out, a):
-        return op("v", lambda e: e.tensor_copy(out[0], a[0]), [a], [out])
+    def copy(out, a, q="v", scale=None):
+        if q == "v":
+            return op("v", lambda e: e.tensor_copy(out[0], a[0]), [a], [out], stream(out, a))
+        c = max(64, cols(out)) * cyc
+        if scale is None:
+            return op("a", lambda e: e.activation(out[0], a[0], AF.Copy), [a], [out], c)
+        return op("a", lambda e: e.activation(out[0], a[0], AF.Copy, scale=scale), [a], [out], c)
 
-    def acopy(out, a):
-        return op("a", lambda e: e.activation(out[0], a[0], AF.Copy), [a], [out])
-
-    def vgather(out, win, of):
-        return op("v", lambda e: e.tensor_copy(out[0], ind(win, of)), [win, of], [out])
-
-    def agather(out, win, of):
-        return op("a", lambda e: e.activation(out[0], ind(win, of), AF.Copy), [win, of], [out])
-
-    def vtrans(out, a):
-        return op("v", lambda e: e.transpose(out[0], a[0]), [a], [out])
+    def gather(out, win, of, q="v"):
+        if q == "v":
+            return op("v", lambda e: e.tensor_copy(out[0], ind(win, of)), [win, of], [out], picked(out))
+        return op("a", lambda e: e.activation(out[0], ind(win, of), AF.Copy), [win, of], [out], picked(out))
 
     def memset(out, c):
-        return op("v", lambda e: e.memset(out[0], c), [], [out])
+        return op("v", lambda e: e.memset(out[0], c), [], [out], stream(out))
 
-    def scan(out, d0, d1):
-        return op("v", lambda e: e.tensor_tensor_scan(out[0], d0[0], d1[0], 0.0, AL.add, AL.min), [d0, d1], [out])
+    def running_sum(out, keep, a):
+        return op("v", lambda e: e.tensor_tensor_scan(out[0], keep[0], a[0], 0.0, AL.mult, AL.add), [keep, a], [out], stream(out, a))
 
-    def mm(out, l, r, start, stop):
-        return op("p", lambda e: e.matmul(out[0], l[0], r[0], start, stop), [l, r], [out])
+    def least(out, a):
+        return op("v", lambda e: e.tensor_reduce(out[0], a[0], AxisListType.X, AL.min), [a], [out], 64 * cyc)
 
-    def load(q, out, src):
-        k = nload[0]
-        nload[0] += 1
-        return op(q, lambda e: e.dma_start(out[0], src), [], [out], sem="ld%d" % k, inc=16)
+    def mm(out, l, r, start, stop, join=False, **more):
+        def fn(e):
+            if isinstance(stop, list):
+                stop[0] -= 1
+                return e.matmul(out[0], l[0], r[0], start, stop[0] == 0)
+            return e.matmul(out[0], l[0], r[0], start, stop)
+        if isinstance(stop, list):
+            stop[0] += 1
+        return op("p", fn, [l, r], [out], max(64, cols(r)) * PLAN["pe"], join=join, **more)
 
-    def store(q, out, src, sem):
-        return op(q, lambda e: e.dma_start(out, src[0]), [src], [], sem=sem, inc=16)
+    def mms(out, pairs):
+        for i, (l, r) in enumerate(pairs):
+            mm(out, l, r, i == 0, i == len(pairs) - 1, i > 0)
 
-    def iota(out, pattern, base, cm, f=True):
-        if f:
-            return op("g", lambda e: e.iota(out[0], pattern, base, cm, allow_small_or_imprecise_dtypes=True), [], [out])
-        return op("g", lambda e: e.iota(out[0], pattern, base, cm), [], [out])
+    def turn_over(out, a, ident):
+        return op("p", lambda e: e.transpose(out[0], a[0], ident[0]), [a, ident], [out], 512 * PLAN["pe"])
 
-    def sel(out, a, pattern, cmp, base, cm):
-        return op("g", lambda e: e.affine_select(out[0], a[0], pattern, cmp, 0.0, base, cm), [a], [out])
+    def dma(q, kind, out, src, reads, writes, v):
+        k = ndma[kind]
+        ndma[kind] += 1
+        size = v[6] * cols(v) * (2 if SCRATCH[v[1]][2] == "bfloat16" else 4)
+        return op(q, lambda e: e.dma_start(out, src), reads, writes, 0.1, sem="%s%d" % (kind, k), inc=16, lat=PLAN["load"], bytes=size,
+                  load=kind == "ld")
 
-    def apos(s):
-        return s if s < DS else s - ND
+    def load(q, out, src, reads=()):
+        return dma(q, "ld", out[0], src, list(reads), [out], out)
 
-    def weight(gh, k):
-        n = 15 * gh + k
-        return (T.WT[:, 8 * n:8 * n + 8, :], "WT", n, n + 1)
+    def store(q, out, src):
+        return dma(q, "st", out, src[0], [src], [], src)
 
-    def put_weight(gh, k, q):
-        lo = 15 - k if gh == 0 else 31 - k
-        (vcopy if q == "v" else acopy)(weight(gh, k), (T.B48[:, :, lo:lo + 16], "B48", 0, 384))
+    def iota(out, pattern, base, cm):
+        c = (160 + 2 * cols(out)) * cyc
+        if SCRATCH[out[1]][2] == "int32":
+            return op("g", lambda e: e.iota(out[0], pattern, base, cm), [], [out], c)
+        return op("g", lambda e: e.iota(out[0], pattern, base, cm, allow_small_or_imprecise_dtypes=True), [], [out], c)
 
-    def swap(field, col, extra=None, name="E", a=0, b=16):
-        fb, fo = field
-        for h in range(2):
-            o = B("psS", col + a + h, col + b, 2)
-            if extra is not None:
-                mm(o, B("I"), B(extra, a + h, b, 2), True, False)
-            for e in range(2):
-                k = 128 * (2 * e + h)
-                mm(o, B(name, k, k + 128), B(fb, fo + a + e, fo + b, 2), extra is None and e == 0, e == 1)
+    sends, folded, scalar_last, placed = [], [], [], {}
 
-    W = ["W0", "W1", "W2"]
-    load("s", B("rawR"), T.resid[:])
-    load("a", B("raws"), T.src0[:])
-    load("a", B("rawn"), T.nx0[:])
-    load("s", B("S", 0, CUT), T.prof[:, 0:CUT])
-    load("a", B("obs_s"), T.obs[:])
-    memset(B("ones"), 1.0)
-    memset(B("E"), 0.0)
-    memset(B("fitb"), 0)
-    op("v", lambda e: e.memset(T.B48[:, :, 0:16], 0.0), [], [("", "B48", 0, 384)])
-    op("v", lambda e: e.memset(T.B48[:, :, 16:32], 64.0), [], [("", "B48", 0, 384)])
-    op("v", lambda e: e.memset(T.B48[:, :, 32:48], 0.0), [], [("", "B48", 0, 384)])
-    op("a", lambda e: e.dma_start(T.fitb[0:128:16, :], T.fit0[:]), [], [B("fitb")], sem="ldf", inc=16)
-    iota(B("pi"), [[0, 1]], 0, 1, False)
-    sel(B("I"), B("ones"), [[-1, 128]], AL.is_equal, 0, 1)
-    iota(B("ilt"), [[16, 16]], 0, 0)
-    iota(B("zit"), [[1, 16]], 0, 0)
-    sel(B("BLK"), B("ones"), [[-16, 8], [0, 16]], AL.is_ge, 0, 1)
-    sel(B("BLK"), B("BLK"), [[16, 8], [0, 16]], AL.is_ge, 15, -1)
-    memset(B("RS3"), 0.0)
-    memset(B("RS3", 0, 420, 3), BIG)
-    vcopy(B("W0", 0, 16), B("raws"))
-    vcopy(B("W0", 16, PAY), B("rawR"))
-
-    def send(t, piece):
-        p, a, b = piece
+    def send(m, p, *src):
+        t, land, parts = message(m)
+        a, b = parts[p]
         dst, via = route(rank, t, T.cores, topo)
         to = dst if via is None else via
-        m, n = pick(core, to, topo)
+        mask, n = pick(core, to, topo, T.cores if m else ())
         rid, pid = topo.addr(to, core)
-        rs, ls = T.sem["%s%s%d" % ("arr" if via is None else "hop", p, t)], "loc%s%d" % (p, t)
-        src = B(W[t], a, b)
-        op("g", lambda e: e.remote_dma(out_ap=T["land%d" % t][:, a:b], in_ap=src[0], remote_sem=rs, local_sem=T.sem[ls],
-                                       pid=pid, routing_id=rid, dma_engine_mask=m), [src], [], sem=ls, inc=n, then=False)
+        rs, ls = T.sem["%s%d%d" % ("arr" if via is None else "hop", m, p)], "loc%d%d" % (m, p)
+        tr = RemoteDMATransfer(dst_ids=[DstId(rid=rid, pnc=pid)], dma_engine_mask=mask, remote_sem=rs, srcs=[v[0] for v in src],
+                               dsts=[T[land][:, a:b]], alu_op=len(src) - 1)
+        sends.append(op("g", lambda e: e.remote_dma_fused([tr], local_sem=T.sem[ls]),
+                        list(src), [], PLAN["issue"] + (0 if sends else PLAN["first"]), sem=ls, inc=n, then=False, ghost=[B(land, a, b)],
+                        lat=PLAN["message"] + (0 if sends else PLAN["first"]), bytes=512 * (b - a), after=sends[-1:]))
 
-    def expect(t):
+    for m in range(NT - 1):
+        t, land, parts = message(m)
         for q in range(len(T.cores)):
             dst, via = route(q, t, T.cores, topo)
             if dst == core:
-                for p, a, b in pieces(t):
-                    arrived("land%d" % t, a, b, "arr%s%d" % (p, t), pick(T.cores[q] if via is None else via, core, topo)[1])
+                for p, (a, b) in enumerate(parts):
+                    s = "arr%d%d" % (m, p)
+                    total[s] = pick(T.cores[q] if via is None else via, core, topo, T.cores if m else ())[1]
+                    rec.setdefault(land, []).append(("w", B(land, a, b), "x" + s, (s, total[s])))
 
-    for piece in pieces(0):
-        send(0, piece)
-    g.sem_inc(T.sem["go"], 1)
-    total["go"] = 1
-    g.sync.wait_ge(T.sem["go"], 1)
-    load("s", B("S", CUT, 4096), T.prof[:, CUT:4096])
-    sel(B("TRI"), B("BLK"), [[1, 128]], AL.is_ge, 0, -1)
-    iota(B("kct"), [[0, 40], [16, 3]], 16, 0)
-    b48 = (T.B48[:], "B48", 0, 384)
-    sel(b48, b48, [[-16, 8], [0, 48]], AL.is_ge, 0, 1)
-    sel(b48, b48, [[16, 8], [0, 48]], AL.is_ge, 15, -1)
-    iota(B("odd", 6 * DE, 1536), [[2, V - DE], [0, 6]], 2 * DE + 1, 0)
-    iota(B("odd", 0, 6 * DS), [[2, DS], [0, 6]], 1, 0)
-    for s0, s1 in DBLK + [DLATE]:
-        iota(B("odd", 6 * s0, 6 * s1), [[0, 2], [2, s1 - s0], [0, 3]], 2 * s0 + 1, 0)
-    sel(B("BLK32"), B("ones"), [[-32, 4], [0, 32]], AL.is_ge, 0, 1)
-    sel(B("BLK32"), B("BLK32"), [[32, 4], [0, 32]], AL.is_ge, 31, -1)
-    for e in range(2):
+    HALF = [(0, 64), (64, 128)]
+
+    name[0] = "set"
+    load("s", B("rawR"), T.resid[:])
+    load("a", B("raws"), T.src0[:])
+    load("a", B("rawn"), T.nx0[:])
+    for h in range(2):
+        load("s", B("S0", 0, CUT, p=HALF[h]), T.prof[0:64, 0:CUT])
+    for x in range(2):
         for h in range(2):
-            for a in range(4):
-                k = 128 * (2 * e + h) + 32 * a
-                vcopy(B("E", k + 16 * e, k + 16 * e + 16), B("I", 32 * a + 16 * h, 32 * a + 16 * h + 16))
-    ts(B("E16"), B("E"), 16.0, None, AL.mult)
-    vcopy(B("nL"), B("rawn"))
-    swap(("nL", 0), 32)
-    swap(("W0", 0), 48)
-    vcopy(B("n0U"), B("rawn"))
-    vcopy(B("nLn"), B("psS", 32, 48))
-    vcopy(B("srcA"), B("psS", 48, 64))
-    ts(B("pj"), B("pi"), 15, None, AL.bitwise_and)
-    vcopy(B("jcol"), B("pj"))
-    ts(B("ilist"), B("ilt"), None, None, AL.add, col=B("jcol"))
-    ts(B("ZI"), B("zit"), None, None, AL.is_equal, col=B("jcol"))
+            load("a", B("obs%d" % x, p=HALF[h]), T.obs[64 * x:64 * x + 64, 128 * h:128 * h + 128])
+    load("a", B("fitb", p=(0, 8)), T.fit0[:])
+    iota(B("pi"), [[0, 1]], 0, 1)
+    iota(B("qi"), [[1, 256]], 0, 0)
+    iota(B("row", 128, 256), [[0, 2], [1, 4], [0, 16]], 0, 0)
+    iota(B("row", 0, 128), [[1, 8], [0, 16]], 0, 0)
+    for k, (sh, msk) in ((0, (0, 127)), (1, (0, 15)), (2, (4, 7)), (3, (0, 63)), (4, (4, 3)), (5, (6, 1)), (8, (0, 7)), (9, (3, 1))):
+        ts(B("ci", k, k + 1), B("pi"), sh, msk, AL.arith_shift_right, AL.bitwise_and)
+    copy(B("cf", 0, 6), B("ci", 0, 6))
+    copy(B("cf", 8, 10), B("ci", 8, 10))
+
+    def col(k):
+        return B("cf", k, k + 1)
+
+    def same(out, row, k, w=None):
+        if w is None:
+            return ts(out, row, col(k), None, AL.is_equal)
+        return ts(out, row, col(k), w, AL.is_equal, AL.mult)
+
+    copy(B("M0", 0, 16), B("raws"))
+    copy(B("M0", 16, 272), B("rawR"))
+    send(0, 0, B("M0"))
+    go = (None, "go", 0, 1, 1, True)
+    op("g", lambda e: e.sem_inc(T.sem["go"], 1), [], [go], 0.01, sem="go", then=False, after=sends[-1:])
+    for h in range(2):
+        load("s", B("S0", CUT, 4096, p=HALF[h]), T.prof[0:64, CUT:4096], [go])
+    for h in range(2):
+        load("s", B("S1", p=HALF[h]), T.prof[64:128, :], [go])
+    iota(B("row", 256, 384), [[0, 16], [1, 8]], 0, 0)
+    iota(B("odd"), [[0, 2], [2, 128]], 1, 0)
+    iota(B("row", 384, 512), [[1, 2], [2, 4], [0, 16]], 0, 0)
+    iota(B("row", 512, 640), [[0, 2], [2, 4], [0, 16]], 0, 0)
+    iota(B("KC"), [[16, 3], [1, 16], [0, 8]], 16, 0)
+    iota(B("cnt", 0, 128), [[1, 16], [0, 8]], 0, 0)
+    iota(B("cnt", 128, 256), [[-1, 16], [0, 8]], 16, 0)
+    iota(B("thrc"), [[16, 4], [0, 8]], 16, 0)
+    q128, q8 = B("qi", 0, 128), B("row", 256, 384)
+    ts(B("q16"), B("qi"), 15, None, AL.bitwise_and)
+    ts(B("q64"), q128, 63, None, AL.bitwise_and)
+    copy(B("idx", 0, 16), B("qi", 0, 16))
+    same(B("MASKR"), B("q16"), 1)
+    same(B("DUP", 0, 128), B("q64"), 3)
+    ts(col(14), col(5), 0.0, None, AL.is_equal)
+    same(B("DUP", 128, 256), B("q64"), 3, col(14))
+    same(B("DUP", 256, 384), B("q64"), 3, col(5))
+    same(B("DUPB"), B("row", 128, 256), 4)
+    same(B("I"), q128, 0)
+    ts(B("RSM"), B("q16", 0, 128), 0.0, None, AL.is_gt)
+    same(B("BLK"), B("row", 0, 128), 2)
+    ts(B("TRI"), q128, col(0), None, AL.is_ge)
+    tt(B("SWP"), B("DUP", 0, 128), B("I"), AL.subtract)
+    copy(B("nl"), B("rawn"))
+    tt(B("TRI"), B("TRI"), B("BLK"), AL.mult)
     memset(B("c4096"), 4096.0)
-    memset(B("cm127"), -127.5)
+    for x in range(2):
+        kx = HALF[x]
+        mms(B("psD", 128 * x, 128 * x + 128), [(B("I", p=kx), B("M0", 16 + 128 * x, 144 + 128 * x, p=kx)),
+                                               (B("SWP", p=kx), B("M0", 144 - 128 * x, 272 - 128 * x, p=kx))])
+        mms(B("psE", 8 * x, 8 * x + 8), [(B("I", p=kx), B("nl", 8 * x, 8 * x + 8, p=kx)), (B("SWP", p=kx), B("nl", 8 - 8 * x, 16 - 8 * x, p=kx))])
+    for x in range(2):
+        copy(B("W%d" % x, 0, 128), B("psD", 128 * x, 128 * x + 128), "a")
+        copy(B("nU%d" % x, 0, 8), B("psE", 8 * x, 8 * x + 8))
     tt(B("TMO"), B("TRI"), B("BLK"), AL.subtract)
+    ts(col(10), col(5), 256.0, None, AL.mult)
+    ts(col(6), col(4), 2.0, col(5), AL.mult, AL.add)
+    ts(B("odd"), B("odd"), col(10), None, AL.add)
+    for x in range(2):
+        for k in range(16):
+            copy(B("Xe%d" % x, k, CH, 16), B("obs%d" % x), "a")
+    for x in range(2):
+        mms(B("psX", 128 * x, 128 * x + 128), [(B("I"), B("obs%d" % x))])
+    memset(B("obsM"), 0.0)
+    for n in range(NT):
+        if SHARE[n][0] % 128:
+            copy(B("obsM", 128 * n, 128 * n + SHARE[n][0] % 128), B("obs%d" % (n % 2), 0, SHARE[n][0] % 128), "a")
+    copy(B("NBLK"), B("BLK"), "a", -1.0)
+    copy(B("NI"), B("I"), "a", -1.0)
+    copy(B("I13"), B("I"), "a", 13.0)
     tt(B("IMO"), B("I"), B("BLK"), AL.subtract)
-    ts(B("NBLK"), B("BLK"), -1.0, None, AL.mult)
-    ts(B("BIGI"), B("I"), 4194304.0, None, AL.mult)
-    memset(B("B1"), 0.0)
-    memset(B("B2"), 0.0)
-    memset(B("RS16"), 0.0)
-    memset(B("RS16", 0, 256, 16), BIG)
-    ts(B("nobs"), B("obs_s"), -1.0, None, AL.mult)
-    for k in range(48):
-        (acopy if k % 2 else vcopy)(B("Xe", k, ND * 48, 48), B("obs_s", DS, DE))
-    for gh in range(2):
-        for k in range(15 + gh):
-            put_weight(gh, k, "a" if k % 2 else "v")
-    ts(B("KC"), B("kct"), None, None, AL.add, col=B("jcol"))
-    vcopy(B("fitf"), B("fitb"))
-    vtrans(B("fitt"), B("fitf"))
-    vcopy(B("F"), B("fitt", 0, 256, 16))
-    ts(B("thr"), B("F"), 64.0, None, AL.mult)
+    memset(B("cm127"), -127.5)
+    memset(B("ones"), 1.0 / 128)
+    same(B("W128"), q8, 6, 128.0)
+    same(B("Wm64"), q8, 6, -64.0)
+    ts(col(7), col(1), 8.0, col(6), AL.mult, AL.add)
+    memset(B("BB"), 0.0)
+    same(B("SEL"), B("qi", 0, 8), 2)
+    same(B("BIGP"), q128, 7, 4194304.0)
+    same(B("BB", 8, 16), B("qi", 0, 8), 6, -1.0)
+    same(B("BB", 16, 24), B("qi", 0, 8), 6)
+    tt(B("WX", 0, 128), B("Wm64"), B("cnt", 0, 128), AL.mult)
+    tt(B("WX", 128, 256), B("Wm64"), B("cnt", 128, 256), AL.mult)
+    ts(B("WX", 256, 384), B("Wm64"), 16.0, None, AL.mult)
+    gtt(B("LxN"), B("nl"), B("idx", 0, 16), B("MASKR"), AL.mult)
+    gtt(B("LxS"), B("M0", 0, 16), B("idx", 0, 16), B("MASKR"), AL.mult)
+    copy(B("fitf", p=(0, 8)), B("fitb", p=(0, 8)))
+    same(B("I32"), q128, 0)
+    for x in range(2):
+        for h in range(2):
+            mms(B("psE", 16 + 16 * x + h, 24 + 16 * x, 2), [(B("LxN", 128 * h, 128 * h + 128), B("SEL", 4 * x, 4 * x + 4))])
+            mms(B("psE", 24 + 16 * x + h, 32 + 16 * x, 2), [(B("LxS", 128 * h, 128 * h + 128), B("SEL", 4 * x, 4 * x + 4))])
+    for h in range(2):
+        turn_over(B("psE", 48 + 8 * h, 56 + 8 * h), B("fitf", 128 * h, 128 * h + 128, p=(0, 8)), B("I32", 0, 8, p=(0, 8)))
+    for x in range(2):
+        copy(B("NX%d" % x), B("psE", 16 + 16 * x, 24 + 16 * x))
+        copy(B("SR%d" % x), B("psE", 24 + 16 * x, 32 + 16 * x))
+        for h in range(2):
+            ts(B("psK%d" % x, 384 + h, 392, 2), B("psE", 48 + 8 * h + 4 * x, 52 + 8 * h + 4 * x), 64.0, None, AL.mult)
+    memset(B("seven"), 7.0)
+    memset(B("EW"), 0.0)
+    memset(B("FLD0"), 0.0)
+    memset(B("FLD1"), 0.0)
+    copy(B("EW", 112, 128), B("MASKR", 0, 16))
+    same(B("mA8"), B("row", 256, 320), 2, 8.0)
+    same(B("mA1"), B("row", 256, 320), 2)
+    ts(B("idx", 16, 20), B("qi", 0, 8, 2), col(9), None, AL.add)
+    ts(B("idx", 20, 22), B("qi", 0, 2), 0.0, col(8), AL.mult, AL.add)
+    ts(B("ilist"), B("qi", 0, 128, 16), col(1), None, AL.add)
+    copy(B("idx", 24, 32), B("row", 384, 512, 16))
+    memset(B("DT0", 0, 128), 0.0)
+    memset(B("DT1", 0, 128), 0.0)
+    ts(col(11), col(0), 8.0, 100.0, AL.is_lt, AL.mult)
+    ts(col(12), col(11), col(8), None, AL.add)
+    ts(col(13), col(12), -1.0, None, AL.add)
+    same(B("RX", 0, 128), B("row", 512, 640), 12)
+    same(B("RX", 128, 256), B("row", 512, 640), 13)
 
-    nown, sown = ["nLn", "nL"], ["srcA", "srcB"]
-    for t in range(NR):
-        w, land, last = W[t], "land%d" % t, t == NR - 1
-        wn = None if last else W[t + 1]
-        expect(t)
+    def search(n):
+        x, t = n % 2, n // 2
+        X = str(x)
+        w, K, kx, wo, lo = "W" + X, "psK" + X, HALF[x], 512 * t, 256 * (t - 1)
+        R0, nU, Tb = B(w, 0, 128), "nU" + X, "Tb" + X
 
-        def ro(a, b):
-            return B(w, 16 + a, 16 + b)
+        def rc(z):
+            return B(w, wo + 128 * (z + 1), wo + 128 * (z + 2))
 
-        def rc(z, a, b):
-            return B(w, 16 + 256 * (z + 1) + a, 16 + 256 * (z + 1) + b)
-
-        lists = B(land, 16, PAY)
-        f0 = 2 * (DE // 32)
-        f1 = f0 + 2 * ((DE + 15) // 32 - DE // 32 + 1)
-        rest = [(0, f0), (f1, 16)]
-
-        def nx(c0, c1):
-            return B("n0U", c0, c1)
-        vcopy(B("srcU"), B(land, 0, 16))
-        agather(B("LQ1", 0, 128), lists, B("srcU", 0, 8))
-        vgather(B("LQ1", 128, 256), lists, B("srcU", 8, 16))
-        vgather(rc(0, 16 * f0, 16 * f1), lists, nx(f0, f1))
-        agather(B("LQ2", 0, 128), B("LQ1"), B("srcU", 0, 8))
-        vgather(B("LQ2", 128, 256), B("LQ1"), B("srcU", 8, 16))
-        vgather(rc(1, 16 * f0, 16 * f1), B("LQ1"), nx(f0, f1))
-        vgather(rc(2, 16 * f0, 16 * f1), B("LQ2"), nx(f0, f1))
-        for c0, c1 in rest:
-            agather(rc(1, 16 * c0, 16 * c1), B("LQ1"), nx(c0, c1))
-            agather(rc(2, 16 * c0, 16 * c1), B("LQ2"), nx(c0, c1))
-        def prefix(ci):
-            ch = CHUNKS[ci]
-            c0 = ch[0][1]
-            P = "psP%d" % (ci % 2)
-            for kind, s0, s1 in ch:
-                n = s1 - s0
-                for z in range(3):
-                    b = 6 * (s0 - c0)
-                    if kind == "A":
-                        og, oh = B(P, b + 2 * z, b + 6 * n, 6), B(P, b + 2 * z + 1, b + 6 * n, 6)
-                    else:
-                        og, oh = B(P, b + z, b + 3 * n, 3), B(P, b + 3 * n + z, b + 6 * n, 3)
-                    mm(og, B("I"), B("c4096", 0, n), True, False)
-                    mm(og, B("TRI"), rc(z, s0, s1), False, True)
-                    mm(oh, B("I"), B("c4096", 0, n), True, False)
-                    mm(oh, B("BLK"), ro(s0, s1), False, False)
-                    mm(oh, B("TMO"), rc(z, s0, s1), False, True)
-
-        def times(ci):
-            c0, c1 = CHUNKS[ci][0][1], CHUNKS[ci][-1][2]
-            n = 6 * (c1 - c0)
-            tt(B("v1" + "ab"[ci % 2], 0, n), B("psP%d" % (ci % 2), 0, n), B("odd", 6 * c0, 6 * c1), AL.mult)
-
-        def floor(ci):
-            n = 6 * (CHUNKS[ci][-1][2] - CHUNKS[ci][0][1])
-            ts(B("v2" + "ab"[ci % 2], 0, n), B("v1" + "ab"[ci % 2], 0, n), 2, 4095, AL.arith_shift_right, AL.bitwise_and)
-
-        def place(ci):
-            c0, c1 = CHUNKS[ci][0][1], CHUNKS[ci][-1][2]
-            vcopy(B("off", 6 * c0, 6 * c1), B("v2" + "ab"[ci % 2], 0, 6 * (c1 - c0)))
-
-        def allowed(P, c0, c1):
-            for z in range(3):
-                o = B(P, z, 3 * (c1 - c0), 3)
-                mm(o, B("I"), B("cm127", 0, c1 - c0), True, False)
-                mm(o, B("BLK"), ro(c0, c1), False, False)
-                mm(o, B("IMO"), rc(z, c0, c1), False, True)
-            ts(B("pen", 3 * c0, 3 * c1), B(P, 0, 3 * (c1 - c0)), MAGIC, MAGIC, AL.add, AL.not_equal)
-
-        prefix(0)
-        a, b = rest[0]
-        vgather(rc(0, 16 * a, 16 * b), lists, nx(a, b))
-        times(0)
-        floor(0)
-        place(0)
-        a, b = rest[1]
-        vgather(rc(0, 16 * a, 16 * b), lists, nx(a, b))
-        for c in (1, 3):
-            prefix(c)
-            prefix(c + 1)
-            times(c)
-            times(c + 1)
-            floor(c)
-            floor(c + 1)
-            place(c)
-            place(c + 1)
-        prefix(5)
-        times(5)
-        allowed("psQ", DE, V)
-        floor(5)
-        allowed("psP0", 32, DE)
-        place(5)
-        allowed("psP1", 0, 32)
-        swap((land, 0), 32)
-        n0, srcl = B(nown[0]), B(sown[0])
-        tt(B("PQ", 0, 16), n0, srcl, AL.subtract)
-
-        def absd(s0, s1):
-            for s in range(s0, s1):
-                p = 96 * apos(s)
-                o, of, bi = B("A", p, p + 96), B("off", 6 * s, 6 * s + 6), B("nobs", s, s + 1)
-                op("a", lambda e: e.activation(o[0], ind(B("S"), of), AF.Abs, bias=bi[0]), [B("S"), of, bi], [o])
-
-        def gat(blk):
-            s0, s1 = blk
-            n, base = 48 * (s1 - s0), 96 * (s0 - DS)
-            for gh in range(2):
-                lo = base + gh * n
-                c = 6 * s0 + gh * 3 * (s1 - s0)
-                of, x, o = B("off", c, c + 3 * (s1 - s0)), B("Xe", 48 * (s0 - DS), 48 * (s1 - DS)), B("dd", lo, lo + n)
-                op("v", lambda e: e.tensor_tensor(o[0], ind(B("S"), of), x[0], AL.subtract), [B("S"), of, x], [o])
-            for gh in range(2):
-                lo = base + gh * n
-                ts(B("rr", lo, lo + n), B("dd", lo, lo + n), 0.0, -2.0, AL.min, AL.mult)
-
-        def sums(kind, blk):
-            s0, s1 = blk
-            kb = [x for x in KEYBANK if x[0] <= s0 and s1 <= x[1]][0]
-            o, n = B(kb[2], 3 * (s0 - kb[0]), 3 * (s1 - kb[0])), 3 * (s1 - s0)
-            mm(o, B("I"), B("KC", 0, n), True, False)
-            mm(o, B("BIGI"), B("pen", 3 * s0, 3 * s1), False, False)
-            todo = []
-            for gh in range(2):
-                for buf in ("A",) if kind == "A" else ("dd", "rr"):
-                    for k in range(15 + gh):
-                        if kind == "A":
-                            p = 96 * apos(s0)
-                            todo.append((weight(gh, k), B(buf, p + 16 * gh + k, p + 32 * n, 32)))
-                        else:
-                            lo = 96 * (s0 - DS) + gh * 16 * n
-                            todo.append((weight(gh, k), B(buf, lo + k, lo + 16 * n, 16)))
-            for i, (wt, r) in enumerate(todo):
-                mm(o, wt, r, False, i == len(todo) - 1)
-
-        def best1(lo, hi, ps):
-            scan(B("z1", 3 * lo, 3 * hi), B("RS3", 0, 3 * (hi - lo)), B(ps, 0, 3 * (hi - lo)))
-
-        def turn(lo, hi):
-            vtrans(B("tr", lo, hi), B("z1", 3 * lo + 2, 3 * hi, 3))
-
-        def best2(lo, hi):
-            scan(B("s2", lo, hi), B("RS16", 0, hi - lo), B("tr", lo, hi))
-
-        def accept(lo, hi):
-            a, b = lo // 16, hi // 16
-            bi, ac = B("s2", lo + 15, hi, 16), B("IND", a, b)
-            ts(B("st", a, b), bi, 15, None, AL.bitwise_and)
-            ts(B("z16", a, b), bi, 48, None, AL.bitwise_and)
-            tt(ac, bi, B("thr", a, b), AL.is_lt)
-            vcopy(B("SWa", 16 + a, 16 + b), B("st", a, b))
-            tt(B("SWa", a, b), B("z16", a, b), ac, AL.mult)
-            swap(("SWa", 16), 16, None, "E", a, b)
-            swap(("SWa", 0), 0, "ilist", "E16", a, b)
-
-        def offsets(lo, hi):
-            a, b = lo // 16, hi // 16
-            vcopy(B("offB", a, b), B("psS", a, b))
-            vcopy(B("offB", 16 + a, 16 + b), B("psS", 16 + a, 16 + b))
-
-        def readlist(lo, hi):
-            agather(B("Rb", lo, hi), B(w, 16, 1040), B("offB", lo // 16, hi // 16))
-
-        def newlist(lo, hi, ps):
-            mm(B(ps, 0, hi - lo), B("BLK"), ro(lo, hi), True, False)
-            mm(B(ps, 0, hi - lo), B("NBLK"), B("Rb", lo, hi), False, True)
-            mm(B(ps, 256, 256 + hi - lo), B("I"), B("Rb", lo, hi), True, True)
-
-        def site(lo, hi, ps):
-            tt(B("md", lo, hi), B(ps, 0, hi - lo), B("OH", lo, hi), AL.mult)
-
-        def putlist(lo, hi, ps):
-            out = B("Rf", lo, hi) if last else B(wn, 16 + lo, 16 + hi)
-            tt(out, B(ps, 256, 256 + hi - lo), B("md", lo, hi), AL.add)
-            if last:
-                store("s", T.yr[:, lo:hi], out, "st%d" % (3 if lo else 0))
-
-        for s0, s1 in ABLK + [ALATE]:
-            absd(s0, s1)
-        for blk in DBLK:
-            gat(blk)
-        for nm in ORDER:
-            sums(nm[0], (ABLK if nm[0] == "A" else DBLK)[int(nm[1])])
-        vcopy(B("B1", 0, 256, 16), B("psS", 32, 48))
-        vtrans(B("X"), B("B1"))
-        gat(DLATE)
-        sums("D", DLATE)
-        sums("A", ALATE)
-        best1(32, DE, "psKC")
-        best1(DE, V, "psKA")
-        turn(32, V)
-        best2(32, V)
-        accept(32, V)
-        agather(B("nX", 0, 256), B("X"), B("n0U"))
-        agather(B("X2"), B("X"), B("srcU"))
-        agather(B("nX", 256, 512), B("X2"), B("n0U"))
-        vtrans(B("T12", 0, 256), B("nX", 0, 256))
-        best1(0, 32, "psKB")
-        n1, n2 = B("T12", 0, 256, 16), B("T12", 256, 512, 16)
-        acc = B("IND", 0, 16)
-        tt(B("PQ", 16, 32), n1, n0, AL.subtract)
-        turn(0, 32)
-        offsets(32, V)
-        best2(0, 32)
-        readlist(32, V)
-        agather(B("OH", 32, V), B("ZI"), B("offB", 18, 32))
-        accept(0, 32)
-        newlist(32, V, "psD")
-        vtrans(B("T12", 256, 512), B("nX", 256, 512))
-        ts(B("IND", 16, 32), B("SWa", 0, 16), 32.0, None, AL.is_ge)
-        ts(B("IND", 32, 48), B("SWa", 0, 16), 48.0, None, AL.is_ge)
-        tt(B("PQ", 32, 48), n2, n1, AL.subtract)
-        offsets(0, 32)
-        readlist(0, 32)
-        agather(B("OH", 0, 32), B("ZI"), B("offB", 16, 18))
-        newlist(0, 32, "psP1")
-        tt(B("TP"), B("IND"), B("PQ"), AL.mult)
-        if last:
-            tt(B("b1"), B("TP", 0, 16), B("TP", 16, 32), AL.add)
-        site(32, V, "psD")
-        if not last:
-            for h in range(2):
-                o = B("psP0", h, 16, 2)
-                mm(o, B("I"), B(w, h, 16, 2), True, False)
-                for f in range(3):
-                    for e in range(2):
-                        k = 128 * (2 * e + h)
-                        mm(o, B("E", k, k + 128), B("TP", 16 * f + e, 16 * f + 16, 2), False, f == 2 and e == 1)
-        if not last:
-            site(0, 32, "psP1")
-            putlist(32, V, "psD")
-            vcopy(B(wn, 0, 16), B("psP0", 0, 16))
-            putlist(0, 32, "psP1")
-            send(t + 1, pieces(t + 1)[0])
-            tt(B("b1"), B("TP", 0, 16), B("TP", 16, 32), AL.add)
-        tt(B("bn"), B("TP", 32, 48), B("b1"), AL.add)
-        ts(B("sc"), B("s2", 15, 256, 16), 6, None, AL.logical_shift_right)
-        if last:
-            site(0, 32, "psP1")
-        tt(B(sown[1]), B("bn"), srcl, AL.add)
-        if last:
-            putlist(32, V, "psD")
-        tt(B("d5"), B("sc"), B("F"), AL.subtract)
-        ts(B("h1"), B(sown[1]), 13.0, None, AL.mult)
-        if last:
-            putlist(0, 32, "psP1")
-        tt(B("d6"), B("d5"), acc, AL.mult)
-        tt(B("h2"), B("h1"), B("sc"), AL.add)
-        ts(B("h3"), B("h2"), 255, None, AL.bitwise_and)
-        tt(B("d3"), B("h3"), n2, AL.subtract)
-        if not last:
-            tt(B("F"), B("d6"), B("F"), AL.add)
-            tt(B("d4"), B("d3"), acc, AL.mult)
-            tt(B(nown[1]), B("d4"), n2, AL.add)
-            swap((nown[1], 0), 48)
-            vcopy(B("acc%d" % t, 0, 16), acc)
-            vcopy(B("acc%d" % t, 16, 32), acc)
-            vcopy(B("n0U"), B("psS", 48, 64))
-            k = 0
-            for r in range(t + 1):
-                for s in range(8):
-                    mm(B("psS", 64, 80), B("BLK32"), B("acc%d" % r, 2 * s, 2 * s + 16), k == 0, k == 8 * (t + 1) - 1)
-                    k += 1
-            vcopy(B("Ai"), B("psS", 64, 80))
-            ts(B("A7"), B("Ai"), 7, None, AL.bitwise_and)
-            tt(B("thr"), B("F"), B("A7"), AL.subtract)
-            ts(B("thr"), B("thr"), 64.0, None, AL.mult)
-            nown, sown = nown[::-1], sown[::-1]
+        name[0] = "src%d" % n
+        if t == 0:
+            if x == 0:
+                gtt(B("Lx"), B("land", 0, 16), B("idx", 0, 16), B("MASKR"), AL.mult)
+            mms(B("psQ", 0, 256), [(B("DUPB", p=kx), B("Lx", p=kx))])
         else:
-            tt(B("B2", 0, 256, 16), B("d6"), B("F"), AL.add)
-            tt(B("d4"), B("d3"), acc, AL.mult)
-            tt(B("B2", 1, 256, 16), B("d4"), n2, AL.add)
-            vtrans(B("oT"), B("B2"))
-            op("s", lambda e: e.dma_start(T.yf[:], T.oT[0:128:16, :]), [B("oT")], [], sem="st1", inc=16)
-            op("a", lambda e: e.dma_start(T.yn[:], T.oT[1:128:16, :]), [B("oT")], [], sem="st2", inc=16)
+            for h in range(2):
+                mms(B("psQ", 128 * h, 128 * h + 128), [(B("RX", 128 * h, 128 * h + 128), B("ld" + X, lo, lo + 128))])
+        copy(B(Tb, 256, 512), B("psQ", 0, 256), ON["src"])
+        name[0] = "ch%d" % n
+        for z in (1, 2):
+            buf = B("nXa" if z == 1 else "nXb")
+            gtt(buf, B(Tb, 256, 512), B(nU, 8 * z - 8, 8 * z), B("MASKR", 0, 128), AL.mult)
+            running_sum(B("s1"), B("RSM"), buf)
+            copy(B(nU, 8 * z, 8 * z + 8), B("s1", 15, 128, 16))
+        name[0] = "pq%d" % n
+        mm(B(K, 392, 424), B("nXa"), B("BB"), True, False)
+        mm(B(K, 408, 424), B("nXb"), B("BB", 8, 24), False, False, True)
+        mm(B(K, 392, 400), B("I"), B("SR" + X), False, False, True)
+        mm(B(K, 392, 400), B("NI"), B("NX" + X), False, False, True)
+        mm(B(K, 400, 408), B("I"), B("NX" + X), False, True, True)
+        name[0] = "lt%d" % n
+        if t == 0:
+            mms(B("psP1", 256, 512), [(B("DUP", 128 * x + 128, 128 * x + 256), B("land", 16, 272))])
+        else:
+            for h in range(2):
+                mms(B("psP1", 128 * h + 256, 128 * h + 384), [(B("DUP", 128 * h + 128, 128 * h + 256), B("ld" + X, lo + 128, lo + 256))])
+        copy(B(Tb, 0, 256), B("psP1", 256, 512), ON["table"])
+        for z in range(3):
+            name[0] = "l%d" % n
+            gather(rc(z), B(Tb, 0, 256), B(nU, 8 * z, 8 * z + 8), ON["lists"][z])
+            name[0] = "col%d" % n
+            P, c = ["psP0", "psP1", "psP0"][z], 256 * z
+            mm(B(P, 0, 256), B("I"), B("c4096"), True, False)
+            mm(B(P, 128, 256), B("BLK"), R0, False, False, True)
+            mm(B(P, 0, 128), B("TRI"), rc(z), False, False)
+            mm(B(P, 128, 256), B("TMO"), rc(z), False, True, True)
+            for a, b in [(0, 64), (64, 256)] if z == 0 else [(0, 256)]:
+                tt(B("v1", c + a, c + b), B(P, a, b), B("odd", a, b), AL.mult)
+                ts(B("v2", c + a, c + b), B("v1", c + a, c + b), 2, 4095, AL.arith_shift_right, AL.bitwise_and)
+                placed[n, z] = copy(B("off" + X, c + a, c + b), B("v2", c + a, c + b))
+        name[0] = "pen%d" % n
+        for z in range(3):
+            mms(B("psQ", 128 * z, 128 * z + 128), [(B("I"), B("cm127")), (B("BLK"), R0), (B("IMO"), rc(z))])
+        ts(B("pen" + X), B("psQ", 0, 384), MAGIC, MAGIC, AL.add, AL.not_equal)
+        for z in range(3):
+            mms(B("psQ", 128 * z, 128 * z + 128), [(B("BLK"), R0), (B("NBLK"), rc(z))])
+        copy(B("DT" + X, 128, 512), B("psQ", 0, 384), ON["own"])
+
+        hc = helper(core, T.cores, topo)
+        rid, pid = topo.addr(hc, core)
+
+        def fold(u, s, xe, c0, c1):
+            sem, es = "fb%d%d" % (x, u), lane(core, hc, u, topo)
+            tr = RemoteDMATransfer(dst_ids=[DstId(rid=rid, pnc=pid)], dma_engine_mask=sum(1 << k for k in es), remote_sem=T.sem["fa%d%d" % (x, u)],
+                                   srcs=[s[0], xe[0]], dsts=[T[held(n)][:, c0:c1]], alu_op=2)
+            folded.append(op("g", lambda e: e.remote_dma_fused([tr], local_sem=T.sem[sem]), [s, xe], [B("Mx" + X, c0, c1)], PLAN["issue"],
+                             sem=sem, inc=len(es) + len(topo.engines(hc, core)), then=False, bytes=256 * (c1 - c0),
+                             lane=len(es) / len(topo.engines(core, hc)),
+                             lat=PLAN["landed"], back=True, after=folded[-1:]))
+        def due(s):
+            k = SHARE[n][0]
+            return n + s / k if s < k else n + PLAN["from"] + (PLAN["to"] - PLAN["from"]) * (s - k) / (768 - k)
+        u, later = 0, []
+        for e, ch, a, b, f in pieces(*SHARE[n]):
+            name[0] = "g%d.%d" % (n, ch)
+            c0, c1 = CH * ch + 16 * a, CH * ch + 16 * b
+            s, of, xe = B("Sg" + X, c0, c1), B("off" + X, 128 * ch + a, 128 * ch + b), B("Xe" + X, 16 * a, 16 * b)
+            if e == "a":
+                i = gather(s, B("S" + X), of, e)
+                steps[i]["due"] = due(128 * ch + a)
+                steps[i]["after"] = scalar_last[-1:]
+                scalar_last.append(i)
+                if f:
+                    if u < PLAN["before"]:
+                        fold(u, s, xe, c0, c1)
+                    else:
+                        later.append((u, s, xe, c0, c1))
+                    u += 1
+                else:
+                    for k in range(15 + ch % 2):
+                        i = tt(B("Mx" + X, c0 + k, c1, 16), B("Sg" + X, c0 + k, c1, 16), B("psX", 128 * x + a, 128 * x + b), AL.max)
+                        steps[i]["due"] = due(128 * ch + a) + PLAN["soon"]
+            else:
+                steps[gtt(s, B("S" + X), of, xe, AL.subtract)]["due"] = due(128 * ch + a)
+                steps[ts(B("Mx" + X, c0, c1), s, 0.0, None, AL.max)]["due"] = due(128 * ch + a) + 0.07
+
+        if n:
+            decide(n - 1)
+        name[0] = "f%d" % n
+        for args in later:
+            fold(*args)
+            steps[-1]["after"] = steps[-1]["after"] + sends[-1:]
+        name[0] = "key%d" % n
+        left = [0]
+        mm(B(K, 0, 384), B("ones"), B("KC"), True, left)
+        for z in range(3):
+            e = [min(128, max(0, SHARE[n][0] - 128 * (2 * z + gh))) for gh in range(2)]
+            for k, m in [(2, 128)] if e == [128, 128] else [(gh, e[gh]) for gh in range(2) if e[gh]]:
+                xs = B("obs" + X) if m == 128 else B("obsM", 128 * n, 128 * n + 128)
+                mm(B(K, 128 * z, 128 * z + 128), xs, B("WX", 128 * k, 128 * k + 128), False, left, loose=True)
+            mm(B(K, 128 * z, 128 * z + 128), B("pen" + X, 128 * z, 128 * z + 128), B("BIGP"), False, left, loose=True)
+        for ch in range(6):
+            name[0] = "s%d.%d" % (n, ch)
+            z, gh = ch // 2, ch % 2
+            for buf, wt in (("Sg", "Wm64"), ("Mx", "W128")):
+                for k in range(15 + gh):
+                    a, b = (8 * k + 8, 128) if gh == 0 else (0, 8 * k + 8)
+                    more = {"join": True} if k % 4 else {"loose": True}
+                    mm(B(K, 128 * z + a, 128 * z + b), B(buf + X, CH * ch + k, CH * ch + CH, 16), B(wt, a, b), False, left, **more)
+
+    def decide(n):
+        x, t = n % 2, n // 2
+        X, last = str(x), t == NR - 1
+        w, K, wo = "W" + X, "psK" + X, 512 * t
+        R0 = B(w, 0, 128)
+        IND, nacc = B("IND" + X, 32 * t, 32 * t + 32), B("IND" + X, 32 * t, 32 * t + 8)
+
+        def to_list(out, src, first):
+            mms(out, first + [(B("EW", 112 - 16 * (4 * (c % 2) + c // 2), 240 - 16 * (4 * (c % 2) + c // 2)), B(src, 8 * c, 8 * c + 8))
+                              for c in range(8)])
+        name[0] = "d%d" % n
+        for c in range(8):
+            i = least(B("best", c, c + 1), B(K, c, 392, 8))
+            if n + 1 < NT and PLAN["first_z"] >= 0:
+                steps[i]["after"] = [placed[n + 1, PLAN["first_z"]]]
+        ts(B("bi", 8, 16), B("best"), 48, None, AL.bitwise_and)
+        ts(B("bi", 0, 8), B("best"), 15, None, AL.bitwise_and)
+        gtt(B("Lz"), B("bi", 8, 16), B("idx", 16, 20), B("mA8"), AL.mult)
+        gtt(IND, B("bi", 8, 16), B("idx", 20, 22), B("thrc"), AL.is_lt)
+        gtt(B("site"), B("bi", 0, 8), B("idx", 24, 32), B("q16", 0, 128), AL.is_equal)
+        to_list(B("psD", 0, 8), "Lz", [(B("I"), B("ilist"))])
+        mms(B("psE", 0, 128), [(B("site"), B("I"))])
+        tt(B("FLD" + X, 8, 40), IND, B(K, 392, 424), AL.mult)
+        copy(B("offW"), B("psD", 0, 8))
+        copy(B("mask"), B("psE", 0, 128))
+        mms(B(K, 0, 128), [(B("FLD" + X), B("I"))])
+        gather(B("Rb"), B(w, wo, wo + 512), B("offW"), ON["chosen"])
+        copy(B("T1s" + X), B(K, 0, 128))
+        gtt(B("md"), B("DT" + X), B("offW"), B("mask"), AL.mult)
+        if last:
+            tt(B("Rf" + X), B("Rb"), B("md"), AL.add)
+            for h in range(2):
+                store("sa"[h] if n == NT - 1 else "s", T.yr[64 * x:64 * x + 64, 128 * h:128 * h + 128], B("Rf" + X, p=HALF[h]))
+        else:
+            send(n + 1, 0, B("T1s" + X))
+            send(n + 1, 1, B("Rb"), B("md"))
+            mms(B("psE", 128, 256), [(B("I"), B("Rb")), (B("I"), B("md"))])
+            copy(B(w, wo + 512, wo + 640), B("psE", 128, 256), ON["own"])
+        name[0] = "e%d" % n
+        ts(B("sc"), B("best"), 6, None, AL.arith_shift_right)
+        mms(B("psD", 128, 136), [(B("I"), B("FLD" + X, 8 + 8 * f, 16 + 8 * f)) for f in range(4)])
+        copy(B("SR" + X), B("psD", 128, 136))
+        mms(B("psD", 136, 144), [(B("I13"), B("SR" + X))])
+        tt(B("h2"), B("psD", 136, 144), B("sc"), AL.add)
+        ts(B("h3"), B("h2"), 255, None, AL.bitwise_and)
+        F = B("OF" + X, 0, 8) if last else B("Fn") if t else B("sc")
+        if t:
+            tt(B("u"), nacc, B("A7" + X), AL.mult)
+            tt(F, B("sc"), B("u"), AL.add)
+        tt(B("d3"), B("h3"), B(K, 416, 424), AL.subtract)
+        tt(B("d4"), B("d3"), nacc, AL.mult)
+        tt(B("OF" + X, 8, 16) if last else B("NX" + X), B("h3"), B("d4"), AL.subtract)
+        if last:
+            turn_over(B("psD", 256, 384, p=(0, 16)), B("OF" + X), B("I32"))
+            copy(B("oT" + X, p=(0, 16)), B("psD", 256, 384, p=(0, 16)))
+            store("s", T.yf[4 * x:4 * x + 4, :], B("oT" + X, p=(0, 8)))
+            store("sa"[x], T.yn[4 * x:4 * x + 4, :], B("oT" + X, p=(8, 16)))
+        else:
+            for h in range(2):
+                mms(B("psE", 256 + h, 264, 2), [(B("seven"), B("IND" + X, 32 * r + k, 32 * r + 8, 2)) for r in range(t + 1) for k in range(2)])
+            copy(B("Ai"), B("psE", 256, 264))
+            ts(B("A7" + X), B("Ai"), 7, None, AL.bitwise_and)
+            tt(B("Tn"), F, B("A7" + X), AL.subtract)
+            ts(B(K, 384, 392), B("Tn"), 64.0, None, AL.mult)
+            gtt(B("Ln"), B("NX" + X), B("idx", 16, 20), B("mA1"), AL.mult)
+            to_list(B("psD", 256, 264), "Ln", [])
+            copy(B("nU" + X, 0, 8), B("psD", 256, 264))
+
+    for n in range(NT):
+        search(n)
+    decide(NT - 1)
+    if "order" not in ORDER:
+        ORDER["order"], ORDER["end"] = arrange(steps)
+    for i in ORDER["order"]:
+        TAGGER[0][0] = steps[i]["name"]
+        for call in steps[i]["calls"]:
+            issue(*call)
     for s in sorted(total):
         if known["g"].get(s, 0) < total[s]:
             g.wait_ge(T.sem[s], total[s])
+
+
+TAGGER = [[""]]
+ON = {"table": "a", "lists": "vaa", "chosen": "v", "own": "a", "src": "v"}

@@ -9,23 +9,40 @@ NT = 2 * NR
 CUT = 1024
 MAGIC = 1.5 * 2.0 ** 31
 CH = 2048
+ROWS = [12, 16, 16, 16, 16, 16]
+ALL = 128 * sum(ROWS)
+DENSE = [(0, 0, 0, 12), (1, 0, 12, 16), (1, 1, -4, 8), (2, 1, 8, 16), (2, 2, -8, 4), (3, 2, 4, 16)]
+
+
+def place_of(ch, s):
+    return 128 * sum(ROWS[:ch]) + ROWS[ch] * s
+
+
+def terms(ch):
+    z = ch // 2
+    out = [(k, z, k + 1, 16) if ch % 2 == 0 else (k, z, 0, k + 1) for k in range(min(15, ROWS[ch]))]
+    if ch == 1:
+        out += [(15, y, 0, 16) for y in range(3)]
+    if ch in (2, 3, 4):
+        out.append((15, 0, 11 + ch, 16))
+    return out
 
 
 def pieces(on_scalar, folded, cut=32):
     out, s = [], 0
     while s < 768:
-        e = min(s + (64 if s < on_scalar else cut), s // 128 * 128 + 128)
+        e = min(s + (96 if s + 96 == on_scalar else 64 if s < on_scalar else cut), s // 128 * 128 + 128)
         e = min([e] + [x for x in (on_scalar, folded) if x > s])
         out.append(("a" if s < on_scalar else "v", s // 128, s % 128, s % 128 + e - s, s < folded))
         s = e
     return out
 
 
-SHARE = [(576, 320)] * (NT - 1) + [(576, 256)]
+SHARE = [(576, 384)] + [(608, 448)] * (NT - 2) + [(576, 320)]
 NU = 12
-PLAN = {"cycle": 0.00087, "pe": 0.00044, "gather": 1.5, "wake": 0.17, "issue": 0.5, "first": 1.0, "load": 1.4, "rate": 150e3,
-        "fold": 2.1, "landed": 0.7, "message": 3.8, "passes": 400, "leash": 2.0, "move": 0.3, "lift": 1.0,
-        "turn": 13, "tail": 0.4, "from": 0.1, "to": 1.1, "soon": 0.15, "first_z": 2, "before": 9}
+PLAN = {"cycle": 0.00087, "pe": 0.00044, "gather": 1.6, "wake": 0.17, "issue": 0.5, "first": 1.0, "load": 1.4, "rate": 250e3,
+        "fold": 2.1, "landed": 0.7, "message": 4.5, "passes": 300, "leash": 2.0, "move": 0.3, "lift": 1.0,
+        "turn": 13, "tail": 0.4, "from": 0.1, "to": 1.1, "soon": 0.15, "first_z": -1, "before": 9}
 
 
 def sb(cols, kind="bfloat16"):
@@ -39,20 +56,20 @@ SCRATCH = {
     "best": sb(8, "int32"), "bi": sb(16, "int32"), "sc": sb(8, "int32"), "Lz": sb(64), "Ln": sb(64), "offW": sb(8, "uint16"),
     "Rb": sb(128), "mask": sb(128), "md": sb(128), "h2": sb(8, "int32"), "h3": sb(8, "int32"), "d3": sb(8, "float32"), "d4": sb(8, "float32"),
     "Ai": sb(8, "int32"), "u": sb(8, "float32"), "Fn": sb(8, "float32"), "Tn": sb(8, "float32"),
-    "qi": sb(256, "int32"), "pi": sb(1, "int32"), "ci": sb(16, "int32"), "cf": sb(16, "float32"), "row": sb(640, "int32"),
+    "qi": sb(256, "int32"), "pi": sb(1, "int32"), "ci": sb(16, "int32"), "cf": sb(24, "float32"), "row": sb(640, "int32"),
     "ones": sb(128), "seven": sb(128), "I": sb(128), "NI": sb(128), "I13": sb(128), "I32": sb(128, "float32"), "BLK": sb(128), "NBLK": sb(128),
-    "TRI": sb(128), "TMO": sb(128), "IMO": sb(128), "DUP": sb(384), "SWP": sb(128), "DUPB": sb(128), "MASKR": sb(256), "RSM": sb(128),
+    "TRI": sb(128), "PF": sb(12 * 128), "IMO": sb(128), "DUP": sb(384), "SWP": sb(128), "DUPB": sb(128), "MASKR": sb(256), "RSM": sb(128),
     "W128": sb(128), "Wm64": sb(128), "BIGP": sb(128), "WX": sb(384), "cnt": sb(256), "KC": sb(384), "BB": sb(32), "EW": sb(240),
     "mA8": sb(64), "mA1": sb(64), "idx": sb(32, "uint16"), "thrc": sb(32), "RX": sb(256), "site": sb(128), "SEL": sb(8), "ilist": sb(8),
-    "odd": sb(256, "float32"), "c4096": sb(256), "cm127": sb(128), "obsM": sb(768),
+    "odd": sb(352, "float32"), "c4096": sb(256), "cm127": sb(128), "obsM": sb(1024),
     "psK0": ("psum", [128, 512], "float32"), "psK1": ("psum", [128, 512], "float32"), "psP0": ("psum", [128, 512], "float32"),
     "psP1": ("psum", [128, 512], "float32"), "psQ": ("psum", [128, 512], "float32"), "psX": ("psum", [128, 512], "float32"),
     "psD": ("psum", [128, 512], "float32"), "psE": ("psum", [128, 512], "float32"),
 }
 for x in range(2):
     SCRATCH.update({n + str(x): v for n, v in {
-        "S": sb(4096), "obs": sb(128), "Xe": sb(CH), "W": sb(NR * 512), "ld": sb(512), "Tb": sb(512), "nU": sb(24, "uint16"),
-        "off": sb(768, "uint16"), "pen": sb(384), "Sg": sb(6 * CH), "Mx": sb(6 * CH), "Fh": sb(6 * CH), "FLD": sb(128), "DT": sb(512), "T1s": sb(128),
+        "S": sb(4096), "obs": sb(128), "Xe": sb(CH + 128 * ROWS[0]), "W": sb(NR * 512), "ld": sb(512), "Tb": sb(512), "nU": sb(24, "uint16"),
+        "off": sb(ALL // 16, "uint16"), "pen": sb(384), "Sg": sb(ALL), "Mx": sb(ALL), "Fh": sb(ALL), "FLD": sb(128), "DT": sb(512), "T1s": sb(128),
         "NX": sb(8), "SR": sb(8), "IND": sb(NR * 32), "A7": sb(8, "int32"), "Rf": sb(128, "float32"), "OF": sb(16, "float32"),
         "oT": sb(128, "float32")}.items()})
 SEMAPHORES = (["qv", "qa", "qp", "qg", "go", "hb"] + ["ld%d" % i for i in range(15)] + ["st%d" % i for i in range(8)]
@@ -111,7 +128,7 @@ def other_program(g, core, T, topo):
                 for u, (ch, a, b) in enumerate(folds(n)):
                     s = "%d%d" % (n % 2, u)
                     seen[s] = seen.get(s, 0) + len(lane(c, core, u, topo))
-                    lo, hi = CH * ch + 16 * a, CH * ch + 16 * b
+                    lo, hi = place_of(ch, a), place_of(ch, b)
                     g.wait_ge(T.sem["fa" + s], seen[s])
                     g.remote_dma(out_ap=T["Mx%d" % (n % 2)][:, lo:hi], in_ap=T[held(n)][:, lo:hi], remote_sem=T.sem["fb" + s],
                                  local_sem=T.sem["hb"], pid=pid, routing_id=rid, dma_engine_mask=topo.mask(core, c))
@@ -399,6 +416,9 @@ def rank_program(g, core, T, topo):
             return op("g", lambda e: e.iota(out[0], pattern, base, cm), [], [out], c)
         return op("g", lambda e: e.iota(out[0], pattern, base, cm, allow_small_or_imprecise_dtypes=True), [], [out], c)
 
+    def select(out, a, pattern, base, cm):
+        return op("g", lambda e: e.affine_select(out[0], a[0], pattern, AL.is_ge, 0.0, base, cm), [a], [out], (200 + 2 * cols(out)) * cyc)
+
     sends, folded, scalar_last, placed = [], [], [], {}
 
     def send(m, p, *src):
@@ -464,12 +484,13 @@ def rank_program(g, core, T, topo):
     for h in range(2):
         load("s", B("S1", p=HALF[h]), T.prof[64:128, :], [go])
     iota(B("row", 256, 384), [[0, 16], [1, 8]], 0, 0)
-    iota(B("odd"), [[0, 2], [2, 128]], 1, 0)
+    iota(B("odd", 0, 96), [[8, 32], [2, 3]], 1, 0)
+    iota(B("odd", 96, 352), [[0, 2], [2, 128]], 1, 0)
     iota(B("row", 384, 512), [[1, 2], [2, 4], [0, 16]], 0, 0)
     iota(B("row", 512, 640), [[0, 2], [2, 4], [0, 16]], 0, 0)
     iota(B("KC"), [[16, 3], [1, 16], [0, 8]], 16, 0)
     iota(B("cnt", 0, 128), [[1, 16], [0, 8]], 0, 0)
-    iota(B("cnt", 128, 256), [[-1, 16], [0, 8]], 16, 0)
+    iota(B("cnt", 128, 256), [[-1, 16], [0, 8]], 15, 0)
     iota(B("thrc"), [[16, 4], [0, 8]], 16, 0)
     q128, q8 = B("qi", 0, 128), B("row", 256, 384)
     ts(B("q16"), B("qi"), 15, None, AL.bitwise_and)
@@ -497,19 +518,36 @@ def rank_program(g, core, T, topo):
     for x in range(2):
         copy(B("W%d" % x, 0, 128), B("psD", 128 * x, 128 * x + 128), "a")
         copy(B("nU%d" % x, 0, 8), B("psE", 8 * x, 8 * x + 8))
-    tt(B("TMO"), B("TRI"), B("BLK"), AL.subtract)
+    def pf(k):
+        return B("PF", 128 * k, 128 * k + 128)
+    tt(pf(0), B("TRI"), B("BLK"), AL.subtract)
+    for k, (v, c, shift, end) in enumerate(DENSE):
+        select(pf(6 + k), B("BLK"), [[16, 8], [1, 16]], -shift, -1)
+        if end < 16:
+            select(pf(6 + k), pf(6 + k), [[0, 8], [-1, 16]], end - 1, 0)
+    for k, src in ((1, "TRI"), (2, "BLK")):
+        select(pf(k), B(src), [[0, 8], [-1, 16]], 14, 0)
+    memset(B("PF", 384, 768), 0.0)
+    for k in range(3):
+        copy(B("PF", 399 + 128 * k, 512 + 128 * k, 16), B("TRI", 12 + k, 128, 16))
     ts(col(10), col(5), 256.0, None, AL.mult)
     ts(col(6), col(4), 2.0, col(5), AL.mult, AL.add)
-    ts(B("odd"), B("odd"), col(10), None, AL.add)
+    ts(B("odd", 96, 352), B("odd", 96, 352), col(10), None, AL.add)
+    for c in range(3):
+        ts(col(16 + c), col(1), 12.0 - 4 * c, 2.0, AL.is_ge, AL.mult)
+        ts(B("odd", c, 96, 3), B("odd", c, 96, 3), col(16 + c), col(10), AL.add, AL.add)
     for x in range(2):
         for k in range(16):
             copy(B("Xe%d" % x, k, CH, 16), B("obs%d" % x), "a")
+        for k in range(ROWS[0]):
+            copy(B("Xe%d" % x, CH + k, None, ROWS[0]), B("obs%d" % x), "a")
+        copy(B("obsM", 768 + 128 * x, 896 + 128 * x), B("obs%d" % x), "a", -1.0)
     for x in range(2):
         mms(B("psX", 128 * x, 128 * x + 128), [(B("I"), B("obs%d" % x))])
-    memset(B("obsM"), 0.0)
+    memset(B("obsM", 0, 768), 0.0)
     for n in range(NT):
         if SHARE[n][0] % 128:
-            copy(B("obsM", 128 * n, 128 * n + SHARE[n][0] % 128), B("obs%d" % (n % 2), 0, SHARE[n][0] % 128), "a")
+            copy(B("obsM", 128 * n + SHARE[n][0] % 128, 128 * n + 128), B("obs%d" % (n % 2), SHARE[n][0] % 128, 128), "a", -1.0)
     copy(B("NBLK"), B("BLK"), "a", -1.0)
     copy(B("NI"), B("I"), "a", -1.0)
     copy(B("I13"), B("I"), "a", 13.0)
@@ -574,11 +612,11 @@ def rank_program(g, core, T, topo):
         if t == 0:
             if x == 0:
                 gtt(B("Lx"), B("land", 0, 16), B("idx", 0, 16), B("MASKR"), AL.mult)
-            mms(B("psQ", 0, 256), [(B("DUPB", p=kx), B("Lx", p=kx))])
+            mms(B("psE", 256, 512), [(B("DUPB", p=kx), B("Lx", p=kx))])
         else:
             for h in range(2):
-                mms(B("psQ", 128 * h, 128 * h + 128), [(B("RX", 128 * h, 128 * h + 128), B("ld" + X, lo, lo + 128))])
-        copy(B(Tb, 256, 512), B("psQ", 0, 256), ON["src"])
+                mms(B("psE", 128 * h + 256, 128 * h + 384), [(B("RX", 128 * h, 128 * h + 128), B("ld" + X, lo, lo + 128))])
+        copy(B(Tb, 256, 512), B("psE", 256, 512), ON["src"])
         name[0] = "ch%d" % n
         for z in (1, 2):
             buf = B("nXa" if z == 1 else "nXb")
@@ -602,13 +640,22 @@ def rank_program(g, core, T, topo):
             name[0] = "l%d" % n
             gather(rc(z), B(Tb, 0, 256), B(nU, 8 * z, 8 * z + 8), ON["lists"][z])
             name[0] = "col%d" % n
-            P, c = ["psP0", "psP1", "psP0"][z], 256 * z
-            mm(B(P, 0, 256), B("I"), B("c4096"), True, False)
-            mm(B(P, 128, 256), B("BLK"), R0, False, False, True)
-            mm(B(P, 0, 128), B("TRI"), rc(z), False, False)
-            mm(B(P, 128, 256), B("TMO"), rc(z), False, True, True)
-            for a, b in [(0, 64), (64, 256)] if z == 0 else [(0, 256)]:
-                tt(B("v1", c + a, c + b), B(P, a, b), B("odd", a, b), AL.mult)
+            P, c, wg = ["psP0", "psP1", "psP0"][z], place_of(2 * z, 0) // 16, 8 * ROWS[2 * z]
+            G, Hh = B(P, 0, wg), B(P, wg, wg + 128)
+            mm(B(P, 0, wg + 128), B("I"), B("c4096", 0, wg + 128), True, False)
+            mm(Hh, pf(2) if z == 1 else B("BLK"), R0, False, False, True)
+            if z == 0:
+                for k, (v, cc, shift, end) in enumerate(DENSE):
+                    mm(B(P, cc, wg, 3), pf(6 + k), B(w, wo + 128 + v, wo + 256, 4), False, False, k > 0)
+            else:
+                mm(G, pf(3 if z == 1 else 5), rc(0), False, False)
+                if z == 1:
+                    mm(Hh, pf(4), rc(0), False, False, True)
+                mm(G, pf(1), rc(z), False, False)
+            mm(Hh, pf(0), rc(z), False, True, True)
+            o = 96 if z else 0
+            for a, b in [(0, 48), (48, 224)] if z == 0 else [(0, 256)]:
+                tt(B("v1", c + a, c + b), B(P, a, b), B("odd", o + a, o + b), AL.mult)
                 ts(B("v2", c + a, c + b), B("v1", c + a, c + b), 2, 4095, AL.arith_shift_right, AL.bitwise_and)
                 placed[n, z] = copy(B("off" + X, c + a, c + b), B("v2", c + a, c + b))
         name[0] = "pen%d" % n
@@ -636,8 +683,9 @@ def rank_program(g, core, T, topo):
         u, later = 0, []
         for e, ch, a, b, f in pieces(*SHARE[n]):
             name[0] = "g%d.%d" % (n, ch)
-            c0, c1 = CH * ch + 16 * a, CH * ch + 16 * b
-            s, of, xe = B("Sg" + X, c0, c1), B("off" + X, 128 * ch + a, 128 * ch + b), B("Xe" + X, 16 * a, 16 * b)
+            c0, c1 = place_of(ch, a), place_of(ch, b)
+            xe = B("Xe" + X, 16 * a, 16 * b) if ch else B("Xe" + X, CH + c0, CH + c1)
+            s, of = B("Sg" + X, c0, c1), B("off" + X, c0 // 16, c1 // 16)
             if e == "a":
                 i = gather(s, B("S" + X), of, e)
                 steps[i]["due"] = due(128 * ch + a)
@@ -650,7 +698,7 @@ def rank_program(g, core, T, topo):
                         later.append((u, s, xe, c0, c1))
                     u += 1
                 else:
-                    for k in range(15 + ch % 2):
+                    for k in sorted({v[0] for v in terms(ch)}):
                         i = tt(B("Mx" + X, c0 + k, c1, 16), B("Sg" + X, c0 + k, c1, 16), B("psX", 128 * x + a, 128 * x + b), AL.max)
                         steps[i]["due"] = due(128 * ch + a) + PLAN["soon"]
             else:
@@ -667,19 +715,22 @@ def rank_program(g, core, T, topo):
         left = [0]
         mm(B(K, 0, 384), B("ones"), B("KC"), True, left)
         for z in range(3):
-            e = [min(128, max(0, SHARE[n][0] - 128 * (2 * z + gh))) for gh in range(2)]
-            for k, m in [(2, 128)] if e == [128, 128] else [(gh, e[gh]) for gh in range(2) if e[gh]]:
-                xs = B("obs" + X) if m == 128 else B("obsM", 128 * n, 128 * n + 128)
-                mm(B(K, 128 * z, 128 * z + 128), xs, B("WX", 128 * k, 128 * k + 128), False, left, loose=True)
+            mm(B(K, 128 * z, 128 * z + 128), B("obs" + X), B("WX", 256, 384), False, left, loose=True)
             mm(B(K, 128 * z, 128 * z + 128), B("pen" + X, 128 * z, 128 * z + 128), B("BIGP"), False, left, loose=True)
+        for ch in (4, 5):
+            m = min(128, max(0, SHARE[n][0] - 128 * ch))
+            if m < 128:
+                xs = B("obsM", 128 * n, 128 * n + 128) if m else B("obsM", 768 + 128 * x, 896 + 128 * x)
+                mm(B(K, 256, 384), xs, B("WX", 128 * ch - 512, 128 * ch - 384), False, left, loose=True)
+                if ch == 4:
+                    mm(B(K, 120, 128), xs, B("Wm64", 120, 128), False, left, True)
         for ch in range(6):
             name[0] = "s%d.%d" % (n, ch)
-            z, gh = ch // 2, ch % 2
             for buf, wt in (("Sg", "Wm64"), ("Mx", "W128")):
-                for k in range(15 + gh):
-                    a, b = (8 * k + 8, 128) if gh == 0 else (0, 8 * k + 8)
-                    more = {"join": True} if k % 4 else {"loose": True}
-                    mm(B(K, 128 * z + a, 128 * z + b), B(buf + X, CH * ch + k, CH * ch + CH, 16), B(wt, a, b), False, left, **more)
+                for i, (k, z, a, b) in enumerate(terms(ch)):
+                    more = {"join": True} if i % 4 else {"loose": True}
+                    mm(B(K, 128 * z + 8 * a, 128 * z + 8 * b), B(buf + X, place_of(ch, 0) + k, place_of(ch, 128), ROWS[ch]), B(wt, 8 * a, 8 * b),
+                       False, left, **more)
 
     def decide(n):
         x, t = n % 2, n // 2
@@ -717,14 +768,16 @@ def rank_program(g, core, T, topo):
         else:
             send(n + 1, 0, B("T1s" + X))
             send(n + 1, 1, B("Rb"), B("md"))
-            mms(B("psE", 128, 256), [(B("I"), B("Rb")), (B("I"), B("md"))])
-            copy(B(w, wo + 512, wo + 640), B("psE", 128, 256), ON["own"])
+            mms(B(K, 128, 256), [(B("I"), B("Rb")), (B("I"), B("md"))])
+            copy(B(w, wo + 512, wo + 640), B(K, 128, 256), ON["mine"])
         name[0] = "e%d" % n
         ts(B("sc"), B("best"), 6, None, AL.arith_shift_right)
-        mms(B("psD", 128, 136), [(B("I"), B("FLD" + X, 8 + 8 * f, 16 + 8 * f)) for f in range(4)])
-        copy(B("SR" + X), B("psD", 128, 136))
-        mms(B("psD", 136, 144), [(B("I13"), B("SR" + X))])
+        mms(B("psD", 136, 144), [(B("I13"), B("FLD" + X, 8 + 8 * f, 16 + 8 * f)) for f in range(4)])
+        if not last:
+            mms(B("psD", 128, 136), [(B("I"), B("FLD" + X, 8 + 8 * f, 16 + 8 * f)) for f in range(4)])
         tt(B("h2"), B("psD", 136, 144), B("sc"), AL.add)
+        if not last:
+            copy(B("SR" + X), B("psD", 128, 136))
         ts(B("h3"), B("h2"), 255, None, AL.bitwise_and)
         F = B("OF" + X, 0, 8) if last else B("Fn") if t else B("sc")
         if t:
@@ -740,8 +793,8 @@ def rank_program(g, core, T, topo):
             store("sa"[x], T.yn[4 * x:4 * x + 4, :], B("oT" + X, p=(8, 16)))
         else:
             for h in range(2):
-                mms(B("psE", 256 + h, 264, 2), [(B("seven"), B("IND" + X, 32 * r + k, 32 * r + 8, 2)) for r in range(t + 1) for k in range(2)])
-            copy(B("Ai"), B("psE", 256, 264))
+                mms(B("psD", 264 + h, 272, 2), [(B("seven"), B("IND" + X, 32 * r + k, 32 * r + 8, 2)) for r in range(t + 1) for k in range(2)])
+            copy(B("Ai"), B("psD", 264, 272))
             ts(B("A7" + X), B("Ai"), 7, None, AL.bitwise_and)
             tt(B("Tn"), F, B("A7" + X), AL.subtract)
             ts(B(K, 384, 392), B("Tn"), 64.0, None, AL.mult)
@@ -764,4 +817,4 @@ def rank_program(g, core, T, topo):
 
 
 TAGGER = [[""]]
-ON = {"table": "a", "lists": "vaa", "chosen": "v", "own": "a", "src": "v"}
+ON = {"table": "v", "lists": "vaa", "chosen": "v", "own": "a", "src": "v", "mine": "a"}

@@ -6,12 +6,14 @@ AL = AluOpType
 AF = ActivationFunctionType
 NR = 3
 NT = 2 * NR
-CUT = 1024
+CUT = 2048
 MAGIC = 1.5 * 2.0 ** 31
 CH = 2048
-ROWS = [12, 16, 16, 16, 16, 16]
+SITE = 1.5 * 2.0 ** 33
+ROWS = [10, 16, 16, 16, 16, 16]
 ALL = 128 * sum(ROWS)
-DENSE = [(0, 0, 0, 12), (1, 0, 12, 16), (1, 1, -4, 8), (2, 1, 8, 16), (2, 2, -8, 4), (3, 2, 4, 16)]
+W0 = 8 * ROWS[0]
+DENSE = [(v, c, 10 * v - 16 * c, min(16, 10 * v + 10 - 16 * c)) for v in range(8) for c in range(5) if 10 * v - 16 < 16 * c < 10 * v + 10]
 
 
 def place_of(ch, s):
@@ -21,28 +23,33 @@ def place_of(ch, s):
 def terms(ch):
     z = ch // 2
     out = [(k, z, k + 1, 16) if ch % 2 == 0 else (k, z, 0, k + 1) for k in range(min(15, ROWS[ch]))]
-    if ch == 1:
-        out += [(15, y, 0, 16) for y in range(3)]
-    if ch in (2, 3, 4):
-        out.append((15, 0, 11 + ch, 16))
+    if ch:
+        out.append((15, 0, 10 + ch, 16))
     return out
 
 
-def pieces(on_scalar, folded, cut=32):
+def pieces(on_scalar, folded, first):
     out, s = [], 0
-    while s < 768:
-        e = min(s + (96 if s + 96 == on_scalar else 64 if s < on_scalar else cut), s // 128 * 128 + 128)
-        e = min([e] + [x for x in (on_scalar, folded) if x > s])
-        out.append(("a" if s < on_scalar else "v", s // 128, s % 128, s % 128 + e - s, s < folded))
+    while s < 640:
+        step = PLAN["cut"] if s >= on_scalar else 128 if s < PLAN["long"] else 96 if s + 96 in (on_scalar, folded) else 64
+        e = min([s + step, s // 128 * 128 + 128] + [x for x in [on_scalar, folded] + [folded - k for k in PLAN["small"]] if x > s])
+        out.append(("a" if s < on_scalar else "v", 1 + s // 128, s % 128, s % 128 + e - s, s < folded))
+        if e == 128 and first:
+            out.append(("a", 0, 0, first, True))
+        if e == on_scalar:
+            out += [("a", 0, a, min(128, a + PLAN["last"]), False) for a in range(first, 128, PLAN["last"])]
         s = e
     return out
 
 
-SHARE = [(576, 384)] + [(608, 448)] * (NT - 2) + [(576, 320)]
+SHARE = [(480, 320, 0)] + [(480, 384, 0)] * (NT - 2) + [(496, 320, 0)]
 NU = 12
-PLAN = {"cycle": 0.00087, "pe": 0.00044, "gather": 1.6, "wake": 0.17, "issue": 0.5, "first": 1.0, "load": 1.4, "rate": 250e3,
-        "fold": 2.1, "landed": 0.7, "message": 4.5, "passes": 300, "leash": 2.0, "move": 0.3, "lift": 1.0,
-        "turn": 13, "tail": 0.4, "from": 0.1, "to": 1.1, "soon": 0.15, "first_z": -1, "before": 9}
+PLAN = {"cycle": 0.00083, "pe": 0.00042, "gather": 1.56, "wake": 0.17, "issue": 0.35, "first": 1.3, "behind": 5.0, "early": -0.6, "relay": 0.6, "load": 1.5, "rate": 190e3,
+        "fold": 1.2, "landed": 0.65, "message": 3.9, "cases": [(1.0, 230e3, 0.0), (1.1, 150e3, 0.3)], "loss": 0.15, "passes": 20000, "leash": 0.02, "pull": 0.2, "reach": 60,
+        "turn": 12, "long": 0, "fb": 1000, "pad": 0.02, "cut": 32, "last": 64, "small": (), "look": 60, "depth": 3, "tol": 0.22, "alpha": 1,
+        "urgent": {"v": ("d", "lt"), "a": (), "p": ("d", "lt"), "g": ("set",), "s": ()},
+        "lt": -0.7, "src": -0.65, "ch": -0.65, "cb": 0.05, "cc": 0.06, "cd": 0.07, "pen": 0.08, "f": 1.3, "pq": 0.4, "key": 0.45, "g": 0.5, "late": 0.55,
+        "s": 0.6, "d": 1.0, "mine": 1.2, "e": 1.03, "cst": 0.25}
 
 
 def sb(cols, kind="bfloat16"):
@@ -50,30 +57,32 @@ def sb(cols, kind="bfloat16"):
 
 
 SCRATCH = {
-    "rawR": sb(256, "int32"), "raws": sb(16, "int32"), "rawn": sb(16, "int32"), "fitb": sb(256, "int32"), "fitf": sb(256, "float32"),
-    "M0": sb(272), "land": sb(272), "nl": sb(16), "Lx": sb(256), "LxN": sb(256), "LxS": sb(256),
-    "nXa": sb(128), "nXb": sb(128), "s1": sb(128), "v1": sb(768, "int32"), "v2": sb(768, "int32"), "q16": sb(256, "int32"), "q64": sb(128, "int32"),
-    "best": sb(8, "int32"), "bi": sb(16, "int32"), "sc": sb(8, "int32"), "Lz": sb(64), "Ln": sb(64), "offW": sb(8, "uint16"),
-    "Rb": sb(128), "mask": sb(128), "md": sb(128), "h2": sb(8, "int32"), "h3": sb(8, "int32"), "d3": sb(8, "float32"), "d4": sb(8, "float32"),
+    "fitb": sb(256, "int32"), "fitf": sb(256, "float32"), "Lx": sb(512), "LxN": sb(256),
+    "nXa": sb(128), "nXb": sb(128), "s1": sb(128), "v1": sb(768, "int32"), "v2": sb(768, "int32"), "q16": sb(256),
+    "best": sb(8, "int32"), "bi": sb(16, "int32"), "sc": sb(8, "int32"), "Ln": sb(64), "offW": sb(8, "uint16"),
+    "Rb": sb(128), "mask": sb(128), "md": sb(128), "h2": sb(16, "int32"), "d3": sb(16, "float32"),
     "Ai": sb(8, "int32"), "u": sb(8, "float32"), "Fn": sb(8, "float32"), "Tn": sb(8, "float32"),
-    "qi": sb(256, "int32"), "pi": sb(1, "int32"), "ci": sb(16, "int32"), "cf": sb(24, "float32"), "row": sb(640, "int32"),
-    "ones": sb(128), "seven": sb(128), "I": sb(128), "NI": sb(128), "I13": sb(128), "I32": sb(128, "float32"), "BLK": sb(128), "NBLK": sb(128),
-    "TRI": sb(128), "PF": sb(12 * 128), "IMO": sb(128), "DUP": sb(384), "SWP": sb(128), "DUPB": sb(128), "MASKR": sb(256), "RSM": sb(128),
-    "W128": sb(128), "Wm64": sb(128), "BIGP": sb(128), "WX": sb(384), "cnt": sb(256), "KC": sb(384), "BB": sb(32), "EW": sb(240),
-    "mA8": sb(64), "mA1": sb(64), "idx": sb(32, "uint16"), "thrc": sb(32), "RX": sb(256), "site": sb(128), "SEL": sb(8), "ilist": sb(8),
-    "odd": sb(352, "float32"), "c4096": sb(256), "cm127": sb(128), "obsM": sb(1024),
+    "hf": sb(512, "float32"), "hi": sb(64, "int32"), "ho": sb(16, "uint16"), "hd": sb(512), "cst": sb(16, "float32"), "c8": sb(32),
+    "qi": sb(128), "pi": sb(1, "int32"), "ci": sb(16, "int32"), "cf": sb(24, "float32"), "row": sb(896),
+    "ones": sb(128), "seven": sb(128), "I": sb(128), "I13": sb(128), "I32": sb(128, "float32"), "BLK": sb(128), "dif": sb(128),
+    "TRI": sb(128), "PF": sb((8 + len(DENSE)) * 128), "IMO": sb(128), "DUP": sb(256), "MASKR": sb(256), "RSM": sb(128),
+    "W128": sb(128), "Wm64": sb(128), "BIGP": sb(128), "WX": sb(256), "cnt": sb(128), "KC": sb(384), "BB": sb(160), "EW": sb(240),
+    "mA8": sb(80), "mA1": sb(64), "idx": sb(32, "uint16"), "thrc": sb(64), "RX": sb(256), "RY": sb(128), "ilist": sb(8),
+    "odd": sb(W0 + 256, "float32"), "oddM": sb(128, "float32"), "c4096": sb(256), "cm127": sb(128),
+    "obsM": sb(128 * (NT + 2)),
     "psK0": ("psum", [128, 512], "float32"), "psK1": ("psum", [128, 512], "float32"), "psP0": ("psum", [128, 512], "float32"),
     "psP1": ("psum", [128, 512], "float32"), "psQ": ("psum", [128, 512], "float32"), "psX": ("psum", [128, 512], "float32"),
     "psD": ("psum", [128, 512], "float32"), "psE": ("psum", [128, 512], "float32"),
 }
 for x in range(2):
     SCRATCH.update({n + str(x): v for n, v in {
-        "S": sb(4096), "obs": sb(128), "Xe": sb(CH + 128 * ROWS[0]), "W": sb(NR * 512), "ld": sb(512), "Tb": sb(512), "nU": sb(24, "uint16"),
-        "off": sb(ALL // 16, "uint16"), "pen": sb(384), "Sg": sb(ALL), "Mx": sb(ALL), "Fh": sb(ALL), "FLD": sb(128), "DT": sb(512), "T1s": sb(128),
-        "NX": sb(8), "SR": sb(8), "IND": sb(NR * 32), "A7": sb(8, "int32"), "Rf": sb(128, "float32"), "OF": sb(16, "float32"),
+        "S": sb(4096), "obs": sb(128), "Xe": sb(CH), "W": sb(NR * 512), "ld": sb(512), "Tb": sb(512), "nU": sb(24, "uint16"),
+        "off": sb(ALL // 16, "uint16"), "pen": sb(384), "Sg": sb(ALL), "Mx": sb(ALL), "Fh": sb(ALL), "FLD": sb(192), "T1s": sb(128),
+        "rawR": sb(256, "int32"), "raws": sb(16, "int32"), "rawn": sb(8, "int32"), "M0": sb(512), "land": sb(512),
+        "NX": sb(8), "SR": sb(8), "IND": sb(NR * 64), "A7": sb(8, "int32"), "Rf": sb(128, "float32"), "OF": sb(16, "float32"),
         "oT": sb(128, "float32")}.items()})
-SEMAPHORES = (["qv", "qa", "qp", "qg", "go", "hb"] + ["ld%d" % i for i in range(15)] + ["st%d" % i for i in range(8)]
-              + ["%s%d%d" % (n, m, p) for n in ("arr", "hop", "loc") for m in range(NT - 1) for p in range(2)]
+SEMAPHORES = (["qv", "qa", "qp", "qg", "go0", "go1", "go2", "hb"] + ["ld%d" % i for i in range(23)] + ["st%d" % i for i in range(8)]
+              + ["%s%d%d" % (n, m, p) for n in ("arr", "hop", "loc") for m in range(NT) for p in range(2)]
               + ["%s%d%d" % (n, x, u) for n in ("fa", "fb") for x in range(2) for u in range(NU)])
 ORDER = {}
 
@@ -99,14 +108,14 @@ def lane(c, hc, u, topo):
 
 
 def pick(src, dst, topo, ranks=()):
-    e = topo.engines(src, dst)[:8]
+    e = topo.engines(src, dst)[:16 if ranks else 8]
     return sum(1 << i for i in e), len(e)
 
 
 def message(m):
-    if m == 0:
-        return 0, "land", [(0, 272)]
-    t, x = (m + 1) // 2, (m + 1) % 2
+    t, x = m // 2, m % 2
+    if t == 0:
+        return 0, "land%d" % x, [(0, 256), (256, 512)]
     return t, "ld%d" % x, [(256 * (t - 1), 256 * (t - 1) + 128), (256 * (t - 1) + 128, 256 * t)]
 
 
@@ -133,7 +142,7 @@ def other_program(g, core, T, topo):
                     g.remote_dma(out_ap=T["Mx%d" % (n % 2)][:, lo:hi], in_ap=T[held(n)][:, lo:hi], remote_sem=T.sem["fb" + s],
                                  local_sem=T.sem["hb"], pid=pid, routing_id=rid, dma_engine_mask=topo.mask(core, c))
                     sent += len(topo.engines(core, c))
-    for m in range(NT - 1):
+    for m in range(NT):
         t, land, parts = message(m)
         for q in range(len(T.cores)):
             dst, via = route(q, t, T.cores, topo)
@@ -142,7 +151,7 @@ def other_program(g, core, T, topo):
             mask, n2 = pick(core, dst, topo)
             rid, pid = topo.addr(dst, core)
             for p, (a, b) in enumerate(parts):
-                g.wait_ge(T.sem["hop%d%d" % (m, p)], pick(T.cores[q], core, topo, T.cores if m else ())[1])
+                g.wait_ge(T.sem["hop%d%d" % (m, p)], pick(T.cores[q], core, topo, t)[1])
                 g.remote_dma(out_ap=T[land][:, a:b], in_ap=T[land][:, a:b], remote_sem=T.sem["arr%d%d" % (m, p)], local_sem=T.sem["hb"],
                              pid=pid, routing_id=rid, dma_engine_mask=mask)
                 sent += n2
@@ -186,10 +195,153 @@ def arrange(steps):
             if v[1][:2] != "ps":
                 rec[v[1]] = [e for e in rec.get(v[1], []) if not (k == "w" and covers(v, e[1]))] + [(k, v, i)]
     span = [st["cost"] + st["bytes"] / PLAN["rate"] * (1 / st["lane"] + st["back"]) + (PLAN["fold"] if st["back"] else 0) for st in steps]
-    ahead = [max(span[i] + st["lat"], (NT + PLAN["tail"] - st["due"]) * PLAN["turn"]) for i, st in enumerate(steps)]
+    ahead = [-st["due"] * PLAN["turn"] for i, st in enumerate(steps)]
     for i in range(n - 1, -1, -1):
         for a, lat in pred[i].items():
-            ahead[a] = max(ahead[a], (span[a] + lat if lat >= 0 else steps[a]["cost"]) + ahead[i])
+            ahead[a] = max(ahead[a], ahead[i] + PLAN["pad"] * (span[a] + lat if lat >= 0 else steps[a]["cost"]) + 1e-5)
+    todo = {}
+    for i in sorted(range(n), key=lambda i: (-ahead[i], i)):
+        todo.setdefault(steps[i]["q"], []).append(i)
+    start, end, free, order = [None] * n, [None] * n, dict({q: 0.0 for q in todo}, dma=0.0, helper=0.0), []
+
+    def ready(i, depth, now):
+        t = 0.0
+        for a, lat in pred[i].items():
+            if start[a] is None:
+                s = ready(a, depth - 1, now) if depth else None
+                if s is None:
+                    return None
+                s = max(s, now, free[steps[a]["q"]])
+                t = max(t, s + (span[a] + lat if lat >= 0 else steps[a]["cost"]))
+            else:
+                t = max(t, end[a] + lat if lat >= 0 else start[a] + steps[a]["cost"])
+        return t
+    clock = {q: 0.0 for q in todo}
+    while len(order) < n:
+        q = min((q for q in todo if todo[q]), key=lambda q: clock[q])
+        now, soon, pick_ = clock[q], [], None
+        for i in todo[q][:PLAN["look"]]:
+            t = ready(i, PLAN["depth"], now)
+            if t is None:
+                continue
+            d = steps[i]["cost"] + steps[i]["back"] * steps[i]["bytes"] / PLAN["rate"]
+            if t <= now and all(start[a] is not None for a in pred[i]):
+                if all(now + d - u <= max(PLAN["tol"], PLAN["alpha"] * (q != "g") * (u - now)) for u in soon):
+                    pick_ = i
+                    break
+            elif steps[i]["name"].rstrip("0123456789.") in PLAN["urgent"][q]:
+                soon.append(max(t, now + 0.01))
+        if pick_ is None:
+            clock[q] = now + 0.03
+            continue
+        i, st = pick_, steps[pick_]
+        todo[q].remove(i)
+        order.append(i)
+        start[i], t = now, now + st["cost"]
+        clock[q] = free[q] = t
+        if st["bytes"]:
+            t = free["dma"] = max(t, free["dma"]) + st["bytes"] / PLAN["rate"]
+        if st["back"]:
+            t = free["helper"] = max(t + PLAN["fold"], free["helper"]) + st["bytes"] / PLAN["rate"]
+        end[i] = t
+    succ = [[] for _ in steps]
+    for i in range(n):
+        for a in pred[i]:
+            succ[a].append(i)
+    queue = [st["q"] for st in steps]
+    costs = [[st["cost"] * slow if st["q"] in "vap" else st["cost"] + more * (st["q"] == "g" and st["bytes"] > 0) for st in steps]
+             for slow, rate, more in PLAN["cases"]]
+    moves = [[st["bytes"] / rate for st in steps] for slow, rate, more in PLAN["cases"]]
+    back = [st["back"] for st in steps]
+    late = [st["lat"] for st in steps]
+    ends = [[(a, lat) for a, lat in pred[i].items() if lat >= 0] for i in range(n)]
+    issued = [[a for a, lat in pred[i].items() if lat < 0] for i in range(n)]
+    fold = PLAN["fold"]
+
+    def times(order, p, old, case):
+        start, end, cause, state, behind = old[0][:], old[1][:], old[2][:], old[3][:], old[6][:]
+        free, last, dma, hand, moved = state[p // 32]
+        free, last, cost, move, extra = dict(free), dict(last), costs[case], moves[case], fold + PLAN["cases"][case][2]
+        for k in range(p // 32 * 32, n):
+            if k % 32 == 0:
+                state[k // 32] = (dict(free), dict(last), dma, hand, moved)
+            i = order[k]
+            q = queue[i]
+            t, c = free[q], last[q]
+            for a, lat in ends[i]:
+                if end[a] + lat > t:
+                    t, c = end[a] + lat, a
+            for a in issued[i]:
+                if start[a] + cost[a] > t:
+                    t, c = start[a] + cost[a], a
+            start[i], cause[i], last[q] = t, c, i
+            t = free[q] = t + cost[i]
+            if move[i]:
+                behind[i], moved = (None if t >= dma else moved), i
+                t = dma = (t if t > dma else dma) + move[i]
+                if back[i]:
+                    t = hand = max(t + extra, hand) + move[i]
+            end[i] = t
+        j = max(finals, key=lambda i: end[i] + late[i])
+        return start, end, cause, state, end[j] + late[j] + PLAN["pull"] * sum(start) / n, j, behind
+    finals, cases = [i for i in range(n) if not succ[i]], range(len(PLAN["cases"]))
+    blank = [[0.0] * n, [0.0] * n, [None] * n, [({q: 0.0 for q in todo}, {q: None for q in todo}, 0.0, 0.0, None)] * (n // 32 + 1), 0, 0, [None] * n]
+    now = [times(order, 0, blank, c) for c in cases]
+    scale = [100.0 / len(cases) / v[4] for v in now]
+
+    def worth(vs):
+        return sum(v[4] * s for v, s in zip(vs, scale))
+    best, seed = (order, now), [1]
+
+    def draw(k):
+        seed[0] = (seed[0] * 1103515245 + 12345) % 2 ** 31
+        return (seed[0] >> 8) % k
+    for it in range(PLAN["passes"]):
+        if it == 0 or fresh:
+            at = {i: k for k, i in enumerate(order)}
+            chain = []
+            for v in now:
+                i = v[5]
+                while i is not None:
+                    c = v[2][i] if v[6][i] is None else v[6][i]
+                    if c is not None and c not in pred[i]:
+                        chain.append(i)
+                    i = c
+        fresh = False
+        j = chain[draw(len(chain))] if chain and draw(8) else draw(n)
+        mates = [k for k in range(at[j] - 1, max(-1, at[j] - PLAN["reach"]), -1) if queue[order[k]] == queue[j]][:6]
+        if not mates:
+            continue
+        k, pj = mates[draw(len(mates))], at[j]
+        if draw(2):
+            keep = {j}
+            for m in range(pj - 1, k - 1, -1):
+                if any(s in keep for s in succ[order[m]]):
+                    keep.add(order[m])
+            if order[k] in keep:
+                continue
+            part_ = [i for i in order[k:pj + 1] if i in keep] + [i for i in order[k:pj + 1] if i not in keep]
+        else:
+            keep = {order[k]}
+            for m in range(k + 1, pj + 1):
+                if any(a in keep for a in pred[order[m]]):
+                    keep.add(order[m])
+            if j in keep:
+                continue
+            part_ = [i for i in order[k:pj + 1] if i not in keep] + [i for i in order[k:pj + 1] if i in keep]
+        trial = order[:k] + part_ + order[pj + 1:]
+        new = [times(trial, k, now[0], 0)]
+        if (new[0][4] - now[0][4]) * scale[0] > PLAN["loss"]:
+            continue
+        new += [times(trial, k, now[c], c) for c in cases[1:]]
+        if worth(new) <= worth(now) + PLAN["leash"] * (1 - it / PLAN["passes"]) * draw(1000) / 1000:
+            order, now, fresh = trial, new, True
+            if worth(now) < worth(best[1]):
+                best = (order, now)
+    order, now = best
+    start = now[0][0]
+    ORDER["when"] = [(st["q"], st["name"], start[i], start[i] + st["cost"], -ahead[i] / PLAN["turn"]) for i, st in enumerate(steps)]
+    return order, now[0][1][now[0][5]] + late[now[0][5]]
     succ = [dict() for _ in steps]
     for i in range(n):
         for a, lat in pred[i].items():
@@ -220,13 +372,24 @@ def arrange(steps):
                 t += d
             end[i] = t
         return start, end
+    def ranked(key):
+        key = list(key)
+        for i in range(n - 1, -1, -1):
+            for a in pred[i]:
+                key[a] = max(key[a], key[i] + 1e-6)
+        return key, sorted(range(n), key=lambda i: (-key[i], i))
     best, rank, seed = None, list(ahead), 1
-    for _ in range(PLAN["passes"]):
+    for it in range(PLAN["passes"]):
         start, end = place(sorted(range(n), key=lambda i: (-rank[i], i)), pred, False)
+        if it % PLAN["fb"] == PLAN["fb"] - 1:
+            start, end = place(ranked([-e for e in end])[1][::-1], succ, True)
+            rank, order = ranked(end)
+            start, end = place(order, pred, False)
         i = max(range(n), key=lambda i: end[i] + steps[i]["lat"])
         length = end[i] + steps[i]["lat"]
         if best is None or length < best[1]:
             best = (sorted(range(n), key=lambda i: (start[i], i)), length, list(rank))
+            ORDER["when"] = [(st["q"], st["name"], start[i], start[i] + st["cost"], -rank[i] / PLAN["turn"]) for i, st in enumerate(steps)]
         elif length > best[1] + PLAN["leash"]:
             rank = list(best[2])
         ends = {(steps[a]["q"], round(start[a] + steps[a]["cost"], 6)): a for a in range(n)}
@@ -252,9 +415,12 @@ def rank_program(g, core, T, topo):
         return
     ENG = {"v": g.vector, "a": g.scalar, "p": g.tensor, "g": g, "s": g.sync}
     total, known, hist, rec, bank = {}, {k: {} for k in ENG}, {}, {}, {}
-    ndma = {"ld": 0, "st": 0}
-    steps, name, tile = [], [""], {}
+    ndma, loads = {"ld": 0, "st": 0}, {}
+    steps, name, tile = [], ["", 0.2], {}
     cyc = PLAN["cycle"]
+
+    def part(kind, n, later=0.0):
+        name[:] = ["%s%d" % (kind, n), n + PLAN[kind] + later]
 
     def need(want, tok):
         s, c = tok
@@ -322,7 +488,7 @@ def rank_program(g, core, T, topo):
             st["reads"], st["writes"], st["cost"] = st["reads"] + reads, st["writes"] + writes, st["cost"] + cost
         else:
             steps.append(dict({"q": q, "calls": [call], "reads": reads, "writes": writes, "cost": cost, "lat": 0.0, "bytes": 0, "after": [],
-                               "ghost": [], "loose": False, "load": False, "back": False, "due": 99, "lane": 1, "name": name[0]}, **more))
+                               "ghost": [], "loose": False, "load": False, "back": False, "due": name[1], "lane": 1, "name": name[0]}, **more))
         return len(steps) - 1
 
     def B(name, lo=0, hi=None, step=1, p=None):
@@ -401,8 +567,8 @@ def rank_program(g, core, T, topo):
         k = ndma[kind]
         ndma[kind] += 1
         size = v[6] * cols(v) * (2 if SCRATCH[v[1]][2] == "bfloat16" else 4)
-        return op(q, lambda e: e.dma_start(out, src), reads, writes, 0.1, sem="%s%d" % (kind, k), inc=16, lat=PLAN["load"], bytes=size,
-                  load=kind == "ld")
+        loads.setdefault(q, []).append(op(q, lambda e: e.dma_start(out, src), reads, writes, 0.06, sem="%s%d" % (kind, k), inc=16, lat=PLAN["load"],
+                                          bytes=size, load=kind == "ld", after=loads.get(q, [])[-1:] if kind == "ld" else []))
 
     def load(q, out, src, reads=()):
         return dma(q, "ld", out[0], src, list(reads), [out], out)
@@ -416,8 +582,8 @@ def rank_program(g, core, T, topo):
             return op("g", lambda e: e.iota(out[0], pattern, base, cm), [], [out], c)
         return op("g", lambda e: e.iota(out[0], pattern, base, cm, allow_small_or_imprecise_dtypes=True), [], [out], c)
 
-    def select(out, a, pattern, base, cm):
-        return op("g", lambda e: e.affine_select(out[0], a[0], pattern, AL.is_ge, 0.0, base, cm), [a], [out], (200 + 2 * cols(out)) * cyc)
+    def select(out, a, pattern, base, cm, o=AL.is_ge):
+        return op("g", lambda e: e.affine_select(out[0], a[0], pattern, o, 0.0, base, cm), [a], [out], (200 + 2 * cols(out)) * cyc)
 
     sends, folded, scalar_last, placed = [], [], [], {}
 
@@ -426,40 +592,51 @@ def rank_program(g, core, T, topo):
         a, b = parts[p]
         dst, via = route(rank, t, T.cores, topo)
         to = dst if via is None else via
-        mask, n = pick(core, to, topo, T.cores if m else ())
+        mask, n = pick(core, to, topo, t)
         rid, pid = topo.addr(to, core)
         rs, ls = T.sem["%s%d%d" % ("arr" if via is None else "hop", m, p)], "loc%d%d" % (m, p)
         tr = RemoteDMATransfer(dst_ids=[DstId(rid=rid, pnc=pid)], dma_engine_mask=mask, remote_sem=rs, srcs=[v[0] for v in src],
                                dsts=[T[land][:, a:b]], alu_op=len(src) - 1)
         sends.append(op("g", lambda e: e.remote_dma_fused([tr], local_sem=T.sem[ls]),
                         list(src), [], PLAN["issue"] + (0 if sends else PLAN["first"]), sem=ls, inc=n, then=False, ghost=[B(land, a, b)],
-                        lat=PLAN["message"] + (0 if sends else PLAN["first"]), bytes=512 * (b - a), after=sends[-1:]))
+                        lat=PLAN["message"] + [PLAN["relay"], PLAN["behind"], 0][min(m, 2)], bytes=512 * (b - a), after=sends[-1:]))
 
-    for m in range(NT - 1):
+    for m in range(NT):
         t, land, parts = message(m)
         for q in range(len(T.cores)):
             dst, via = route(q, t, T.cores, topo)
             if dst == core:
                 for p, (a, b) in enumerate(parts):
                     s = "arr%d%d" % (m, p)
-                    total[s] = pick(T.cores[q] if via is None else via, core, topo, T.cores if m else ())[1]
+                    total[s] = pick(T.cores[q] if via is None else via, core, topo, t if via is None else 0)[1]
                     rec.setdefault(land, []).append(("w", B(land, a, b), "x" + s, (s, total[s])))
 
     HALF = [(0, 64), (64, 128)]
 
     name[0] = "set"
-    load("s", B("rawR"), T.resid[:])
-    load("a", B("raws"), T.src0[:])
-    load("a", B("rawn"), T.nx0[:])
-    for h in range(2):
-        load("s", B("S0", 0, CUT, p=HALF[h]), T.prof[0:64, 0:CUT])
+    def go(k):
+        return [(None, "go%d" % k, 0, 1, 1, True)]
+
+    def signal(k):
+        op("g", lambda e: e.sem_inc(T.sem["go%d" % k], 1), [], go(k), 0.01, sem="go%d" % k, then=False, after=sends[-1:], due=-1)
+
+    def inputs(x, when):
+        for h in range(2):
+            load("sa"[h], B("rawR%d" % x, p=HALF[h]), T.resid[64 * x:64 * x + 64, :], when)
+        for h in range(2):
+            load("sa"[h], B("raws%d" % x, p=HALF[h]), T.src0[64 * x:64 * x + 64, :], when)
+        for h in range(2):
+            load("sa"[h], B("rawn%d" % x, p=HALF[h]), T.nx0[64 * x:64 * x + 64, 8 * h:8 * h + 8], when)
+    inputs(0, [])
     for x in range(2):
         for h in range(2):
-            load("a", B("obs%d" % x, p=HALF[h]), T.obs[64 * x:64 * x + 64, 128 * h:128 * h + 128])
+            load("sa"[h], B("obs%d" % x, p=HALF[h]), T.obs[64 * x:64 * x + 64, 128 * h:128 * h + 128])
     load("a", B("fitb", p=(0, 8)), T.fit0[:])
+    inputs(1, [])
+    load("s", B("S0", 0, CUT, p=HALF[0]), T.prof[0:64, 0:CUT])
     iota(B("pi"), [[0, 1]], 0, 1)
-    iota(B("qi"), [[1, 256]], 0, 0)
-    iota(B("row", 128, 256), [[0, 2], [1, 4], [0, 16]], 0, 0)
+    iota(B("q16"), [[0, 16], [1, 16]], 0, 0)
+    iota(B("qi"), [[1, 128]], 0, 0)
     iota(B("row", 0, 128), [[1, 8], [0, 16]], 0, 0)
     for k, (sh, msk) in ((0, (0, 127)), (1, (0, 15)), (2, (4, 7)), (3, (0, 63)), (4, (4, 3)), (5, (6, 1)), (8, (0, 7)), (9, (3, 1))):
         ts(B("ci", k, k + 1), B("pi"), sh, msk, AL.arith_shift_right, AL.bitwise_and)
@@ -474,130 +651,155 @@ def rank_program(g, core, T, topo):
             return ts(out, row, col(k), None, AL.is_equal)
         return ts(out, row, col(k), w, AL.is_equal, AL.mult)
 
-    copy(B("M0", 0, 16), B("raws"))
-    copy(B("M0", 16, 272), B("rawR"))
-    send(0, 0, B("M0"))
-    go = (None, "go", 0, 1, 1, True)
-    op("g", lambda e: e.sem_inc(T.sem["go"], 1), [], [go], 0.01, sem="go", then=False, after=sends[-1:])
-    for h in range(2):
-        load("s", B("S0", CUT, 4096, p=HALF[h]), T.prof[0:64, CUT:4096], [go])
-    for h in range(2):
-        load("s", B("S1", p=HALF[h]), T.prof[64:128, :], [go])
-    iota(B("row", 256, 384), [[0, 16], [1, 8]], 0, 0)
-    iota(B("odd", 0, 96), [[8, 32], [2, 3]], 1, 0)
-    iota(B("odd", 96, 352), [[0, 2], [2, 128]], 1, 0)
-    iota(B("row", 384, 512), [[1, 2], [2, 4], [0, 16]], 0, 0)
-    iota(B("row", 512, 640), [[0, 2], [2, 4], [0, 16]], 0, 0)
-    iota(B("KC"), [[16, 3], [1, 16], [0, 8]], 16, 0)
-    iota(B("cnt", 0, 128), [[1, 16], [0, 8]], 0, 0)
-    iota(B("cnt", 128, 256), [[-1, 16], [0, 8]], 15, 0)
-    iota(B("thrc"), [[16, 4], [0, 8]], 16, 0)
     q128, q8 = B("qi", 0, 128), B("row", 256, 384)
-    ts(B("q16"), B("qi"), 15, None, AL.bitwise_and)
-    ts(B("q64"), q128, 63, None, AL.bitwise_and)
-    copy(B("idx", 0, 16), B("qi", 0, 16))
+    copy(B("M00", 0, 256), B("rawR0"))
+    send(0, 0, B("M00", 0, 256))
+    copy(B("idx", 0, 16), B("q16", 0, 16))
     same(B("MASKR"), B("q16"), 1)
-    same(B("DUP", 0, 128), B("q64"), 3)
+    same(B("BLK"), B("row", 0, 128), 2)
+    for x in range(2):
+        X = str(x)
+        gtt(B("Lx", 256 * x, 256 * x + 256), B("raws" + X), B("idx", 0, 16), B("MASKR"), AL.mult)
+        mms(B("psE", 256 * x, 256 * x + 256), [(B("BLK"), B("Lx", 256 * x, 256 * x + 256))])
+        copy(B("M0" + X, 256, 512), B("psE", 256 * x, 256 * x + 256), "a")
+        if x:
+            copy(B("M01", 0, 256), B("rawR1"))
+            send(1, 0, B("M01", 0, 256))
+        send(x, 1, B("M0" + X, 256, 512))
+        signal(x)
+        for h in range(1 + x):
+            load("s", B("S" + X, CUT * (1 - x), 4096, p=HALF[h]), T.prof[64 * x:64 * x + 64, CUT * (1 - x):4096], go(x))
+        for a in range(0, 4096 * (1 - x), 1024):
+            copy(B("S0", a, a + 1024, p=HALF[1]), B("S0", a, a + 1024, p=HALF[0]), ON["twice"][a // 1024])
+
+        for h in range(2):
+            copy(B("W" + X, 0, 128, p=HALF[h]), B("M0" + X, 128 * h, 128 * h + 128, p=HALF[h]), "a")
+        copy(B("nU" + X, 0, 8), B("rawn" + X))
+    iota(q8, [[0, 16], [1, 8]], 0, 0)
+    iota(B("row", 128, 256), [[1, 16], [0, 8]], 0, 0)
+    iota(B("row", 512, 640), [[0, 2], [2, 4], [0, 16]], 0, 0)
+    iota(B("row", 640, 768), [[0, 2], [1, 64]], 0, 0)
+    iota(B("row", 384, 512), [[1, 2], [2, 4], [0, 16]], 0, 0)
+    iota(B("row", 768, 896), [[0, 8], [-1024, 16]], 0, 0)
+    iota(B("KC"), [[16, 3], [1, 16], [0, 8]], 16, 0)
+    iota(B("cnt"), [[-1, 16], [0, 8]], 15, 0)
+    iota(B("thrc"), [[0, 2], [16, 4], [0, 8]], 0, 0)
     ts(col(14), col(5), 0.0, None, AL.is_equal)
-    same(B("DUP", 128, 256), B("q64"), 3, col(14))
-    same(B("DUP", 256, 384), B("q64"), 3, col(5))
-    same(B("DUPB"), B("row", 128, 256), 4)
+    same(B("DUP", 0, 128), B("row", 640, 768), 3, col(14))
+    same(B("DUP", 128, 256), B("row", 640, 768), 3, col(5))
     same(B("I"), q128, 0)
     ts(B("RSM"), B("q16", 0, 128), 0.0, None, AL.is_gt)
-    same(B("BLK"), B("row", 0, 128), 2)
-    ts(B("TRI"), q128, col(0), None, AL.is_ge)
-    tt(B("SWP"), B("DUP", 0, 128), B("I"), AL.subtract)
-    copy(B("nl"), B("rawn"))
-    tt(B("TRI"), B("TRI"), B("BLK"), AL.mult)
+    ts(B("dif"), q128, col(0), 99.0, AL.subtract, AL.add)
+    tt(B("dif"), B("dif"), B("BLK"), AL.mult)
+    ts(B("TRI"), B("dif"), 99.0, None, AL.is_ge)
     memset(B("c4096"), 4096.0)
-    for x in range(2):
-        kx = HALF[x]
-        mms(B("psD", 128 * x, 128 * x + 128), [(B("I", p=kx), B("M0", 16 + 128 * x, 144 + 128 * x, p=kx)),
-                                               (B("SWP", p=kx), B("M0", 144 - 128 * x, 272 - 128 * x, p=kx))])
-        mms(B("psE", 8 * x, 8 * x + 8), [(B("I", p=kx), B("nl", 8 * x, 8 * x + 8, p=kx)), (B("SWP", p=kx), B("nl", 8 - 8 * x, 16 - 8 * x, p=kx))])
-    for x in range(2):
-        copy(B("W%d" % x, 0, 128), B("psD", 128 * x, 128 * x + 128), "a")
-        copy(B("nU%d" % x, 0, 8), B("psE", 8 * x, 8 * x + 8))
+
     def pf(k):
         return B("PF", 128 * k, 128 * k + 128)
-    tt(pf(0), B("TRI"), B("BLK"), AL.subtract)
+    copy(B("IMO"), B("BLK"), "a", -1.0)
+    select(pf(0), B("IMO"), [[-1, 128]], -1, 1)
+    select(B("IMO"), B("IMO"), [[-1, 128]], 0, 1, AL.not_equal)
     for k, (v, c, shift, end) in enumerate(DENSE):
-        select(pf(6 + k), B("BLK"), [[16, 8], [1, 16]], -shift, -1)
+        ts(pf(8 + k), B("dif"), 99.0 + shift, None, AL.is_ge)
         if end < 16:
-            select(pf(6 + k), pf(6 + k), [[0, 8], [-1, 16]], end - 1, 0)
+            select(pf(8 + k), pf(8 + k), [[0, 8], [-1, 16]], end - 1, 0)
     for k, src in ((1, "TRI"), (2, "BLK")):
         select(pf(k), B(src), [[0, 8], [-1, 16]], 14, 0)
-    memset(B("PF", 384, 768), 0.0)
-    for k in range(3):
-        copy(B("PF", 399 + 128 * k, 512 + 128 * k, 16), B("TRI", 12 + k, 128, 16))
+    copy(pf(3), pf(0), "a")
+    memset(B("PF", 512, 1024), 0.0)
+    for k in range(5):
+        copy(B("PF", 399 + 128 * k, 512 + 128 * k, 16), B("TRI", 10 + k, 128, 16), "a")
     ts(col(10), col(5), 256.0, None, AL.mult)
+    ts(col(15), col(10), 1.0, None, AL.add)
     ts(col(6), col(4), 2.0, col(5), AL.mult, AL.add)
-    ts(B("odd", 96, 352), B("odd", 96, 352), col(10), None, AL.add)
-    for c in range(3):
-        ts(col(16 + c), col(1), 12.0 - 4 * c, 2.0, AL.is_ge, AL.mult)
-        ts(B("odd", c, 96, 3), B("odd", c, 96, 3), col(16 + c), col(10), AL.add, AL.add)
+    for k in range(2):
+        ts(B("odd", W0 + 128 * k, W0 + 128 * k + 128), q128, 2.0, col(15), AL.mult, AL.add)
+    ts(col(19), col(1), -4.5, None, AL.add)
+    ts(B("odd", 0, W0), B("qi", 0, W0), 16.0, col(19), AL.mult, AL.add)
+    ts(B("v2", 0, W0), B("odd", 0, W0), 1.0 / ROWS[0], None, AL.mult)
+    ts(B("odd", 0, W0), B("v2", 0, W0), 2.0, col(15), AL.mult, AL.add)
     for x in range(2):
         for k in range(16):
             copy(B("Xe%d" % x, k, CH, 16), B("obs%d" % x), "a")
-        for k in range(ROWS[0]):
-            copy(B("Xe%d" % x, CH + k, None, ROWS[0]), B("obs%d" % x), "a")
         copy(B("obsM", 768 + 128 * x, 896 + 128 * x), B("obs%d" % x), "a", -1.0)
     for x in range(2):
         mms(B("psX", 128 * x, 128 * x + 128), [(B("I"), B("obs%d" % x))])
-    memset(B("obsM", 0, 768), 0.0)
     for n in range(NT):
-        if SHARE[n][0] % 128:
-            copy(B("obsM", 128 * n + SHARE[n][0] % 128, 128 * n + 128), B("obs%d" % (n % 2), SHARE[n][0] % 128, 128), "a", -1.0)
-    copy(B("NBLK"), B("BLK"), "a", -1.0)
-    copy(B("NI"), B("I"), "a", -1.0)
+        m = SHARE[n][0] % 128
+        if m:
+            select(B("obsM", 128 * n, 128 * n + 128), B("obsM", 768 + 128 * (n % 2), 896 + 128 * (n % 2)), [[1, 128]], -m, 0)
+            steps[-1]["due"] = n + PLAN["cst"]
     copy(B("I13"), B("I"), "a", 13.0)
-    tt(B("IMO"), B("I"), B("BLK"), AL.subtract)
     memset(B("cm127"), -127.5)
     memset(B("ones"), 1.0 / 128)
     same(B("W128"), q8, 6, 128.0)
-    same(B("Wm64"), q8, 6, -64.0)
+    copy(B("Wm64"), B("W128"), "a", -0.5)
     ts(col(7), col(1), 8.0, col(6), AL.mult, AL.add)
-    memset(B("BB"), 0.0)
-    same(B("SEL"), B("qi", 0, 8), 2)
     same(B("BIGP"), q128, 7, 4194304.0)
-    same(B("BB", 8, 16), B("qi", 0, 8), 6, -1.0)
-    same(B("BB", 16, 24), B("qi", 0, 8), 6)
-    tt(B("WX", 0, 128), B("Wm64"), B("cnt", 0, 128), AL.mult)
-    tt(B("WX", 128, 256), B("Wm64"), B("cnt", 128, 256), AL.mult)
-    ts(B("WX", 256, 384), B("Wm64"), 16.0, None, AL.mult)
-    gtt(B("LxN"), B("nl"), B("idx", 0, 16), B("MASKR"), AL.mult)
-    gtt(B("LxS"), B("M0", 0, 16), B("idx", 0, 16), B("MASKR"), AL.mult)
+    copy(B("BB", 96, 136), B("W128", 0, 40), "a", 0.0)
+    copy(B("BB", 136, 160), B("W128", 0, 24), "a", 1.0 / 128)
+    copy(B("BB", 32, 56), B("W128", 0, 24), "a", 1.0 / 128)
+    for k, wt in enumerate((-1.0, 2.0, -15.0, col(14), col(5))):
+        if k < 3:
+            copy(B("BB", 56 + 8 * k, 64 + 8 * k), B("W128", 0, 8), "a", wt / 128)
+        else:
+            same(B("BB", 56 + 8 * k, 64 + 8 * k), B("qi", 0, 8), 6, wt)
+    tt(B("WX", 0, 128), B("Wm64"), B("row", 128, 256), AL.mult)
+    tt(B("WX", 128, 256), B("Wm64"), B("cnt"), AL.mult)
+    tt(B("oddM"), B("odd", W0, W0 + 128), B("MASKR", 0, 128), AL.mult)
     copy(B("fitf", p=(0, 8)), B("fitb", p=(0, 8)))
     same(B("I32"), q128, 0)
-    for x in range(2):
-        for h in range(2):
-            mms(B("psE", 16 + 16 * x + h, 24 + 16 * x, 2), [(B("LxN", 128 * h, 128 * h + 128), B("SEL", 4 * x, 4 * x + 4))])
-            mms(B("psE", 24 + 16 * x + h, 32 + 16 * x, 2), [(B("LxS", 128 * h, 128 * h + 128), B("SEL", 4 * x, 4 * x + 4))])
     for h in range(2):
-        turn_over(B("psE", 48 + 8 * h, 56 + 8 * h), B("fitf", 128 * h, 128 * h + 128, p=(0, 8)), B("I32", 0, 8, p=(0, 8)))
+        turn_over(B("psD", 48 + 8 * h, 56 + 8 * h), B("fitf", 128 * h, 128 * h + 128, p=(0, 8)), B("I32", 0, 8, p=(0, 8)))
     for x in range(2):
-        copy(B("NX%d" % x), B("psE", 16 + 16 * x, 24 + 16 * x))
-        copy(B("SR%d" % x), B("psE", 24 + 16 * x, 32 + 16 * x))
+        X, o = str(x), 256 * x
+        gtt(B("LxN", 128 * x, 128 * x + 128), B("rawn" + X), B("idx", 0, 8), B("MASKR", 0, 128), AL.mult)
+        mms(B("psD", 16 * x, 16 * x + 8), [(B("LxN", 128 * x, 128 * x + 128), B("BB", 32, 40))])
+        mms(B("psD", 16 * x + 8, 16 * x + 16), [(B("Lx", o + 128 * h, o + 128 * h + 128), B("BB", 80 + 8 * h, 88 + 8 * h)) for h in range(2)])
+        copy(B("NX" + X), B("psD", 16 * x, 16 * x + 8))
+        copy(B("SR" + X), B("psD", 16 * x + 8, 16 * x + 16))
+        part("cst", x)
+        mms(B("psQ", 128 * x, 128 * x + 128), [(B("I"), B("c4096", 0, 128)), (B("BLK"), B("W" + X, 0, 128))])
+        tt(B("hf", o, o + 128), B("psQ", 128 * x, 128 * x + 128), B("oddM"), AL.mult)
+        running_sum(B("hf", o + 128, o + 256), B("RSM"), B("hf", o, o + 128))
+        copy(B("hi", 32 * x, 32 * x + 8), B("hf", o + 143, o + 256, 16))
+        ts(B("hi", 32 * x + 8, 32 * x + 16), B("hi", 32 * x, 32 * x + 8), 2, 4095, AL.arith_shift_right, AL.bitwise_and)
+        copy(B("ho", 8 * x, 8 * x + 8), B("hi", 32 * x + 8, 32 * x + 16))
+        gtt(B("hd", o, o + 128), B("S" + X), B("ho", 8 * x, 8 * x + 8), B("obs" + X), AL.subtract)
+        ts(B("hd", o + 128, o + 256), B("hd", o, o + 128), 0.0, None, AL.max)
+        mms(B("psD", 32 + 8 * x, 40 + 8 * x), [(B("obs" + X), B("BB", 72, 80)), (B("hd", o, o + 128), B("BB", 56, 64)),
+                                               (B("hd", o + 128, o + 256), B("BB", 64, 72))])
+        copy(B("cst", 8 * x, 8 * x + 8), B("psD", 32 + 8 * x, 40 + 8 * x))
         for h in range(2):
-            ts(B("psK%d" % x, 384 + h, 392, 2), B("psE", 48 + 8 * h + 4 * x, 52 + 8 * h + 4 * x), 64.0, None, AL.mult)
+            tt(B("hf", o + h, o + 8, 2), B("psD", 48 + 8 * h + 4 * x, 52 + 8 * h + 4 * x), B("cst", 8 * x + h, 8 * x + 8, 2), AL.subtract)
+        ts(B("psK" + X, 384, 392), B("hf", o, o + 8), 64.0, None, AL.mult)
+        copy(B("hi", 32 * x + 16, 32 * x + 24), B("cst", 8 * x, 8 * x + 8))
+        ts(B("hi", 32 * x + 24, 32 * x + 32), B("hi", 32 * x + 16, 32 * x + 24), 255, None, AL.bitwise_and)
+        copy(B("c8", 8 * x, 8 * x + 8), B("hi", 32 * x + 24, 32 * x + 32))
+        name[:] = ["set", 0.2]
+        copy(B("FLD" + X, 144, 192), B("W128", 0, 48), "a", 0.0)
+        copy(B("c8", 16 + 8 * x, 24 + 8 * x), B("c8", 8 * x, 8 * x + 8), "a", -1.0)
     memset(B("seven"), 7.0)
     memset(B("EW"), 0.0)
-    memset(B("FLD0"), 0.0)
-    memset(B("FLD1"), 0.0)
     copy(B("EW", 112, 128), B("MASKR", 0, 16))
-    same(B("mA8"), B("row", 256, 320), 2, 8.0)
+    same(B("mA8", 0, 64), B("row", 256, 320), 2, 8.0)
+    memset(B("mA8", 64, 80), 1.0)
     same(B("mA1"), B("row", 256, 320), 2)
     ts(B("idx", 16, 20), B("qi", 0, 8, 2), col(9), None, AL.add)
-    ts(B("idx", 20, 22), B("qi", 0, 2), 0.0, col(8), AL.mult, AL.add)
+    ts(B("idx", 20, 24), B("qi", 0, 8, 2), col(9), 8.0, AL.add, AL.add)
+    copy(B("idx", 24, 25), col(1))
+    ts(B("idx", 26, 30), B("qi", 0, 4), 0.0, col(8), AL.mult, AL.add)
     ts(B("ilist"), B("qi", 0, 128, 16), col(1), None, AL.add)
-    copy(B("idx", 24, 32), B("row", 384, 512, 16))
-    memset(B("DT0", 0, 128), 0.0)
-    memset(B("DT1", 0, 128), 0.0)
-    ts(col(11), col(0), 8.0, 100.0, AL.is_lt, AL.mult)
-    ts(col(12), col(11), col(8), None, AL.add)
+    ts(col(11), col(0), 31.5, 16.0, AL.subtract, AL.is_gt)
+    ts(col(12), col(0), 16.0, col(11), AL.is_lt, AL.add)
+    ts(col(12), col(12), 100.0, col(8), AL.mult, AL.add)
     ts(col(13), col(12), -1.0, None, AL.add)
     same(B("RX", 0, 128), B("row", 512, 640), 12)
     same(B("RX", 128, 256), B("row", 512, 640), 13)
+    ts(col(16), col(0), 8.0, 1024.0, AL.is_lt, AL.mult)
+    ts(col(17), col(0), 56.0, None, AL.is_ge)
+    ts(col(16), col(16), col(17), None, AL.add)
+    same(B("RY"), B("row", 384, 512), 8, col(16))
 
     def search(n):
         x, t = n % 2, n // 2
@@ -608,63 +810,62 @@ def rank_program(g, core, T, topo):
         def rc(z):
             return B(w, wo + 128 * (z + 1), wo + 128 * (z + 2))
 
-        name[0] = "src%d" % n
+        part("src", n)
         if t == 0:
-            if x == 0:
-                gtt(B("Lx"), B("land", 0, 16), B("idx", 0, 16), B("MASKR"), AL.mult)
-            mms(B("psE", 256, 512), [(B("DUPB", p=kx), B("Lx", p=kx))])
+            Tb = "land" + X
         else:
             for h in range(2):
                 mms(B("psE", 128 * h + 256, 128 * h + 384), [(B("RX", 128 * h, 128 * h + 128), B("ld" + X, lo, lo + 128))])
-        copy(B(Tb, 256, 512), B("psE", 256, 512), ON["src"])
-        name[0] = "ch%d" % n
+            copy(B(Tb, 256, 512), B("psE", 256, 512), ON["src"])
+        part("ch", n)
         for z in (1, 2):
             buf = B("nXa" if z == 1 else "nXb")
             gtt(buf, B(Tb, 256, 512), B(nU, 8 * z - 8, 8 * z), B("MASKR", 0, 128), AL.mult)
             running_sum(B("s1"), B("RSM"), buf)
             copy(B(nU, 8 * z, 8 * z + 8), B("s1", 15, 128, 16))
-        name[0] = "pq%d" % n
-        mm(B(K, 392, 424), B("nXa"), B("BB"), True, False)
-        mm(B(K, 408, 424), B("nXb"), B("BB", 8, 24), False, False, True)
-        mm(B(K, 392, 400), B("I"), B("SR" + X), False, False, True)
-        mm(B(K, 392, 400), B("NI"), B("NX" + X), False, False, True)
-        mm(B(K, 400, 408), B("I"), B("NX" + X), False, True, True)
-        name[0] = "lt%d" % n
-        if t == 0:
-            mms(B("psP1", 256, 512), [(B("DUP", 128 * x + 128, 128 * x + 256), B("land", 16, 272))])
-        else:
+        part("lt", n)
+        if t:
             for h in range(2):
-                mms(B("psP1", 128 * h + 256, 128 * h + 384), [(B("DUP", 128 * h + 128, 128 * h + 256), B("ld" + X, lo + 128, lo + 256))])
-        copy(B(Tb, 0, 256), B("psP1", 256, 512), ON["table"])
+                mms(B("psP1", 128 * h + 256, 128 * h + 384), [(B("DUP", 128 * h, 128 * h + 128), B("ld" + X, lo + 128, lo + 256))])
+            copy(B(Tb, 0, 256), B("psP1", 256, 512), ON["table"])
+
+        def offsets(P, c, a, b, o):
+            tt(B("v1", c + a, c + b), B(P, a, b), B("odd", o + a, o + b), AL.mult)
+            ts(B("v2", c + a, c + b), B("v1", c + a, c + b), 2, 4095, AL.arith_shift_right, AL.bitwise_and)
+            copy(B("off" + X, c + a, c + b), B("v2", c + a, c + b))
         for z in range(3):
-            name[0] = "l%d" % n
-            gather(rc(z), B(Tb, 0, 256), B(nU, 8 * z, 8 * z + 8), ON["lists"][z])
-            name[0] = "col%d" % n
-            P, c, wg = ["psP0", "psP1", "psP0"][z], place_of(2 * z, 0) // 16, 8 * ROWS[2 * z]
+            part(["lt", "cb", "cc"][z], n, PLAN["early"] * (n == 1 and z == 1))
+            gather(rc(z), B(Tb, 0, 256), B(nU, 8 * z, 8 * z + 8), ON["lists"][z] if n else ON["opening"][z])
+            P, wg = ["psP0", "psP1", "psP0"][z], 128 if z else 0
             G, Hh = B(P, 0, wg), B(P, wg, wg + 128)
             mm(B(P, 0, wg + 128), B("I"), B("c4096", 0, wg + 128), True, False)
-            mm(Hh, pf(2) if z == 1 else B("BLK"), R0, False, False, True)
-            if z == 0:
-                for k, (v, cc, shift, end) in enumerate(DENSE):
-                    mm(B(P, cc, wg, 3), pf(6 + k), B(w, wo + 128 + v, wo + 256, 4), False, False, k > 0)
-            else:
-                mm(G, pf(3 if z == 1 else 5), rc(0), False, False)
-                if z == 1:
-                    mm(Hh, pf(4), rc(0), False, False, True)
+            mm(Hh, pf(2), R0, False, False, True)
+            if z:
+                mm(G, pf(2 + 2 * z), rc(0), False, False)
+                mm(Hh, pf(3 + 2 * z), rc(0), False, False, True)
                 mm(G, pf(1), rc(z), False, False)
-            mm(Hh, pf(0), rc(z), False, True, True)
-            o = 96 if z else 0
-            for a, b in [(0, 48), (48, 224)] if z == 0 else [(0, 256)]:
-                tt(B("v1", c + a, c + b), B(P, a, b), B("odd", o + a, o + b), AL.mult)
-                ts(B("v2", c + a, c + b), B("v1", c + a, c + b), 2, 4095, AL.arith_shift_right, AL.bitwise_and)
-                placed[n, z] = copy(B("off" + X, c + a, c + b), B("v2", c + a, c + b))
-        name[0] = "pen%d" % n
+            mm(Hh, pf(0 if z else 3), rc(z), False, True, z > 0)
+            for a, b in [(0, 256)] if z else [(0, 64), (64, 128)]:
+                offsets(P, place_of(2 * z if z else 1, 0) // 16, a, b, W0)
+        part("cd", n)
+        mm(B("psP1", 0, W0), B("I"), B("c4096", 0, W0), True, False)
+        for k, (v, cc, shift, end) in enumerate(DENSE):
+            mm(B("psP1", cc, W0, 5), pf(8 + k), B(w, wo + 128 + v, wo + 256, 8), False, k == len(DENSE) - 1, True)
+        offsets("psP1", 0, 0, W0, 0)
+        part("pen", n)
         for z in range(3):
             mms(B("psQ", 128 * z, 128 * z + 128), [(B("I"), B("cm127")), (B("BLK"), R0), (B("IMO"), rc(z))])
         ts(B("pen" + X), B("psQ", 0, 384), MAGIC, MAGIC, AL.add, AL.not_equal)
+        part("pq", n)
+        mm(B(K, 392, 456), R0, B("BB", 96, 160), True, False)
+        mm(B(K, 424, 432), B("I"), B("c8", 16 + 8 * x, 24 + 8 * x), False, False, True)
+        for v in [B("FLD" + X, 80 + 8 * f, 88 + 8 * f) for f in range(4)] if t else [B("SR" + X)]:
+            mm(B(K, 392, 400), B("I"), v, False, False, True)
+        mm(B(K, 400, 408), B("I"), B("NX" + X), False, False, True)
+        mm(B(K, 408, 416), B("nXa"), B("BB", 32, 40), False, False)
+        mm(B(K, 416, 432), B("nXb"), B("BB", 32, 48), False, False, True)
         for z in range(3):
-            mms(B("psQ", 128 * z, 128 * z + 128), [(B("BLK"), R0), (B("NBLK"), rc(z))])
-        copy(B("DT" + X, 128, 512), B("psQ", 0, 384), ON["own"])
+            mm(B(K, 432 + 8 * z, 440 + 8 * z), rc(z), B("BB", 56, 64), False, z == 2, z > 0)
 
         hc = helper(core, T.cores, topo)
         rid, pid = topo.addr(hc, core)
@@ -677,58 +878,47 @@ def rank_program(g, core, T, topo):
                              sem=sem, inc=len(es) + len(topo.engines(hc, core)), then=False, bytes=256 * (c1 - c0),
                              lane=len(es) / len(topo.engines(core, hc)),
                              lat=PLAN["landed"], back=True, after=folded[-1:]))
-        def due(s):
-            k = SHARE[n][0]
-            return n + s / k if s < k else n + PLAN["from"] + (PLAN["to"] - PLAN["from"]) * (s - k) / (768 - k)
-        u, later = 0, []
-        for e, ch, a, b, f in pieces(*SHARE[n]):
-            name[0] = "g%d.%d" % (n, ch)
+        u = 0
+        for j, (e, ch, a, b, f) in enumerate(pieces(*SHARE[n])):
+            part("g", n, j / 1000)
+            name[0] += ".%d" % ch
             c0, c1 = place_of(ch, a), place_of(ch, b)
-            xe = B("Xe" + X, 16 * a, 16 * b) if ch else B("Xe" + X, CH + c0, CH + c1)
+            xe = B("Xe" + X, 16 * a, 16 * b)
             s, of = B("Sg" + X, c0, c1), B("off" + X, c0 // 16, c1 // 16)
             if e == "a":
                 i = gather(s, B("S" + X), of, e)
-                steps[i]["due"] = due(128 * ch + a)
                 steps[i]["after"] = scalar_last[-1:]
                 scalar_last.append(i)
                 if f:
-                    if u < PLAN["before"]:
-                        fold(u, s, xe, c0, c1)
-                    else:
-                        later.append((u, s, xe, c0, c1))
+                    fold(u, s, xe, c0, c1)
                     u += 1
                 else:
-                    for k in sorted({v[0] for v in terms(ch)}):
-                        i = tt(B("Mx" + X, c0 + k, c1, 16), B("Sg" + X, c0 + k, c1, 16), B("psX", 128 * x + a, 128 * x + b), AL.max)
-                        steps[i]["due"] = due(128 * ch + a) + PLAN["soon"]
+                    name[1] = n + PLAN["late"]
+                    for k in range(ROWS[ch]):
+                        tt(B("Mx" + X, c0 + k, c1, ROWS[ch]), B("Sg" + X, c0 + k, c1, ROWS[ch]), B("psX", 128 * x + a, 128 * x + b), AL.max)
             else:
-                steps[gtt(s, B("S" + X), of, xe, AL.subtract)]["due"] = due(128 * ch + a)
-                steps[ts(B("Mx" + X, c0, c1), s, 0.0, None, AL.max)]["due"] = due(128 * ch + a) + 0.07
+                gtt(s, B("S" + X), of, xe, AL.subtract)
+                ts(B("Mx" + X, c0, c1), s, 0.0, None, AL.max)
 
         if n:
             decide(n - 1)
-        name[0] = "f%d" % n
-        for args in later:
-            fold(*args)
-            steps[-1]["after"] = steps[-1]["after"] + sends[-1:]
-        name[0] = "key%d" % n
+        part("key", n)
         left = [0]
         mm(B(K, 0, 384), B("ones"), B("KC"), True, left)
         for z in range(3):
-            mm(B(K, 128 * z, 128 * z + 128), B("obs" + X), B("WX", 256, 384), False, left, loose=True)
             mm(B(K, 128 * z, 128 * z + 128), B("pen" + X, 128 * z, 128 * z + 128), B("BIGP"), False, left, loose=True)
-        for ch in (4, 5):
-            m = min(128, max(0, SHARE[n][0] - 128 * ch))
+        for ch in range(1, 6):
+            m = min(128, max(0, SHARE[n][0] - 128 * ch + 128))
             if m < 128:
                 xs = B("obsM", 128 * n, 128 * n + 128) if m else B("obsM", 768 + 128 * x, 896 + 128 * x)
-                mm(B(K, 256, 384), xs, B("WX", 128 * ch - 512, 128 * ch - 384), False, left, loose=True)
-                if ch == 4:
-                    mm(B(K, 120, 128), xs, B("Wm64", 120, 128), False, left, True)
+                mm(B(K, ch // 2 * 128, ch // 2 * 128 + 128), xs, B("WX", ch % 2 * 128, ch % 2 * 128 + 128), False, left, loose=True)
+                mm(B(K, 80 + 8 * ch, 128), xs, B("Wm64", 80 + 8 * ch, 128), False, left, True)
         for ch in range(6):
-            name[0] = "s%d.%d" % (n, ch)
+            part("s", n)
+            name[0] += ".%d" % ch
             for buf, wt in (("Sg", "Wm64"), ("Mx", "W128")):
                 for i, (k, z, a, b) in enumerate(terms(ch)):
-                    more = {"join": True} if i % 4 else {"loose": True}
+                    more = {"join": True} if i % (4 if ch else 2) else {"loose": True}
                     mm(B(K, 128 * z + 8 * a, 128 * z + 8 * b), B(buf + X, place_of(ch, 0) + k, place_of(ch, 128), ROWS[ch]), B(wt, 8 * a, 8 * b),
                        False, left, **more)
 
@@ -737,70 +927,73 @@ def rank_program(g, core, T, topo):
         X, last = str(x), t == NR - 1
         w, K, wo = "W" + X, "psK" + X, 512 * t
         R0 = B(w, 0, 128)
-        IND, nacc = B("IND" + X, 32 * t, 32 * t + 32), B("IND" + X, 32 * t, 32 * t + 8)
+        IND, nacc, FLD = B("IND" + X, 64 * t, 64 * t + 64), B("IND" + X, 64 * t, 64 * t + 8), "FLD" + X
 
         def to_list(out, src, first):
             mms(out, first + [(B("EW", 112 - 16 * (4 * (c % 2) + c // 2), 240 - 16 * (4 * (c % 2) + c // 2)), B(src, 8 * c, 8 * c + 8))
                               for c in range(8)])
-        name[0] = "d%d" % n
+        part("d", n)
         for c in range(8):
-            i = least(B("best", c, c + 1), B(K, c, 392, 8))
-            if n + 1 < NT and PLAN["first_z"] >= 0:
-                steps[i]["after"] = [placed[n + 1, PLAN["first_z"]]]
+            least(B("best", c, c + 1), B(K, c, 392, 8))
+        mm(B("psE", 128, 256), B("row", 768, 896), B("ones"), True, False)
         ts(B("bi", 8, 16), B("best"), 48, None, AL.bitwise_and)
         ts(B("bi", 0, 8), B("best"), 15, None, AL.bitwise_and)
-        gtt(B("Lz"), B("bi", 8, 16), B("idx", 16, 20), B("mA8"), AL.mult)
-        gtt(IND, B("bi", 8, 16), B("idx", 20, 22), B("thrc"), AL.is_lt)
-        gtt(B("site"), B("bi", 0, 8), B("idx", 24, 32), B("q16", 0, 128), AL.is_equal)
-        to_list(B("psD", 0, 8), "Lz", [(B("I"), B("ilist"))])
-        mms(B("psE", 0, 128), [(B("site"), B("I"))])
-        tt(B("FLD" + X, 8, 40), IND, B(K, 392, 424), AL.mult)
+        gtt(IND, B("bi", 8, 16), B("idx", 26, 30), B("thrc"), AL.is_equal)
+        gtt(B(FLD, 0, 80), B("bi"), B("idx", 20, 25), B("mA8"), AL.mult)
+        tt(B(FLD, 80, 144), IND, B(K, 392, 456), AL.mult)
+        mm(B(K, 0, 128), B(FLD, 64, 192), B("I"), True, True)
+        to_list(B("psD", 0, 8), FLD, [(B("I"), B("ilist"))])
+        copy(B("T1s" + X), B(K, 0, 128), ON["turned"])
         copy(B("offW"), B("psD", 0, 8))
-        copy(B("mask"), B("psE", 0, 128))
-        mms(B(K, 0, 128), [(B("FLD" + X), B("I"))])
         gather(B("Rb"), B(w, wo, wo + 512), B("offW"), ON["chosen"])
-        copy(B("T1s" + X), B(K, 0, 128))
-        gtt(B("md"), B("DT" + X), B("offW"), B("mask"), AL.mult)
+        mm(B("psE", 128, 256), B("RY"), B("T1s" + X), False, True)
+        ts(B("mask"), B("psE", 128, 256), SITE, SITE, AL.add, AL.is_equal)
+        tt(B("md"), B("psE", 128, 256), B("mask"), AL.mult)
         if last:
             tt(B("Rf" + X), B("Rb"), B("md"), AL.add)
             for h in range(2):
                 store("sa"[h] if n == NT - 1 else "s", T.yr[64 * x:64 * x + 64, 128 * h:128 * h + 128], B("Rf" + X, p=HALF[h]))
         else:
-            send(n + 1, 0, B("T1s" + X))
-            send(n + 1, 1, B("Rb"), B("md"))
-            mms(B(K, 128, 256), [(B("I"), B("Rb")), (B("I"), B("md"))])
-            copy(B(w, wo + 512, wo + 640), B(K, 128, 256), ON["mine"])
-        name[0] = "e%d" % n
+            send(n + 2, 0, B("T1s" + X))
+            send(n + 2, 1, B("Rb"), B("md"))
+            part("mine", n)
+            mms(B("psE", 0, 128), [(B("I"), B("Rb")), (B("I"), B("md"))])
+            copy(B(w, wo + 512, wo + 640), B("psE", 0, 128), ON["mine"])
+        part("e", n)
         ts(B("sc"), B("best"), 6, None, AL.arith_shift_right)
-        mms(B("psD", 136, 144), [(B("I13"), B("FLD" + X, 8 + 8 * f, 16 + 8 * f)) for f in range(4)])
-        if not last:
-            mms(B("psD", 128, 136), [(B("I"), B("FLD" + X, 8 + 8 * f, 16 + 8 * f)) for f in range(4)])
-        tt(B("h2"), B("psD", 136, 144), B("sc"), AL.add)
-        if not last:
-            copy(B("SR" + X), B("psD", 128, 136))
-        ts(B("h3"), B("h2"), 255, None, AL.bitwise_and)
-        F = B("OF" + X, 0, 8) if last else B("Fn") if t else B("sc")
-        if t:
+        mms(B("psD", 136, 144), [(B("I"), B("c8", 8 * x, 8 * x + 8)), (B("I"), B(FLD, 112, 120))]
+            + [(B("I13"), B(FLD, 88 + 8 * f, 96 + 8 * f)) for f in range(3)])
+        h3 = B("h2", 8, 16)
+        tt(B("d3", 0, 8), B("sc"), nacc, AL.mult)
+        tt(B("d3", 8, 16), B("sc"), B("d3", 0, 8), AL.subtract)
+        tt(B("h2", 0, 8), B("psD", 136, 144), B("d3", 8, 16), AL.add)
+        ts(h3, B("h2", 0, 8), 255, None, AL.bitwise_and)
+        F = B("Fn") if t else B("sc")
+        if last:
             tt(B("u"), nacc, B("A7" + X), AL.mult)
             tt(F, B("sc"), B("u"), AL.add)
-        tt(B("d3"), B("h3"), B(K, 416, 424), AL.subtract)
-        tt(B("d4"), B("d3"), nacc, AL.mult)
-        tt(B("OF" + X, 8, 16) if last else B("NX" + X), B("h3"), B("d4"), AL.subtract)
+            tt(B("OF" + X, 0, 8), F, B("cst", 8 * x, 8 * x + 8), AL.add)
         if last:
+            copy(B("OF" + X, 8, 16), h3)
             turn_over(B("psD", 256, 384, p=(0, 16)), B("OF" + X), B("I32"))
             copy(B("oT" + X, p=(0, 16)), B("psD", 256, 384, p=(0, 16)))
             store("s", T.yf[4 * x:4 * x + 4, :], B("oT" + X, p=(0, 8)))
             store("sa"[x], T.yn[4 * x:4 * x + 4, :], B("oT" + X, p=(8, 16)))
         else:
+            gtt(B("Ln"), h3, B("idx", 16, 20), B("mA1"), AL.mult)
+            copy(B("NX" + X), h3)
+            to_list(B("psD", 256, 264), "Ln", [])
+            copy(B("nU" + X, 0, 8), B("psD", 256, 264))
+            part("f", n)
+            if t:
+                tt(B("u"), nacc, B("A7" + X), AL.mult)
+                tt(F, B("sc"), B("u"), AL.add)
             for h in range(2):
-                mms(B("psD", 264 + h, 272, 2), [(B("seven"), B("IND" + X, 32 * r + k, 32 * r + 8, 2)) for r in range(t + 1) for k in range(2)])
+                mms(B("psD", 264 + h, 272, 2), [(B("seven"), B("IND" + X, 64 * r + k, 64 * r + 8, 2)) for r in range(t + 1) for k in range(2)])
             copy(B("Ai"), B("psD", 264, 272))
             ts(B("A7" + X), B("Ai"), 7, None, AL.bitwise_and)
             tt(B("Tn"), F, B("A7" + X), AL.subtract)
             ts(B(K, 384, 392), B("Tn"), 64.0, None, AL.mult)
-            gtt(B("Ln"), B("NX" + X), B("idx", 16, 20), B("mA1"), AL.mult)
-            to_list(B("psD", 256, 264), "Ln", [])
-            copy(B("nU" + X, 0, 8), B("psD", 256, 264))
 
     for n in range(NT):
         search(n)
@@ -817,4 +1010,4 @@ def rank_program(g, core, T, topo):
 
 
 TAGGER = [[""]]
-ON = {"table": "v", "lists": "vaa", "chosen": "v", "own": "a", "src": "v", "mine": "a"}
+ON = {"table": "v", "lists": "vaa", "chosen": "v", "turned": "v", "src": "a", "mine": "v", "opening": "vvv", "twice": "avav"}

import numpy as np
from concourse.bass import DstId, RemoteDMATransfer
from concourse.mybir import dt, AluOpType, AxisListType, ActivationFunctionType

AL = AluOpType
AF = ActivationFunctionType
NR = 3
NT = 2 * NR
CUT = 2048
MAGIC = 1.5 * 2.0 ** 31
CH = 2048
SITE = 1.5 * 2.0 ** 33
ROWS = [10, 16, 16, 16, 16, 16]
ALL = 128 * sum(ROWS)
W0 = 8 * ROWS[0]
DENSE = [(v, c, 10 * v - 16 * c, min(16, 10 * v + 10 - 16 * c)) for v in range(8) for c in range(5) if 10 * v - 16 < 16 * c < 10 * v + 10]


def place_of(ch, s):
    return 128 * sum(ROWS[:ch]) + ROWS[ch] * s


def terms(ch):
    z = ch // 2
    out = [(k, z, k + 1, 16) if ch % 2 == 0 else (k, z, 0, k + 1) for k in range(min(15, ROWS[ch]))]
    if ch:
        out.append((15, 0, 10 + ch, 16))
    return out


def pieces(on_scalar, folded, first):
    out, s = [], 0
    while s < 640:
        step = PLAN["cut"] if s >= on_scalar else 128 if s < PLAN["long"] else 96 if s + 96 in (on_scalar, folded) else 64
        e = min([s + step, s // 128 * 128 + 128] + [x for x in [on_scalar, folded] + [folded - k for k in PLAN["small"]] if x > s])
        out.append(("a" if s < on_scalar else "v", 1 + s // 128, s % 128, s % 128 + e - s, s < folded))
        if e == 128 and first:
            out.append(("a", 0, 0, first, True))
        if e == on_scalar:
            out += [("a", 0, a, min(128, a + PLAN["last"]), False) for a in range(first, 128, PLAN["last"])]
        s = e
    return out


SHARE = [(480, 320, 0)] + [(480, 384, 0)] * (NT - 2) + [(496, 320, 0)]
NU = 12
PLAN = {"cycle": 0.00083, "pe": 0.00042, "gather": 1.56, "wake": 0.17, "issue": 0.35, "first": 1.3, "behind": 5.0, "early": -0.6, "relay": 0.6, "load": 1.5, "rate": 190e3,
        "fold": 1.2, "landed": 0.65, "message": 3.9, "cases": [(1.0, 230e3, 0.0), (1.1, 150e3, 0.3)], "loss": 0.15, "passes": 20000, "leash": 0.02, "pull": 0.2, "reach": 60,
        "turn": 12, "long": 0, "fb": 1000, "pad": 0.02, "cut": 32, "last": 64, "small": (), "look": 60, "depth": 3, "tol": 0.22, "alpha": 1,
        "urgent": {"v": ("d", "lt"), "a": (), "p": ("d", "lt"), "g": ("set",), "s": ()},
        "lt": -0.7, "src": -0.65, "ch": -0.65, "cb": 0.05, "cc": 0.06, "cd": 0.07, "pen": 0.08, "f": 1.3, "pq": 0.4, "key": 0.45, "g": 0.5, "late": 0.55,
        "s": 0.6, "d": 1.0, "mine": 1.2, "e": 1.03, "cst": 0.25}


def sb(cols, kind="bfloat16"):
    return ("sbuf", [128, cols], kind)


SCRATCH = {
    "fitb": sb(256, "int32"), "fitf": sb(256, "float32"), "Lx": sb(512), "LxN": sb(256),
    "nXa": sb(128), "nXb": sb(128), "s1": sb(128), "v1": sb(768, "int32"), "v2": sb(768, "int32"), "q16": sb(256),
    "best": sb(8, "int32"), "bi": sb(16, "int32"), "sc": sb(8, "int32"), "Ln": sb(64), "offW": sb(8, "uint16"),
    "Rb": sb(128), "mask": sb(128), "md": sb(128), "h2": sb(16, "int32"), "d3": sb(16, "float32"),
    "Ai": sb(8, "int32"), "u": sb(8, "float32"), "Fn": sb(8, "float32"), "Tn": sb(8, "float32"),
    "hf": sb(512, "float32"), "hi": sb(64, "int32"), "ho": sb(16, "uint16"), "hd": sb(512), "cst": sb(16, "float32"), "c8": sb(32),
    "qi": sb(128), "pi": sb(1, "int32"), "ci": sb(16, "int32"), "cf": sb(24, "float32"), "row": sb(896),
    "ones": sb(128), "seven": sb(128), "I": sb(128), "I13": sb(128), "I32": sb(128, "float32"), "BLK": sb(128), "dif": sb(128),
    "TRI": sb(128), "PF": sb((8 + len(DENSE)) * 128), "IMO": sb(128), "DUP": sb(256), "MASKR": sb(256), "RSM": sb(128),
    "W128": sb(128), "Wm64": sb(128), "BIGP": sb(128), "WX": sb(256), "cnt": sb(128), "KC": sb(384), "BB": sb(160), "EW": sb(240),
    "mA8": sb(80), "mA1": sb(64), "idx": sb(32, "uint16"), "thrc": sb(64), "RX": sb(256), "RY": sb(128), "ilist": sb(8),
    "odd": sb(W0 + 256, "float32"), "oddM": sb(128, "float32"), "c4096": sb(256), "cm127": sb(128),
    "obsM": sb(128 * (NT + 2)),
    "psK0": ("psum", [128, 512], "float32"), "psK1": ("psum", [128, 512], "float32"), "psP0": ("psum", [128, 512], "float32"),
    "psP1": ("psum", [128, 512], "float32"), "psQ": ("psum", [128, 512], "float32"), "psX": ("psum", [128, 512], "float32"),
    "psD": ("psum", [128, 512], "float32"), "psE": ("psum", [128, 512], "float32"),
}
for x in range(2):
    SCRATCH.update({n + str(x): v for n, v in {
        "S": sb(4096), "obs": sb(128), "Xe": sb(CH), "W": sb(NR * 512), "ld": sb(512), "Tb": sb(512), "nU": sb(24, "uint16"),
        "off": sb(ALL // 16, "uint16"), "pen": sb(384), "Sg": sb(ALL), "Mx": sb(ALL), "Fh": sb(ALL), "FLD": sb(192), "T1s": sb(128),
        "rawR": sb(256, "int32"), "raws": sb(16, "int32"), "rawn": sb(8, "int32"), "M0": sb(512), "land": sb(512),
        "NX": sb(8), "SR": sb(8), "IND": sb(NR * 64), "A7": sb(8, "int32"), "Rf": sb(128, "float32"), "OF": sb(16, "float32"),
        "oT": sb(128, "float32")}.items()})
SEMAPHORES = (["qv", "qa", "qp", "qg", "go0", "go1", "go2", "hb"] + ["ld%d" % i for i in range(23)] + ["st%d" % i for i in range(8)]
              + ["%s%d%d" % (n, m, p) for n in ("arr", "hop", "loc") for m in range(NT) for p in range(2)]
              + ["%s%d%d" % (n, x, u) for n in ("fa", "fb") for x in range(2) for u in range(NU)])
ORDER = {}


def route(q, t, cores, topo):
    n = len(cores)
    src, dst = cores[q], cores[(q - 1 - (t % (n - 1))) % n]
    if topo.may_write(src, dst):
        return dst, None
    for c in topo.cores_of(src):
        if c not in cores and topo.die(c) == topo.die(src) and topo.may_write(c, dst):
            return dst, c
    return dst, None


def helper(c, cores, topo):
    used = [route(q, t, cores, topo)[1] for q in range(len(cores)) for t in range(NR)]
    return [x for x in topo.cores_of(c) if x not in cores and x not in used and topo.die(x) == topo.die(c)][0]


def lane(c, hc, u, topo):
    return topo.engines(c, hc)


def pick(src, dst, topo, ranks=()):
    e = topo.engines(src, dst)[:16 if ranks else 8]
    return sum(1 << i for i in e), len(e)


def message(m):
    t, x = m // 2, m % 2
    if t == 0:
        return 0, "land%d" % x, [(0, 256), (256, 512)]
    return t, "ld%d" % x, [(256 * (t - 1), 256 * (t - 1) + 128), (256 * (t - 1) + 128, 256 * t)]


def folds(n):
    return [(c, a, b) for e, c, a, b, f in pieces(*SHARE[n]) if f]


def held(n):
    return ["Mx", "Sg", "Fh"][n // 2] + str(n % 2)


def other_program(g, core, T, topo):
    sent = 0
    for c in T.cores:
        if helper(c, T.cores, topo) == core:
            rid, pid = topo.addr(c, core)
            seen = {}
            for n in range(NT):
                for u, (ch, a, b) in enumerate(folds(n)):
                    s = "%d%d" % (n % 2, u)
                    seen[s] = seen.get(s, 0) + len(lane(c, core, u, topo))
                    lo, hi = place_of(ch, a), place_of(ch, b)
                    g.wait_ge(T.sem["fa" + s], seen[s])
                    g.remote_dma(out_ap=T["Mx%d" % (n % 2)][:, lo:hi], in_ap=T[held(n)][:, lo:hi], remote_sem=T.sem["fb" + s],
                                 local_sem=T.sem["hb"], pid=pid, routing_id=rid, dma_engine_mask=topo.mask(core, c))
                    sent += len(topo.engines(core, c))
    for m in range(NT):
        t, land, parts = message(m)
        for q in range(len(T.cores)):
            dst, via = route(q, t, T.cores, topo)
            if via != core:
                continue
            mask, n2 = pick(core, dst, topo)
            rid, pid = topo.addr(dst, core)
            for p, (a, b) in enumerate(parts):
                g.wait_ge(T.sem["hop%d%d" % (m, p)], pick(T.cores[q], core, topo, t)[1])
                g.remote_dma(out_ap=T[land][:, a:b], in_ap=T[land][:, a:b], remote_sem=T.sem["arr%d%d" % (m, p)], local_sem=T.sem["hb"],
                             pid=pid, routing_id=rid, dma_engine_mask=mask)
                sent += n2
    if sent:
        g.wait_ge(T.sem["hb"], sent)


def clash(r, v):
    s = v[4]
    return r[2] < v[3] and v[2] < r[3] and not (s > 1 and s == r[4] and (r[2] - v[2]) % s)


def covers(v, r):
    s = v[4]
    return v[5] and v[2] <= r[2] and r[3] <= v[3] and (s == 1 or (s == r[4] and (r[2] - v[2]) % s == 0))


def arrange(steps):
    wake, n = PLAN["wake"], len(steps)
    pred, rec, bank = [dict() for _ in steps], {}, {}

    def edge(a, b, data):
        sa = steps[a]
        lat = sa["lat"] + wake if data or sa["q"] != steps[b]["q"] or sa["lat"] else 0.0
        if a != b and pred[b].get(a, -1.0) < lat:
            pred[b][a] = lat
    for i, st in enumerate(steps):
        for a in st["after"]:
            pred[i][a] = -steps[a]["bytes"] / PLAN["rate"]
        views = [("r", v) for v in st["reads"]] + [("w", v) for v in st["writes"] + st["ghost"]]
        for b in {v[1] for k, v in views if v[1][:2] == "ps"}:
            last, loose = bank.get(b, ([], []))
            for a in last + ([] if st["loose"] else loose):
                edge(a, i, steps[a]["q"] != "p" and b in [v[1] for v in steps[a]["writes"]])
            bank[b] = (last, loose + [i]) if st["loose"] else ([i], [])
        for k, v in views:
            for k2, r, a in rec.get(v[1], []) if v[1][:2] != "ps" else []:
                if (k == "w" or k2 == "w") and clash(r, v) and not (st["load"] and steps[a]["load"]):
                    edge(a, i, True)
        for k, v in views:
            if v[1][:2] != "ps":
                rec[v[1]] = [e for e in rec.get(v[1], []) if not (k == "w" and covers(v, e[1]))] + [(k, v, i)]
    span = [st["cost"] + st["bytes"] / PLAN["rate"] * (1 / st["lane"] + st["back"]) + (PLAN["fold"] if st["back"] else 0) for st in steps]
    ahead = [-st["due"] * PLAN["turn"] for i, st in enumerate(steps)]
    for i in range(n - 1, -1, -1):
        for a, lat in pred[i].items():
            ahead[a] = max(ahead[a], ahead[i] + PLAN["pad"] * (span[a] + lat if lat >= 0 else steps[a]["cost"]) + 1e-5)
    todo = {}
    for i in sorted(range(n), key=lambda i: (-ahead[i], i)):
        todo.setdefault(steps[i]["q"], []).append(i)
    start, end, free, order = [None] * n, [None] * n, dict({q: 0.0 for q in todo}, dma=0.0, helper=0.0), []

    def ready(i, depth, now):
        t = 0.0
        for a, lat in pred[i].items():
            if start[a] is None:
                s = ready(a, depth - 1, now) if depth else None
                if s is None:
                    return None
                s = max(s, now, free[steps[a]["q"]])
                t = max(t, s + (span[a] + lat if lat >= 0 else steps[a]["cost"]))
            else:
                t = max(t, end[a] + lat if lat >= 0 else start[a] + steps[a]["cost"])
        return t
    clock = {q: 0.0 for q in todo}
    while len(order) < n:
        q = min((q for q in todo if todo[q]), key=lambda q: clock[q])
        now, soon, pick_ = clock[q], [], None
        for i in todo[q][:PLAN["look"]]:
            t = ready(i, PLAN["depth"], now)
            if t is None:
                continue
            d = steps[i]["cost"] + steps[i]["back"] * steps[i]["bytes"] / PLAN["rate"]
            if t <= now and all(start[a] is not None for a in pred[i]):
                if all(now + d - u <= max(PLAN["tol"], PLAN["alpha"] * (q != "g") * (u - now)) for u in soon):
                    pick_ = i
                    break
            elif steps[i]["name"].rstrip("0123456789.") in PLAN["urgent"][q]:
                soon.append(max(t, now + 0.01))
        if pick_ is None:
            clock[q] = now + 0.03
            continue
        i, st = pick_, steps[pick_]
        todo[q].remove(i)
        order.append(i)
        start[i], t = now, now + st["cost"]
        clock[q] = free[q] = t
        if st["bytes"]:
            t = free["dma"] = max(t, free["dma"]) + st["bytes"] / PLAN["rate"]
        if st["back"]:
            t = free["helper"] = max(t + PLAN["fold"], free["helper"]) + st["bytes"] / PLAN["rate"]
        end[i] = t
    succ = [[] for _ in steps]
    for i in range(n):
        for a in pred[i]:
            succ[a].append(i)
    queue = [st["q"] for st in steps]
    costs = [[st["cost"] * slow if st["q"] in "vap" else st["cost"] + more * (st["q"] == "g" and st["bytes"] > 0) for st in steps]
             for slow, rate, more in PLAN["cases"]]
    moves = [[st["bytes"] / rate for st in steps] for slow, rate, more in PLAN["cases"]]
    back = [st["back"] for st in steps]
    late = [st["lat"] for st in steps]
    ends = [[(a, lat) for a, lat in pred[i].items() if lat >= 0] for i in range(n)]
    issued = [[a for a, lat in pred[i].items() if lat < 0] for i in range(n)]
    fold = PLAN["fold"]

    def times(order, p, old, case):
        start, end, cause, state, behind = old[0][:], old[1][:], old[2][:], old[3][:], old[6][:]
        free, last, dma, hand, moved = state[p // 32]
        free, last, cost, move, extra = dict(free), dict(last), costs[case], moves[case], fold + PLAN["cases"][case][2]
        for k in range(p // 32 * 32, n):
            if k % 32 == 0:
                state[k // 32] = (dict(free), dict(last), dma, hand, moved)
            i = order[k]
            q = queue[i]
            t, c = free[q], last[q]
            for a, lat in ends[i]:
                if end[a] + lat > t:
                    t, c = end[a] + lat, a
            for a in issued[i]:
                if start[a] + cost[a] > t:
                    t, c = start[a] + cost[a], a
            start[i], cause[i], last[q] = t, c, i
            t = free[q] = t + cost[i]
            if move[i]:
                behind[i], moved = (None if t >= dma else moved), i
                t = dma = (t if t > dma else dma) + move[i]
                if back[i]:
                    t = hand = max(t + extra, hand) + move[i]
            end[i] = t
        j = max(finals, key=lambda i: end[i] + late[i])
        return start, end, cause, state, end[j] + late[j] + PLAN["pull"] * sum(start) / n, j, behind
    finals, cases = [i for i in range(n) if not succ[i]], range(len(PLAN["cases"]))
    blank = [[0.0] * n, [0.0] * n, [None] * n, [({q: 0.0 for q in todo}, {q: None for q in todo}, 0.0, 0.0, None)] * (n // 32 + 1), 0, 0, [None] * n]
    now = [times(order, 0, blank, c) for c in cases]
    scale = [100.0 / len(cases) / v[4] for v in now]

    def worth(vs):
        return sum(v[4] * s for v, s in zip(vs, scale))
    best, seed = (order, now), [1]

    def draw(k):
        seed[0] = (seed[0] * 1103515245 + 12345) % 2 ** 31
        return (seed[0] >> 8) % k
    for it in range(PLAN["passes"]):
        if it == 0 or fresh:
            at = {i: k for k, i in enumerate(order)}
            chain = []
            for v in now:
                i = v[5]
                while i is not None:
                    c = v[2][i] if v[6][i] is None else v[6][i]
                    if c is not None and c not in pred[i]:
                        chain.append(i)
                    i = c
        fresh = False
        j = chain[draw(len(chain))] if chain and draw(8) else draw(n)
        mates = [k for k in range(at[j] - 1, max(-1, at[j] - PLAN["reach"]), -1) if queue[order[k]] == queue[j]][:6]
        if not mates:
            continue
        k, pj = mates[draw(len(mates))], at[j]
        if draw(2):
            keep = {j}
            for m in range(pj - 1, k - 1, -1):
                if any(s in keep for s in succ[order[m]]):
                    keep.add(order[m])
            if order[k] in keep:
                continue
            part_ = [i for i in order[k:pj + 1] if i in keep] + [i for i in order[k:pj + 1] if i not in keep]
        else:
            keep = {order[k]}
            for m in range(k + 1, pj + 1):
                if any(a in keep for a in pred[order[m]]):
                    keep.add(order[m])
            if j in keep:
                continue
            part_ = [i for i in order[k:pj + 1] if i not in keep] + [i for i in order[k:pj + 1] if i in keep]
        trial = order[:k] + part_ + order[pj + 1:]
        new = [times(trial, k, now[0], 0)]
        if (new[0][4] - now[0][4]) * scale[0] > PLAN["loss"]:
            continue
        new += [times(trial, k, now[c], c) for c in cases[1:]]
        if worth(new) <= worth(now) + PLAN["leash"] * (1 - it / PLAN["passes"]) * draw(1000) / 1000:
            order, now, fresh = trial, new, True
            if worth(now) < worth(best[1]):
                best = (order, now)
    order, now = best
    start = now[0][0]
    ORDER["when"] = [(st["q"], st["name"], start[i], start[i] + st["cost"], -ahead[i] / PLAN["turn"]) for i, st in enumerate(steps)]
    return order, now[0][1][now[0][5]] + late[now[0][5]]
    succ = [dict() for _ in steps]
    for i in range(n):
        for a, lat in pred[i].items():
            succ[a][i] = lat

    def place(order, before, back):
        start, end, busy = [0.0] * n, [0.0] * n, {}
        for i in order:
            st = steps[i]
            parts = [(st["q"], st["cost"])] + ([(st["lane"], st["bytes"] / PLAN["rate"] / st["lane"])] if st["bytes"] else [])
            if st["back"]:
                parts += [(-i, PLAN["fold"]), ("helper", st["bytes"] / PLAN["rate"])]
            t = max([end[a] + lat if lat >= 0 or back else start[a] + steps[a]["cost"] for a, lat in before[i].items()]
                    + [st["lat"] if back else 0.0])
            for j, (q, d) in enumerate(parts[::-1] if back else parts):
                L, k = busy.setdefault(q, []), 0
                lo, hi = 0, len(L)
                while lo < hi:
                    mid = (lo + hi) // 2
                    lo, hi = (mid + 1, hi) if L[mid][1] <= t else (lo, mid)
                for k in range(lo, len(L) + 1):
                    if k == len(L) or t + d <= L[k][0]:
                        break
                    t = max(t, L[k][1])
                L.insert(k, (t, t + d))
                if j == 0:
                    start[i] = t
                t += d
            end[i] = t
        return start, end
    def ranked(key):
        key = list(key)
        for i in range(n - 1, -1, -1):
            for a in pred[i]:
                key[a] = max(key[a], key[i] + 1e-6)
        return key, sorted(range(n), key=lambda i: (-key[i], i))
    best, rank, seed = None, list(ahead), 1
    for it in range(PLAN["passes"]):
        start, end = place(sorted(range(n), key=lambda i: (-rank[i], i)), pred, False)
        if it % PLAN["fb"] == PLAN["fb"] - 1:
            start, end = place(ranked([-e for e in end])[1][::-1], succ, True)
            rank, order = ranked(end)
            start, end = place(order, pred, False)
        i = max(range(n), key=lambda i: end[i] + steps[i]["lat"])
        length = end[i] + steps[i]["lat"]
        if best is None or length < best[1]:
            best = (sorted(range(n), key=lambda i: (start[i], i)), length, list(rank))
            ORDER["when"] = [(st["q"], st["name"], start[i], start[i] + st["cost"], -rank[i] / PLAN["turn"]) for i, st in enumerate(steps)]
        elif length > best[1] + PLAN["leash"]:
            rank = list(best[2])
        ends = {(steps[a]["q"], round(start[a] + steps[a]["cost"], 6)): a for a in range(n)}
        while i is not None:
            ready = [(end[a] + lat if lat >= 0 else start[a] + steps[a]["cost"], a) for a, lat in pred[i].items()]
            t, a = max(ready + [(0.0, None)], key=lambda v: v[0])
            if start[i] > t + 1e-6:
                a = ends.get((steps[i]["q"], round(start[i], 6)), a)
                seed = (seed * 1103515245 + 12345) % 2 ** 31
                if seed >> 16 < PLAN["move"] * 2 ** 15:
                    rank[i] += min(start[i] - t, PLAN["lift"])
            i = a
        for i in range(n - 1, -1, -1):
            for a in pred[i]:
                rank[a] = max(rank[a], rank[i] + 1e-4)
    return best[:2]


def rank_program(g, core, T, topo):
    rank = T.rank_of(core)
    if rank is None:
        other_program(g, core, T, topo)
        return
    ENG = {"v": g.vector, "a": g.scalar, "p": g.tensor, "g": g, "s": g.sync}
    total, known, hist, rec, bank = {}, {k: {} for k in ENG}, {}, {}, {}
    ndma, loads = {"ld": 0, "st": 0}, {}
    steps, name, tile = [], ["", 0.2], {}
    cyc = PLAN["cycle"]

    def part(kind, n, later=0.0):
        name[:] = ["%s%d" % (kind, n), n + PLAN[kind] + later]

    def need(want, tok):
        s, c = tok
        if want.get(s, 0) < c:
            want[s] = c

    def learn(q, s, c):
        k = known[q]
        for a, b in hist.get((s, c), {}).items():
            if k.get(a, 0) < b:
                k[a] = b
        if k.get(s, 0) < c:
            k[s] = c

    def wait(q, want):
        for s, c in sorted(want.items(), key=lambda x: x[0]):
            if known[q].get(s, 0) < c:
                ENG[q].wait_ge(T.sem[s], c)
                learn(q, s, c)

    def issue(q, fn, reads, writes, sem, inc, then):
        own = sem is None
        s = "q" + q if own else sem
        tag = q if own else "x" + sem
        want = {}
        for v in reads + writes:
            if v[1][:2] == "ps":
                for a, tok in bank.get(v[1], {}).items():
                    if a != tag:
                        need(want, tok)
                if q == "p":
                    shape = (reads[0][7], reads[0][6], v[6])
                    if tile.get(v[1], shape) != shape and "p" in bank[v[1]]:
                        need(want, bank[v[1]]["p"])
                    tile[v[1]] = shape
        for v in reads:
            for k, r, tg, tok in rec.get(v[1], []):
                if k == "w" and clash(r, v):
                    need(want, tok)
        for v in writes:
            for k, r, tg, tok in rec.get(v[1], []):
                if clash(r, v) and not (tg[:3] == "xld" and tag[:3] == "xld"):
                    need(want, tok)
        wait(q, want)
        ins = fn(ENG[q])
        total[s] = total.get(s, 0) + inc
        tok = (s, total[s])
        if then:
            ins.then_inc(T.sem[s], inc)
        hist[tok] = dict(known[q])
        for kind, views in (("r", reads), ("w", writes)):
            for v in views:
                if v[1][:2] == "ps":
                    bank.setdefault(v[1], {})[tag] = tok
                    if q == "p":
                        continue
                L = [e for e in rec.get(v[1], []) if not ((kind == "w" or (e[0] == "r" and e[2] == tag)) and covers(v, e[1]))]
                rec[v[1]] = L + [(kind, v, tag, tok)]

    def op(q, fn, reads, writes, cost, sem=None, inc=1, then=True, join=False, **more):
        call = (q, fn, reads, writes, sem, inc, then)
        if join:
            st = steps[-1]
            st["calls"].append(call)
            st["reads"], st["writes"], st["cost"] = st["reads"] + reads, st["writes"] + writes, st["cost"] + cost
        else:
            steps.append(dict({"q": q, "calls": [call], "reads": reads, "writes": writes, "cost": cost, "lat": 0.0, "bytes": 0, "after": [],
                               "ghost": [], "loose": False, "load": False, "back": False, "due": name[1], "lane": 1, "name": name[0]}, **more))
        return len(steps) - 1

    def B(name, lo=0, hi=None, step=1, p=None):
        t = T[name]
        hi = t.shape[1] if hi is None else hi
        a, b = p or (0, 128)
        return (t[a:b, lo:hi] if step == 1 else t[a:b, lo:hi:step], name, lo, hi, step, p is None, b - a, a)

    def ind(win, of):
        return win[0].indirect(of[0])

    def cols(v):
        return (v[3] - v[2] + v[4] - 1) // v[4]

    def stream(out, *ins):
        narrow = all(SCRATCH[v[1]][0] == "sbuf" and SCRATCH[v[1]][2] in ("bfloat16", "uint16") for v in (out,) + ins)
        return max(64, cols(out) * (0.5 if narrow else 1)) * cyc

    def picked(out):
        return (65 + cols(out) * PLAN["gather"]) * cyc

    def tt(out, a, b, o):
        c = max(64, cols(out) * (1 if "ps" in (a[1][:2], b[1][:2]) else 2)) * cyc
        return op("v", lambda e: e.tensor_tensor(out[0], a[0], b[0], o), [a, b], [out], c)

    def gtt(out, win, of, b, o):
        return op("v", lambda e: e.tensor_tensor(out[0], ind(win, of), b[0], o), [win, of, b], [out], picked(out))

    def ts(out, a, s1, s2, o0, o1=None):
        col = [s for s in (s1, s2) if isinstance(s, tuple)]
        x, y = [s[0] if isinstance(s, tuple) else s for s in (s1, s2)]
        if o1 is None:
            return op("v", lambda e: e.tensor_scalar(out[0], a[0], x, None, o0), [a] + col, [out], stream(out, a))
        return op("v", lambda e: e.tensor_scalar(out[0], a[0], x, y, o0, o1), [a] + col, [out], stream(out, a))

    def copy(out, a, q="v", scale=None):
        if q == "v":
            return op("v", lambda e: e.tensor_copy(out[0], a[0]), [a], [out], stream(out, a))
        c = max(64, cols(out)) * cyc
        if scale is None:
            return op("a", lambda e: e.activation(out[0], a[0], AF.Copy), [a], [out], c)
        return op("a", lambda e: e.activation(out[0], a[0], AF.Copy, scale=scale), [a], [out], c)

    def gather(out, win, of, q="v"):
        if q == "v":
            return op("v", lambda e: e.tensor_copy(out[0], ind(win, of)), [win, of], [out], picked(out))
        return op("a", lambda e: e.activation(out[0], ind(win, of), AF.Copy), [win, of], [out], picked(out))

    def memset(out, c):
        return op("v", lambda e: e.memset(out[0], c), [], [out], stream(out))

    def running_sum(out, keep, a):
        return op("v", lambda e: e.tensor_tensor_scan(out[0], keep[0], a[0], 0.0, AL.mult, AL.add), [keep, a], [out], stream(out, a))

    def least(out, a):
        return op("v", lambda e: e.tensor_reduce(out[0], a[0], AxisListType.X, AL.min), [a], [out], 64 * cyc)

    def mm(out, l, r, start, stop, join=False, **more):
        def fn(e):
            if isinstance(stop, list):
                stop[0] -= 1
                return e.matmul(out[0], l[0], r[0], start, stop[0] == 0)
            return e.matmul(out[0], l[0], r[0], start, stop)
        if isinstance(stop, list):
            stop[0] += 1
        return op("p", fn, [l, r], [out], max(64, cols(r)) * PLAN["pe"], join=join, **more)

    def mms(out, pairs):
        for i, (l, r) in enumerate(pairs):
            mm(out, l, r, i == 0, i == len(pairs) - 1, i > 0)

    def turn_over(out, a, ident):
        return op("p", lambda e: e.transpose(out[0], a[0], ident[0]), [a, ident], [out], 512 * PLAN["pe"])

    def dma(q, kind, out, src, reads, writes, v):
        k = ndma[kind]
        ndma[kind] += 1
        size = v[6] * cols(v) * (2 if SCRATCH[v[1]][2] == "bfloat16" else 4)
        loads.setdefault(q, []).append(op(q, lambda e: e.dma_start(out, src), reads, writes, 0.06, sem="%s%d" % (kind, k), inc=16, lat=PLAN["load"],
                                          bytes=size, load=kind == "ld", after=loads.get(q, [])[-1:] if kind == "ld" else []))

    def load(q, out, src, reads=()):
        return dma(q, "ld", out[0], src, list(reads), [out], out)

    def store(q, out, src):
        return dma(q, "st", out, src[0], [src], [], src)

    def iota(out, pattern, base, cm):
        c = (160 + 2 * cols(out)) * cyc
        if SCRATCH[out[1]][2] == "int32":
            return op("g", lambda e: e.iota(out[0], pattern, base, cm), [], [out], c)
        return op("g", lambda e: e.iota(out[0], pattern, base, cm, allow_small_or_imprecise_dtypes=True), [], [out], c)

    def select(out, a, pattern, base, cm, o=AL.is_ge):
        return op("g", lambda e: e.affine_select(out[0], a[0], pattern, o, 0.0, base, cm), [a], [out], (200 + 2 * cols(out)) * cyc)

    sends, folded, scalar_last, placed = [], [], [], {}

    def send(m, p, *src):
        t, land, parts = message(m)
        a, b = parts[p]
        dst, via = route(rank, t, T.cores, topo)
        to = dst if via is None else via
        mask, n = pick(core, to, topo, t)
        rid, pid = topo.addr(to, core)
        rs, ls = T.sem["%s%d%d" % ("arr" if via is None else "hop", m, p)], "loc%d%d" % (m, p)
        tr = RemoteDMATransfer(dst_ids=[DstId(rid=rid, pnc=pid)], dma_engine_mask=mask, remote_sem=rs, srcs=[v[0] for v in src],
                               dsts=[T[land][:, a:b]], alu_op=len(src) - 1)
        sends.append(op("g", lambda e: e.remote_dma_fused([tr], local_sem=T.sem[ls]),
                        list(src), [], PLAN["issue"] + (0 if sends else PLAN["first"]), sem=ls, inc=n, then=False, ghost=[B(land, a, b)],
                        lat=PLAN["message"] + [PLAN["relay"], PLAN["behind"], 0][min(m, 2)], bytes=512 * (b - a), after=sends[-1:]))

    for m in range(NT):
        t, land, parts = message(m)
        for q in range(len(T.cores)):
            dst, via = route(q, t, T.cores, topo)
            if dst == core:
                for p, (a, b) in enumerate(parts):
                    s = "arr%d%d" % (m, p)
                    total[s] = pick(T.cores[q] if via is None else via, core, topo, t if via is None else 0)[1]
                    rec.setdefault(land, []).append(("w", B(land, a, b), "x" + s, (s, total[s])))

    HALF = [(0, 64), (64, 128)]

    name[0] = "set"
    def go(k):
        return [(None, "go%d" % k, 0, 1, 1, True)]

    def signal(k):
        op("g", lambda e: e.sem_inc(T.sem["go%d" % k], 1), [], go(k), 0.01, sem="go%d" % k, then=False, after=sends[-1:], due=-1)

    def inputs(x, when):
        for h in range(2):
            load("sa"[h], B("rawR%d" % x, p=HALF[h]), T.resid[64 * x:64 * x + 64, :], when)
        for h in range(2):
            load("sa"[h], B("raws%d" % x, p=HALF[h]), T.src0[64 * x:64 * x + 64, :], when)
        for h in range(2):
            load("sa"[h], B("rawn%d" % x, p=HALF[h]), T.nx0[64 * x:64 * x + 64, 8 * h:8 * h + 8], when)
    inputs(0, [])
    for x in range(2):
        for h in range(2):
            load("sa"[h], B("obs%d" % x, p=HALF[h]), T.obs[64 * x:64 * x + 64, 128 * h:128 * h + 128])
    load("a", B("fitb", p=(0, 8)), T.fit0[:])
    inputs(1, [])
    load("s", B("S0", 0, CUT, p=HALF[0]), T.prof[0:64, 0:CUT])
    iota(B("pi"), [[0, 1]], 0, 1)
    iota(B("q16"), [[0, 16], [1, 16]], 0, 0)
    iota(B("qi"), [[1, 128]], 0, 0)
    iota(B("row", 0, 128), [[1, 8], [0, 16]], 0, 0)
    for k, (sh, msk) in ((0, (0, 127)), (1, (0, 15)), (2, (4, 7)), (3, (0, 63)), (4, (4, 3)), (5, (6, 1)), (8, (0, 7)), (9, (3, 1))):
        ts(B("ci", k, k + 1), B("pi"), sh, msk, AL.arith_shift_right, AL.bitwise_and)
    copy(B("cf", 0, 6), B("ci", 0, 6))
    copy(B("cf", 8, 10), B("ci", 8, 10))

    def col(k):
        return B("cf", k, k + 1)

    def same(out, row, k, w=None):
        if w is None:
            return ts(out, row, col(k), None, AL.is_equal)
        return ts(out, row, col(k), w, AL.is_equal, AL.mult)

    q128, q8 = B("qi", 0, 128), B("row", 256, 384)
    copy(B("M00", 0, 256), B("rawR0"))
    send(0, 0, B("M00", 0, 256))
    copy(B("idx", 0, 16), B("q16", 0, 16))
    same(B("MASKR"), B("q16"), 1)
    same(B("BLK"), B("row", 0, 128), 2)
    for x in range(2):
        X = str(x)
        gtt(B("Lx", 256 * x, 256 * x + 256), B("raws" + X), B("idx", 0, 16), B("MASKR"), AL.mult)
        mms(B("psE", 256 * x, 256 * x + 256), [(B("BLK"), B("Lx", 256 * x, 256 * x + 256))])
        copy(B("M0" + X, 256, 512), B("psE", 256 * x, 256 * x + 256), "a")
        if x:
            copy(B("M01", 0, 256), B("rawR1"))
            send(1, 0, B("M01", 0, 256))
        send(x, 1, B("M0" + X, 256, 512))
        signal(x)
        for h in range(1 + x):
            load("s", B("S" + X, CUT * (1 - x), 4096, p=HALF[h]), T.prof[64 * x:64 * x + 64, CUT * (1 - x):4096], go(x))
        for a in range(0, 4096 * (1 - x), 1024):
            copy(B("S0", a, a + 1024, p=HALF[1]), B("S0", a, a + 1024, p=HALF[0]), ON["twice"][a // 1024])

        for h in range(2):
            copy(B("W" + X, 0, 128, p=HALF[h]), B("M0" + X, 128 * h, 128 * h + 128, p=HALF[h]), "a")
        copy(B("nU" + X, 0, 8), B("rawn" + X))
    iota(q8, [[0, 16], [1, 8]], 0, 0)
    iota(B("row", 128, 256), [[1, 16], [0, 8]], 0, 0)
    iota(B("row", 512, 640), [[0, 2], [2, 4], [0, 16]], 0, 0)
    iota(B("row", 640, 768), [[0, 2], [1, 64]], 0, 0)
    iota(B("row", 384, 512), [[1, 2], [2, 4], [0, 16]], 0, 0)
    iota(B("row", 768, 896), [[0, 8], [-1024, 16]], 0, 0)
    iota(B("KC"), [[16, 3], [1, 16], [0, 8]], 16, 0)
    iota(B("cnt"), [[-1, 16], [0, 8]], 15, 0)
    iota(B("thrc"), [[0, 2], [16, 4], [0, 8]], 0, 0)
    ts(col(14), col(5), 0.0, None, AL.is_equal)
    same(B("DUP", 0, 128), B("row", 640, 768), 3, col(14))
    same(B("DUP", 128, 256), B("row", 640, 768), 3, col(5))
    same(B("I"), q128, 0)
    ts(B("RSM"), B("q16", 0, 128), 0.0, None, AL.is_gt)
    ts(B("dif"), q128, col(0), 99.0, AL.subtract, AL.add)
    tt(B("dif"), B("dif"), B("BLK"), AL.mult)
    ts(B("TRI"), B("dif"), 99.0, None, AL.is_ge)
    memset(B("c4096"), 4096.0)

    def pf(k):
        return B("PF", 128 * k, 128 * k + 128)
    copy(B("IMO"), B("BLK"), "a", -1.0)
    select(pf(0), B("IMO"), [[-1, 128]], -1, 1)
    select(B("IMO"), B("IMO"), [[-1, 128]], 0, 1, AL.not_equal)
    for k, (v, c, shift, end) in enumerate(DENSE):
        ts(pf(8 + k), B("dif"), 99.0 + shift, None, AL.is_ge)
        if end < 16:
            select(pf(8 + k), pf(8 + k), [[0, 8], [-1, 16]], end - 1, 0)
    for k, src in ((1, "TRI"), (2, "BLK")):
        select(pf(k), B(src), [[0, 8], [-1, 16]], 14, 0)
    copy(pf(3), pf(0), "a")
    memset(B("PF", 512, 1024), 0.0)
    for k in range(5):
        copy(B("PF", 399 + 128 * k, 512 + 128 * k, 16), B("TRI", 10 + k, 128, 16), "a")
    ts(col(10), col(5), 256.0, None, AL.mult)
    ts(col(15), col(10), 1.0, None, AL.add)
    ts(col(6), col(4), 2.0, col(5), AL.mult, AL.add)
    for k in range(2):
        ts(B("odd", W0 + 128 * k, W0 + 128 * k + 128), q128, 2.0, col(15), AL.mult, AL.add)
    ts(col(19), col(1), -4.5, None, AL.add)
    ts(B("odd", 0, W0), B("qi", 0, W0), 16.0, col(19), AL.mult, AL.add)
    ts(B("v2", 0, W0), B("odd", 0, W0), 1.0 / ROWS[0], None, AL.mult)
    ts(B("odd", 0, W0), B("v2", 0, W0), 2.0, col(15), AL.mult, AL.add)
    for x in range(2):
        for k in range(16):
            copy(B("Xe%d" % x, k, CH, 16), B("obs%d" % x), "a")
        copy(B("obsM", 768 + 128 * x, 896 + 128 * x), B("obs%d" % x), "a", -1.0)
    for x in range(2):
        mms(B("psX", 128 * x, 128 * x + 128), [(B("I"), B("obs%d" % x))])
    for n in range(NT):
        m = SHARE[n][0] % 128
        if m:
            select(B("obsM", 128 * n, 128 * n + 128), B("obsM", 768 + 128 * (n % 2), 896 + 128 * (n % 2)), [[1, 128]], -m, 0)
            steps[-1]["due"] = n + PLAN["cst"]
    copy(B("I13"), B("I"), "a", 13.0)
    memset(B("cm127"), -127.5)
    memset(B("ones"), 1.0 / 128)
    same(B("W128"), q8, 6, 128.0)
    copy(B("Wm64"), B("W128"), "a", -0.5)
    ts(col(7), col(1), 8.0, col(6), AL.mult, AL.add)
    same(B("BIGP"), q128, 7, 4194304.0)
    copy(B("BB", 96, 136), B("W128", 0, 40), "a", 0.0)
    copy(B("BB", 136, 160), B("W128", 0, 24), "a", 1.0 / 128)
    copy(B("BB", 32, 56), B("W128", 0, 24), "a", 1.0 / 128)
    for k, wt in enumerate((-1.0, 2.0, -15.0, col(14), col(5))):
        if k < 3:
            copy(B("BB", 56 + 8 * k, 64 + 8 * k), B("W128", 0, 8), "a", wt / 128)
        else:
            same(B("BB", 56 + 8 * k, 64 + 8 * k), B("qi", 0, 8), 6, wt)
    tt(B("WX", 0, 128), B("Wm64"), B("row", 128, 256), AL.mult)
    tt(B("WX", 128, 256), B("Wm64"), B("cnt"), AL.mult)
    tt(B("oddM"), B("odd", W0, W0 + 128), B("MASKR", 0, 128), AL.mult)
    copy(B("fitf", p=(0, 8)), B("fitb", p=(0, 8)))
    same(B("I32"), q128, 0)
    for h in range(2):
        turn_over(B("psD", 48 + 8 * h, 56 + 8 * h), B("fitf", 128 * h, 128 * h + 128, p=(0, 8)), B("I32", 0, 8, p=(0, 8)))
    for x in range(2):
        X, o = str(x), 256 * x
        gtt(B("LxN", 128 * x, 128 * x + 128), B("rawn" + X), B("idx", 0, 8), B("MASKR", 0, 128), AL.mult)
        mms(B("psD", 16 * x, 16 * x + 8), [(B("LxN", 128 * x, 128 * x + 128), B("BB", 32, 40))])
        mms(B("psD", 16 * x + 8, 16 * x + 16), [(B("Lx", o + 128 * h, o + 128 * h + 128), B("BB", 80 + 8 * h, 88 + 8 * h)) for h in range(2)])
        copy(B("NX" + X), B("psD", 16 * x, 16 * x + 8))
        copy(B("SR" + X), B("psD", 16 * x + 8, 16 * x + 16))
        part("cst", x)
        mms(B("psQ", 128 * x, 128 * x + 128), [(B("I"), B("c4096", 0, 128)), (B("BLK"), B("W" + X, 0, 128))])
        tt(B("hf", o, o + 128), B("psQ", 128 * x, 128 * x + 128), B("oddM"), AL.mult)
        running_sum(B("hf", o + 128, o + 256), B("RSM"), B("hf", o, o + 128))
        copy(B("hi", 32 * x, 32 * x + 8), B("hf", o + 143, o + 256, 16))
        ts(B("hi", 32 * x + 8, 32 * x + 16), B("hi", 32 * x, 32 * x + 8), 2, 4095, AL.arith_shift_right, AL.bitwise_and)
        copy(B("ho", 8 * x, 8 * x + 8), B("hi", 32 * x + 8, 32 * x + 16))
        gtt(B("hd", o, o + 128), B("S" + X), B("ho", 8 * x, 8 * x + 8), B("obs" + X), AL.subtract)
        ts(B("hd", o + 128, o + 256), B("hd", o, o + 128), 0.0, None, AL.max)
        mms(B("psD", 32 + 8 * x, 40 + 8 * x), [(B("obs" + X), B("BB", 72, 80)), (B("hd", o, o + 128), B("BB", 56, 64)),
                                               (B("hd", o + 128, o + 256), B("BB", 64, 72))])
        copy(B("cst", 8 * x, 8 * x + 8), B("psD", 32 + 8 * x, 40 + 8 * x))
        for h in range(2):
            tt(B("hf", o + h, o + 8, 2), B("psD", 48 + 8 * h + 4 * x, 52 + 8 * h + 4 * x), B("cst", 8 * x + h, 8 * x + 8, 2), AL.subtract)
        ts(B("psK" + X, 384, 392), B("hf", o, o + 8), 64.0, None, AL.mult)
        copy(B("hi", 32 * x + 16, 32 * x + 24), B("cst", 8 * x, 8 * x + 8))
        ts(B("hi", 32 * x + 24, 32 * x + 32), B("hi", 32 * x + 16, 32 * x + 24), 255, None, AL.bitwise_and)
        copy(B("c8", 8 * x, 8 * x + 8), B("hi", 32 * x + 24, 32 * x + 32))
        name[:] = ["set", 0.2]
        copy(B("FLD" + X, 144, 192), B("W128", 0, 48), "a", 0.0)
        copy(B("c8", 16 + 8 * x, 24 + 8 * x), B("c8", 8 * x, 8 * x + 8), "a", -1.0)
    memset(B("seven"), 7.0)
    memset(B("EW"), 0.0)
    copy(B("EW", 112, 128), B("MASKR", 0, 16))
    same(B("mA8", 0, 64), B("row", 256, 320), 2, 8.0)
    memset(B("mA8", 64, 80), 1.0)
    same(B("mA1"), B("row", 256, 320), 2)
    ts(B("idx", 16, 20), B("qi", 0, 8, 2), col(9), None, AL.add)
    ts(B("idx", 20, 24), B("qi", 0, 8, 2), col(9), 8.0, AL.add, AL.add)
    copy(B("idx", 24, 25), col(1))
    ts(B("idx", 26, 30), B("qi", 0, 4), 0.0, col(8), AL.mult, AL.add)
    ts(B("ilist"), B("qi", 0, 128, 16), col(1), None, AL.add)
    ts(col(11), col(0), 31.5, 16.0, AL.subtract, AL.is_gt)
    ts(col(12), col(0), 16.0, col(11), AL.is_lt, AL.add)
    ts(col(12), col(12), 100.0, col(8), AL.mult, AL.add)
    ts(col(13), col(12), -1.0, None, AL.add)
    same(B("RX", 0, 128), B("row", 512, 640), 12)
    same(B("RX", 128, 256), B("row", 512, 640), 13)
    ts(col(16), col(0), 8.0, 1024.0, AL.is_lt, AL.mult)
    ts(col(17), col(0), 56.0, None, AL.is_ge)
    ts(col(16), col(16), col(17), None, AL.add)
    same(B("RY"), B("row", 384, 512), 8, col(16))

    def search(n):
        x, t = n % 2, n // 2
        X = str(x)
        w, K, kx, wo, lo = "W" + X, "psK" + X, HALF[x], 512 * t, 256 * (t - 1)
        R0, nU, Tb = B(w, 0, 128), "nU" + X, "Tb" + X

        def rc(z):
            return B(w, wo + 128 * (z + 1), wo + 128 * (z + 2))

        part("src", n)
        if t == 0:
            Tb = "land" + X
        else:
            for h in range(2):
                mms(B("psE", 128 * h + 256, 128 * h + 384), [(B("RX", 128 * h, 128 * h + 128), B("ld" + X, lo, lo + 128))])
            copy(B(Tb, 256, 512), B("psE", 256, 512), ON["src"])
        part("ch", n)
        for z in (1, 2):
            buf = B("nXa" if z == 1 else "nXb")
            gtt(buf, B(Tb, 256, 512), B(nU, 8 * z - 8, 8 * z), B("MASKR", 0, 128), AL.mult)
            running_sum(B("s1"), B("RSM"), buf)
            copy(B(nU, 8 * z, 8 * z + 8), B("s1", 15, 128, 16))
        part("lt", n)
        if t:
            for h in range(2):
                mms(B("psP1", 128 * h + 256, 128 * h + 384), [(B("DUP", 128 * h, 128 * h + 128), B("ld" + X, lo + 128, lo + 256))])
            copy(B(Tb, 0, 256), B("psP1", 256, 512), ON["table"])

        def offsets(P, c, a, b, o):
            tt(B("v1", c + a, c + b), B(P, a, b), B("odd", o + a, o + b), AL.mult)
            ts(B("v2", c + a, c + b), B("v1", c + a, c + b), 2, 4095, AL.arith_shift_right, AL.bitwise_and)
            copy(B("off" + X, c + a, c + b), B("v2", c + a, c + b))
        for z in range(3):
            part(["lt", "cb", "cc"][z], n, PLAN["early"] * (n == 1 and z == 1))
            gather(rc(z), B(Tb, 0, 256), B(nU, 8 * z, 8 * z + 8), ON["lists"][z] if n else ON["opening"][z])
            P, wg = ["psP0", "psP1", "psP0"][z], 128 if z else 0
            G, Hh = B(P, 0, wg), B(P, wg, wg + 128)
            mm(B(P, 0, wg + 128), B("I"), B("c4096", 0, wg + 128), True, False)
            mm(Hh, pf(2), R0, False, False, True)
            if z:
                mm(G, pf(2 + 2 * z), rc(0), False, False)
                mm(Hh, pf(3 + 2 * z), rc(0), False, False, True)
                mm(G, pf(1), rc(z), False, False)
            mm(Hh, pf(0 if z else 3), rc(z), False, True, z > 0)
            for a, b in [(0, 256)] if z else [(0, 64), (64, 128)]:
                offsets(P, place_of(2 * z if z else 1, 0) // 16, a, b, W0)
        part("cd", n)
        mm(B("psP1", 0, W0), B("I"), B("c4096", 0, W0), True, False)
        for k, (v, cc, shift, end) in enumerate(DENSE):
            mm(B("psP1", cc, W0, 5), pf(8 + k), B(w, wo + 128 + v, wo + 256, 8), False, k == len(DENSE) - 1, True)
        offsets("psP1", 0, 0, W0, 0)
        part("pen", n)
        for z in range(3):
            mms(B("psQ", 128 * z, 128 * z + 128), [(B("I"), B("cm127")), (B("BLK"), R0), (B("IMO"), rc(z))])
        ts(B("pen" + X), B("psQ", 0, 384), MAGIC, MAGIC, AL.add, AL.not_equal)
        part("pq", n)
        mm(B(K, 392, 456), R0, B("BB", 96, 160), True, False)
        mm(B(K, 424, 432), B("I"), B("c8", 16 + 8 * x, 24 + 8 * x), False, False, True)
        for v in [B("FLD" + X, 80 + 8 * f, 88 + 8 * f) for f in range(4)] if t else [B("SR" + X)]:
            mm(B(K, 392, 400), B("I"), v, False, False, True)
        mm(B(K, 400, 408), B("I"), B("NX" + X), False, False, True)
        mm(B(K, 408, 416), B("nXa"), B("BB", 32, 40), False, False)
        mm(B(K, 416, 432), B("nXb"), B("BB", 32, 48), False, False, True)
        for z in range(3):
            mm(B(K, 432 + 8 * z, 440 + 8 * z), rc(z), B("BB", 56, 64), False, z == 2, z > 0)

        hc = helper(core, T.cores, topo)
        rid, pid = topo.addr(hc, core)

        def fold(u, s, xe, c0, c1):
            sem, es = "fb%d%d" % (x, u), lane(core, hc, u, topo)
            tr = RemoteDMATransfer(dst_ids=[DstId(rid=rid, pnc=pid)], dma_engine_mask=sum(1 << k for k in es), remote_sem=T.sem["fa%d%d" % (x, u)],
                                   srcs=[s[0], xe[0]], dsts=[T[held(n)][:, c0:c1]], alu_op=2)
            folded.append(op("g", lambda e: e.remote_dma_fused([tr], local_sem=T.sem[sem]), [s, xe], [B("Mx" + X, c0, c1)], PLAN["issue"],
                             sem=sem, inc=len(es) + len(topo.engines(hc, core)), then=False, bytes=256 * (c1 - c0),
                             lane=len(es) / len(topo.engines(core, hc)),
                             lat=PLAN["landed"], back=True, after=folded[-1:]))
        u = 0
        for j, (e, ch, a, b, f) in enumerate(pieces(*SHARE[n])):
            part("g", n, j / 1000)
            name[0] += ".%d" % ch
            c0, c1 = place_of(ch, a), place_of(ch, b)
            xe = B("Xe" + X, 16 * a, 16 * b)
            s, of = B("Sg" + X, c0, c1), B("off" + X, c0 // 16, c1 // 16)
            if e == "a":
                i = gather(s, B("S" + X), of, e)
                steps[i]["after"] = scalar_last[-1:]
                scalar_last.append(i)
                if f:
                    fold(u, s, xe, c0, c1)
                    u += 1
                else:
                    name[1] = n + PLAN["late"]
                    for k in range(ROWS[ch]):
                        tt(B("Mx" + X, c0 + k, c1, ROWS[ch]), B("Sg" + X, c0 + k, c1, ROWS[ch]), B("psX", 128 * x + a, 128 * x + b), AL.max)
            else:
                gtt(s, B("S" + X), of, xe, AL.subtract)
                ts(B("Mx" + X, c0, c1), s, 0.0, None, AL.max)

        if n:
            decide(n - 1)
        part("key", n)
        left = [0]
        mm(B(K, 0, 384), B("ones"), B("KC"), True, left)
        for z in range(3):
            mm(B(K, 128 * z, 128 * z + 128), B("pen" + X, 128 * z, 128 * z + 128), B("BIGP"), False, left, loose=True)
        for ch in range(1, 6):
            m = min(128, max(0, SHARE[n][0] - 128 * ch + 128))
            if m < 128:
                xs = B("obsM", 128 * n, 128 * n + 128) if m else B("obsM", 768 + 128 * x, 896 + 128 * x)
                mm(B(K, ch // 2 * 128, ch // 2 * 128 + 128), xs, B("WX", ch % 2 * 128, ch % 2 * 128 + 128), False, left, loose=True)
                mm(B(K, 80 + 8 * ch, 128), xs, B("Wm64", 80 + 8 * ch, 128), False, left, True)
        for ch in range(6):
            part("s", n)
            name[0] += ".%d" % ch
            for buf, wt in (("Sg", "Wm64"), ("Mx", "W128")):
                for i, (k, z, a, b) in enumerate(terms(ch)):
                    more = {"join": True} if i % (4 if ch else 2) else {"loose": True}
                    mm(B(K, 128 * z + 8 * a, 128 * z + 8 * b), B(buf + X, place_of(ch, 0) + k, place_of(ch, 128), ROWS[ch]), B(wt, 8 * a, 8 * b),
                       False, left, **more)

    def decide(n):
        x, t = n % 2, n // 2
        X, last = str(x), t == NR - 1
        w, K, wo = "W" + X, "psK" + X, 512 * t
        R0 = B(w, 0, 128)
        IND, nacc, FLD = B("IND" + X, 64 * t, 64 * t + 64), B("IND" + X, 64 * t, 64 * t + 8), "FLD" + X

        def to_list(out, src, first):
            mms(out, first + [(B("EW", 112 - 16 * (4 * (c % 2) + c // 2), 240 - 16 * (4 * (c % 2) + c // 2)), B(src, 8 * c, 8 * c + 8))
                              for c in range(8)])
        part("d", n)
        for c in range(8):
            least(B("best", c, c + 1), B(K, c, 392, 8))
        mm(B("psE", 128, 256), B("row", 768, 896), B("ones"), True, False)
        ts(B("bi", 8, 16), B("best"), 48, None, AL.bitwise_and)
        ts(B("bi", 0, 8), B("best"), 15, None, AL.bitwise_and)
        gtt(IND, B("bi", 8, 16), B("idx", 26, 30), B("thrc"), AL.is_equal)
        gtt(B(FLD, 0, 80), B("bi"), B("idx", 20, 25), B("mA8"), AL.mult)
        tt(B(FLD, 80, 144), IND, B(K, 392, 456), AL.mult)
        mm(B(K, 0, 128), B(FLD, 64, 192), B("I"), True, True)
        to_list(B("psD", 0, 8), FLD, [(B("I"), B("ilist"))])
        copy(B("T1s" + X), B(K, 0, 128), ON["turned"])
        copy(B("offW"), B("psD", 0, 8))
        gather(B("Rb"), B(w, wo, wo + 512), B("offW"), ON["chosen"])
        mm(B("psE", 128, 256), B("RY"), B("T1s" + X), False, True)
        ts(B("mask"), B("psE", 128, 256), SITE, SITE, AL.add, AL.is_equal)
        tt(B("md"), B("psE", 128, 256), B("mask"), AL.mult)
        if last:
            tt(B("Rf" + X), B("Rb"), B("md"), AL.add)
            for h in range(2):
                store("sa"[h] if n == NT - 1 else "s", T.yr[64 * x:64 * x + 64, 128 * h:128 * h + 128], B("Rf" + X, p=HALF[h]))
        else:
            send(n + 2, 0, B("T1s" + X))
            send(n + 2, 1, B("Rb"), B("md"))
            part("mine", n)
            mms(B("psE", 0, 128), [(B("I"), B("Rb")), (B("I"), B("md"))])
            copy(B(w, wo + 512, wo + 640), B("psE", 0, 128), ON["mine"])
        part("e", n)
        ts(B("sc"), B("best"), 6, None, AL.arith_shift_right)
        mms(B("psD", 136, 144), [(B("I"), B("c8", 8 * x, 8 * x + 8)), (B("I"), B(FLD, 112, 120))]
            + [(B("I13"), B(FLD, 88 + 8 * f, 96 + 8 * f)) for f in range(3)])
        h3 = B("h2", 8, 16)
        tt(B("d3", 0, 8), B("sc"), nacc, AL.mult)
        tt(B("d3", 8, 16), B("sc"), B("d3", 0, 8), AL.subtract)
        tt(B("h2", 0, 8), B("psD", 136, 144), B("d3", 8, 16), AL.add)
        ts(h3, B("h2", 0, 8), 255, None, AL.bitwise_and)
        F = B("Fn") if t else B("sc")
        if last:
            tt(B("u"), nacc, B("A7" + X), AL.mult)
            tt(F, B("sc"), B("u"), AL.add)
            tt(B("OF" + X, 0, 8), F, B("cst", 8 * x, 8 * x + 8), AL.add)
        if last:
            copy(B("OF" + X, 8, 16), h3)
            turn_over(B("psD", 256, 384, p=(0, 16)), B("OF" + X), B("I32"))
            copy(B("oT" + X, p=(0, 16)), B("psD", 256, 384, p=(0, 16)))
            store("s", T.yf[4 * x:4 * x + 4, :], B("oT" + X, p=(0, 8)))
            store("sa"[x], T.yn[4 * x:4 * x + 4, :], B("oT" + X, p=(8, 16)))
        else:
            gtt(B("Ln"), h3, B("idx", 16, 20), B("mA1"), AL.mult)
            copy(B("NX" + X), h3)
            to_list(B("psD", 256, 264), "Ln", [])
            copy(B("nU" + X, 0, 8), B("psD", 256, 264))
            part("f", n)
            if t:
                tt(B("u"), nacc, B("A7" + X), AL.mult)
                tt(F, B("sc"), B("u"), AL.add)
            for h in range(2):
                mms(B("psD", 264 + h, 272, 2), [(B("seven"), B("IND" + X, 64 * r + k, 64 * r + 8, 2)) for r in range(t + 1) for k in range(2)])
            copy(B("Ai"), B("psD", 264, 272))
            ts(B("A7" + X), B("Ai"), 7, None, AL.bitwise_and)
            tt(B("Tn"), F, B("A7" + X), AL.subtract)
            ts(B(K, 384, 392), B("Tn"), 64.0, None, AL.mult)

    for n in range(NT):
        search(n)
    decide(NT - 1)
    if "order" not in ORDER:
        ORDER["order"], ORDER["end"] = arrange(steps)
    for i in ORDER["order"]:
        TAGGER[0][0] = steps[i]["name"]
        for call in steps[i]["calls"]:
            issue(*call)
    for s in sorted(total):
        if known["g"].get(s, 0) < total[s]:
            g.wait_ge(T.sem[s], total[s])


TAGGER = [[""]]
ON = {"table": "v", "lists": "vaa", "chosen": "v", "turned": "v", "src": "a", "mine": "v", "opening": "vvv", "twice": "avav"}
